import numpy as np, ml_dtypes
CORES = [66,74,82,90,194,202,210,218]
N = 8
BF = ml_dtypes.bfloat16
def gentries(a):
    return np.ascontiguousarray(a.reshape(8, 16, -1).transpose(0, 2, 1)).reshape(8, -1)
def gtable(e):
    e = np.asarray(e); return np.ascontiguousarray(e.reshape(8, -1, 16).transpose(0, 2, 1)).reshape(128, -1).astype(np.int32)
V, S, L, DS = 1024, 128, 16, (4, 1, 7)
W = N * V
def mix(rng, a):
    return np.take_along_axis(a, np.argsort(rng.random(a.shape), axis=-1), -1)
def some(rng, pool, shape, n):
    q = len(pool) // n
    return pool[np.arange(n) * q + rng.integers(0, q, shape + (n,))]
def parts(rng):
    x = (256 * np.sqrt(rng.random((N, 8, 1, V))) * rng.random((N, 8, 16, V))).astype(np.int64)
    sl = np.empty((N, 8, S, L), np.int64)
    for g in range(8):
        p = rng.permutation(W); a = p[:3 * L][np.argsort(rng.random((N, S, 3 * L)), axis=-1)[..., :L]]
        sl[:, g] = np.where(np.arange(L) < rng.integers(0, L + 1, (N, S, 1)), a, some(rng, p[3 * L:], (N, S), L))
    return x, mix(rng, sl), rng.integers(0, S * L, (N, 8, V))
def pack(x, sl, pr):
    return {"x": np.ascontiguousarray(x.reshape(N, 128, V)).astype(np.float32).astype(BF), "sl": np.stack([gtable(a.reshape(8, -1)) for a in sl]), "prey": np.stack([gtable(a) for a in pr])}
def setup_inputs(rng):
    return pack(*parts(rng))
def setup_inputs_pools(rng):
    x, sl, pr = parts(rng)
    for g in range(8):
        x[:, g] = rng.integers(0, 256, 16)[np.argsort(rng.random((N, 16, V)), axis=1)]
    ms = np.array([0, 1, 2, L // 2, L - 1, L])
    for a in range(N):
        b = a ^ DS[0]
        if a < b:
            for g in range(8):
                e = some(rng, rng.permutation(W), (S,), 2 * L); m = rng.choice(ms, (S, 1)); m[:6, 0] = ms
                if g == 2: m[:] = 0
                if g == 5: m[:] = L
                sl[a, g] = mix(rng, e[:, :L]); sl[b, g] = mix(rng, np.where(np.arange(L) < m, e[:, L:], e[:, :L]))
    return pack(x, sl, pr)
def setup_inputs_ties(rng):
    x, sl, pr = parts(rng)
    kind = rng.integers(0, 4, (N, 8, V)); proto = rng.integers(0, 256, (8, 16, 4))
    proto[1, :, 1] = proto[1, ::-1, 0]; proto[1, :, 3] = proto[1, ::-1, 2]; proto[0] = rng.integers(0, 256, (1, 1))
    for q in range(N):
        for g in range(8): x[q, g] = proto[g][:, kind[q, g]]
    return pack(x, sl, pr)
def setup_inputs_few(rng):
    x, sl, pr = parts(rng); o = rng.permutation(N)
    for g in (0, 4):
        c = np.concatenate([np.array([0, W - 1]), 1 + rng.permutation(W - 2)[:L]])
        sl[:, g] = c[np.argsort(rng.random((N, S, L + 2)), axis=-1)[..., :L]]
    pr[:, 1] = rng.choice(np.array([0, L - 1, L, S * L - 1]), (N, V)); pr[:, 5] = S * L - 1
    sl[1:, 5] = sl[0, 5]
    sl[:, 2] = mix(rng, some(rng, o[0] * V + rng.permutation(V), (N, S), L))
    sl[:, 6] = mix(rng, some(rng, o[1] * V + 1024 * rng.integers(0, V // 1024) + rng.permutation(1024), (N, S), L))
    for g in (3, 7): sl[:, g] = mix(rng, np.zeros((N, S, 1), np.int64) + rng.permutation(W)[:L])
    return pack(x, sl, pr)
def setup_inputs_ends(rng):
    x, sl, pr = parts(rng); x = 255 * rng.integers(0, 2, x.shape)
    for g in (0, 3, 6): x[:, g, :, 0::2] = 0; x[:, g, :, 1::2] = 255
    x[:, 1, :, 0::2] = rng.integers(0, 32, (N, 16, V // 2)); x[:, 1, :, 1::2] = rng.integers(224, 256, (N, 16, V // 2))
    c = np.arange(V); low = 255 * (L - 1) // (2 * L - 1); e = rng.integers(0, 4, (N, 16, V))
    x[:, 2] = np.where(np.arange(16)[:, None] % L == (c // 2) % L, 255 * (1 - c % 2), np.where(c % 2 == 1, 255 - low + e, low - e))
    for a in range(N):
        odd = int(a > (a ^ DS[0]))
        sl[a, 0] = some(rng, 2 * rng.permutation(W // 2) + odd, (S,), L); sl[a, 3] = some(rng, 2 * rng.permutation(W // 2) + 1 - odd, (S,), L)
        sl[a, 1] = some(rng, 2 * rng.permutation(W // 2) + odd, (S,), L)
        sl[a, 2] = mix(rng, 2 * (L * rng.integers(0, W // (2 * L), (S, L)) + np.arange(L)) + odd)
    t = np.arange(S)
    for a in range(N):
        b = a ^ DS[0]
        if a < b: sl[b, 0, t, rng.integers(0, L, S)] = sl[a, 0, t, rng.integers(0, L, S)]
    sl[:, 4] = np.concatenate([rng.permutation(W) for i in range((N * S * L + W - 1) // W)])[:N * S * L].reshape(N, S, L)
    one = rng.integers(0, N) * V + np.concatenate([rng.permutation(V) for i in range((S * L + V - 1) // V)])[:S * L].reshape(S, L)
    sl[:, 5] = mix(rng, np.zeros((N, 1, 1), np.int64) + one)
    sl[:, 7] = mix(rng, some(rng, 16 * rng.permutation(W // 16) + rng.integers(0, 16), (N, S), L))
    for g in (4, 5): pr[:, g] = mix(rng, np.zeros((N, 1), np.int64) + np.arange(max(V, S * L)) % (S * L))[:, :V]
    return pack(x, sl, pr)
def setup_inputs_spread(rng):
    x, sl, pr = parts(rng)
    x = (np.exp2(8 * rng.random((N, 8, 1, V))) * rng.random((N, 8, 16, V)) * (rng.random((N, 8, 1, V)) > 0.0625)).astype(np.int64)
    pr = np.minimum((S * L * rng.random((N, 8, V)) ** 3).astype(np.int64), S * L - 1)
    return pack(x, sl, pr)
def check_inputs(d):
    bad = []
    v = np.asarray(d["x"]).astype(np.float32)
    if not np.all((v >= 0) & (v <= 255) & (v == np.floor(v))): bad.append("range of x")
    for k, hi in (("sl", W - 1), ("prey", S * L - 1)):
        if np.min(d[k]) < 0 or np.max(d[k]) > hi: bad.append("range of " + k)
    e = np.sort(np.stack([gentries(a) for a in d["sl"]]).reshape(N, 8, S, L), axis=-1)
    if np.any(e[..., 1:] == e[..., :-1]): bad.append("different species in a site of sl")
    return bad
def reference(x, sl, prey):
    v = x.astype(np.float32).astype(np.int64).reshape(N, 8, 16, V)
    ls = np.stack([gentries(a) for a in sl]).astype(np.int64).reshape(N, 8, S, L); pl = np.stack([gentries(a) for a in prey]).astype(np.int64)
    j = np.arange(L)
    for d in DS:
        w = np.concatenate([v[a] for a in range(N)], axis=2)
        cs, od = [], []
        for a in range(N):
            c = np.add.reduce(np.take_along_axis(w, ls[a].reshape(8, 1, S * L), 2).reshape(8, 16, S, L), axis=3)
            cs.append(c); od.append(np.argsort(np.arange(S) - S * np.add.reduce(c, axis=1), axis=1))
        new = np.array(ls)
        for a in range(N):
            b = a ^ d
            if a < b:
                la = np.take_along_axis(ls[a], od[a][:, :, None], 1); lb = np.take_along_axis(ls[b], od[b][:, :, None], 1)
                ca = np.take_along_axis(cs[a], od[a][:, None, :], 2)[..., None]; cb = np.take_along_axis(cs[b], od[b][:, None, :], 2)[..., None]
                pool = np.concatenate([la, lb], axis=2)
                px = L * np.take_along_axis(w, pool.reshape(8, 1, -1), 2).reshape(8, 16, S, 2 * L)
                key = 2 * L * np.add.reduce(np.abs(px - ca) - np.abs(px - cb), axis=1) + np.arange(2 * L)
                eq = la[:, :, :, None] == lb[:, :, None, :]
                com = np.concatenate([np.any(eq, axis=3), np.any(eq, axis=2)], axis=2)
                m = np.add.reduce((~com[:, :, :L]).astype(np.int64), axis=2)[:, :, None]
                sp = np.take_along_axis(pool, np.argsort(np.where(com, 2 ** 40 + np.arange(2 * L), key), axis=2), 2)
                np.put_along_axis(new[a], od[a][:, :, None], np.take_along_axis(sp, np.where(j < m, j, m + j), 2), 1)
                np.put_along_axis(new[b], od[b][:, :, None], np.take_along_axis(sp, np.where(j < m, m + j, L + j), 2), 1)
        ls = new
        hx = [np.take_along_axis(w, np.take_along_axis(ls[a].reshape(8, S * L), pl[a], 1)[:, None, :], 2) for a in range(N)]
        v = (v + np.stack(hx) + 1) >> 1
    return {"yl": np.stack([gtable(a.reshape(8, -1)) for a in ls]).astype(np.float32), "yx": v.reshape(N, 128, V).astype(np.float32)}

@@ -1,0 +1,512 @@
+from concourse.bass import DstId, RemoteDMATransfer
+from concourse.mybir import AluOpType as Op, ActivationFunctionType as Fn
+
+BF, F32, F16, I32, U16 = "bfloat16", "float32", "float16", "int32", "uint16"
+N = 8
+DS = (4, 1, 7)
+
+
+def sb(n, d):
+    return ("sbuf", [128, n], d)
+
+
+def dr(n, d):
+    return ("dram", [8, 128, n], d)
+
+
+SCRATCH = {
+    "xs0": dr(64, BF), "xl0": dr(64, BF), "xs1": dr(64, BF), "xl1": dr(64, BF),
+    "ss": dr(16, I32), "sll": dr(16, I32), "prs": dr(8, I32), "prl": dr(8, I32),
+    "ys": dr(16, F32), "yll": dr(16, F32),
+    "vs0": dr(64, BF), "vl0": dr(64, BF), "vs1": dr(64, BF), "vl1": dr(64, BF),
+    "p0": ("psum", [128, 32, 16], F32), "p1": ("psum", [128, 32, 16], F32),
+    "p2": ("psum", [128, 512], F32), "p3": ("psum", [128, 512], F32), "p4": ("psum", [128, 512], F32),
+    "p5": ("psum", [128, 512], F32), "p6": ("psum", [128, 512], F32), "p7": ("psum", [128, 512], F32),
+    "ci": sb(8, I32), "cf": sb(32, F32), "pg": sb(8, F32),
+    "rowx": sb(256, BF), "row16": sb(128, BF), "rowq": sb(256, BF), "row32": sb(128, BF), "rowg": sb(512, BF),
+    "zero": sb(128, BF), "ones": sb(128, BF), "tie": sb(128, BF), "cs": sb(240, BF), "half": sb(8, BF),
+    "trow": sb(1024, BF),
+    "idn": sb(128, BF), "nid": sb(128, BF), "id16": sb(128, BF), "dsg": sb(128, BF), "ndsg": sb(128, BF),
+    "ds128": sb(128, BF), "nds128": sb(128, BF), "dm": sb(128, BF), "dbig": sb(128, BF), "dq": sb(128, BF),
+    "we": sb(128, BF), "we1": sb(128, BF), "we2": sb(128, BF), "swp": sb(128, F32),
+    "vv": sb(1024, BF), "yy": sb(1024, BF), "ny": sb(512, BF),
+    "kp": sb(144, BF), "kn": sb(144, BF), "oa": sb(160, BF), "ob": sb(160, BF), "qs": sb(256, BF),
+    "rd": sb(2048, BF), "ra": sb(2048, BF), "tcol": sb(128, U16),
+    "pm32": sb(256, F32), "pm16": sb(256, BF),
+    "v0": sb(1024, BF), "vo": sb(1024, F16), "vh": sb(1024, F32), "vb": sb(1024, BF),
+    "w": sb(8192, BF), "xg": sb(2048, BF), "g1": sb(2048, BF),
+    "sli": sb(128, I32), "pri": sb(64, I32), "prf": sb(192, F32), "pru": sb(192, U16),
+    "lu": sb(128, U16), "lf": sb(128, F32), "lu2": sb(128, U16), "lf2": sb(128, F32), "lpos": sb(128, F32),
+    "hp": sb(128, BF), "lp": sb(128, F32), "pp": sb(256, BF), "dsg32": sb(128, F32),
+    "rowa": sb(192, BF), "rowb": sb(192, BF), "rowc": sb(192, BF), "rowy": sb(128, BF), "q1": sb(128, BF),
+    "q2": sb(192, BF), "cd": sb(1024, BF), "ca": sb(1024, BF),
+    "ch": sb(128, F16), "cw": sb(128, F32), "cp": sb(128, F32), "csw": sb(128, F32),
+    "gs": ("sbuf", [128, 64, 16], BF), "pos": sb(144, U16),
+    "m1": sb(2048, F16), "m2": sb(2048, F16), "gl": sb(1024, BF), "gk": sb(2048, BF),
+    "rr": sb(128, BF), "r128": sb(128, BF), "com": sb(128, BF),
+    "ks": sb(128, F32), "kq": sb(128, F32), "k32": sb(128, F32), "kh": sb(128, F16), "kl": sb(128, F16),
+    "t1": sb(128, F32), "t2": sb(128, F32), "z": sb(512, F16), "oh": sb(8192, F16),
+}
+TAGS = ["x0", "x1", "sl", "pr", "yl", "y0", "y1"]
+SEMAPHORES = ["e_pe", "e_dve", "e_act", "e_g"] + ["d%d" % k for k in range(32)] + \
+    ["a" + t for t in TAGS] + ["l" + t for t in TAGS]
+
+
+def arrangement(d):
+    out = []
+    for a in range(N):
+        if a < (a ^ d):
+            out += [a, a ^ d]
+    return out
+
+
+def emit(g, T, ops):
+    queue = {"pe": g.tensor, "dve": g.vector, "act": g.scalar, "g": g, "sync": g.sync}
+    seen, clock, nseq, hist = {}, {q: {} for q in queue}, {}, []
+    waits, marked = [], set()
+    for k, (q, src, fn, rd, wr) in enumerate(ops):
+        need = {}
+        for acc, isw in ((rd, False), (wr, True)):
+            for name, lo, hi in acc:
+                ps = name == "ps"
+                if ps:
+                    lo, hi = lo // 512 * 512, (hi + 511) // 512 * 512
+                for lo2, hi2, k2, w2 in seen.get(name, ()):
+                    if lo2 >= hi or hi2 <= lo:
+                        continue
+                    s2 = ops[k2][1]
+                    if s2 == "pe" and src == "pe":
+                        continue
+                    if isw or w2 or (ps and s2 != src):
+                        if hist[k2][0] > need.get(s2, (0, 0))[0]:
+                            need[s2] = (hist[k2][0], k2)
+        mine = []
+        if q is not None:
+            ck = clock[q]
+            for s2, (n2, k2) in sorted(need.items(), key=lambda it: -it[1][1]):
+                if ck.get(s2, 0) < n2:
+                    mine.append(k2)
+                    marked.add(k2)
+                    for s3, n3 in hist[k2][1].items():
+                        if ck.get(s3, 0) < n3:
+                            ck[s3] = n3
+            snap = dict(ck)
+        else:
+            snap = {}
+        nseq[src] = nseq.get(src, 0) + 1
+        snap[src] = nseq[src]
+        hist.append((nseq[src], snap))
+        waits.append(mine)
+        for acc, isw in ((rd, False), (wr, True)):
+            for name, lo, hi in acc:
+                if name == "ps":
+                    lo, hi = lo // 512 * 512, (hi + 511) // 512 * 512
+                lst = seen.setdefault(name, [])
+                if isw:
+                    lst[:] = [e for e in lst if not (lo <= e[0] and e[1] <= hi)]
+                lst.append((lo, hi, k, isw))
+    count, at, waited = {}, {}, {}
+    for k, (q, src, fn, rd, wr) in enumerate(ops):
+        for k2 in waits[k]:
+            queue[q].wait_ge(T.sem[at[k2][0]], at[k2][1])
+            waited[at[k2][0]] = max(waited.get(at[k2][0], 0), at[k2][1])
+        if src in queue:
+            ins = fn(queue[q])
+            if k in marked:
+                count["e_" + src] = count.get("e_" + src, 0) + 1
+                ins.then_inc(T.sem["e_" + src], 1)
+                at[k] = ("e_" + src, count["e_" + src])
+        elif src[0] == "d":
+            fn(queue[q]).then_inc(T.sem[src], 16)
+            count[src] = 16
+            at[k] = (src, 16)
+        else:
+            if fn is not None:
+                fn(queue[q])
+            count[src] = N - 1
+            at[k] = (src, N - 1)
+    for s in sorted(count):
+        if waited.get(s, 0) < count[s]:
+            g.wait_ge(T.sem[s], count[s])
+
+
+def rank_program(g, core, T, topo):
+    rank = T.rank_of(core)
+    if rank is None:
+        return
+    ops, nd = [], [0]
+    arr = [arrangement(d) for d in DS]
+
+    def B(name, lo=0, hi=None, step=1):
+        if hi is None:
+            hi = T[name].shape[1]
+        return (T[name][:, lo:hi:step] if step > 1 else T[name][:, lo:hi], [(name, lo, hi)])
+
+    def P(bank, lo=0, hi=512):
+        t = T["p%d" % bank]
+        return (t[:, lo // 16:hi // 16, :] if bank < 2 else t[:, lo:hi], [("ps", bank * 512 + lo, bank * 512 + hi)])
+
+    def C(k):
+        return B("cf", k, k + 1)
+
+    def IND(win, off):
+        return (win[0].indirect(off[0]), win[1] + off[1])
+
+    def D(name, slot=None):
+        if slot is None:
+            return (T[name][:], [(name, 0, N)])
+        return (T[name][slot], [(name, slot, slot + 1)])
+
+    def sides(*xs):
+        r = []
+        for x in xs:
+            if isinstance(x, tuple):
+                r += x[1]
+        return r
+
+    def val(x):
+        return x[0] if isinstance(x, tuple) else x
+
+    def mm(out, lhsT, rhs, start, stop):
+        ops.append(("pe", "pe", lambda e: e.matmul(out[0], lhsT[0], rhs[0], start, stop), lhsT[1] + rhs[1], out[1]))
+
+    def cp(out, in_):
+        ops.append(("dve", "dve", lambda e: e.tensor_copy(out[0], in_[0]), in_[1] + out[1][1:], out[1][:1]))
+
+    def tt(out, a, b, op):
+        ops.append(("dve", "dve", lambda e: e.tensor_tensor(out[0], a[0], b[0], op), a[1] + b[1], out[1]))
+
+    def ts(out, a, s1, o0, s2=None, o1=None):
+        if o1 is None:
+            f = lambda e: e.tensor_scalar(out[0], a[0], val(s1), None, o0)
+        else:
+            f = lambda e: e.tensor_scalar(out[0], a[0], val(s1), val(s2), o0, o1)
+        ops.append(("dve", "dve", f, sides(a, s1, s2), out[1]))
+
+    def ms(out, c):
+        ops.append(("dve", "dve", lambda e: e.memset(out[0], c), [], out[1]))
+
+    def act(out, a, scale=1.0, bias=0.0, fn=Fn.Identity):
+        ops.append(("act", "act", lambda e: e.activation(out[0], a[0], fn, bias=val(bias), scale=val(scale)),
+                    sides(a, scale, bias), out[1]))
+
+    def iota(out, pat, cm, small=True):
+        if small:
+            f = lambda e: e.iota(out[0], pat, 0, cm, allow_small_or_imprecise_dtypes=True)
+        else:
+            f = lambda e: e.iota(out[0], pat, 0, cm)
+        ops.append(("g", "g", f, [], out[1]))
+
+    def dma(q, out, in_):
+        ops.append((q, "d%d" % nd[0], lambda e: e.dma_start(out[0], in_[0]), in_[1], out[1]))
+        nd[0] += 1
+
+    def exchange(tag, src, src_slot, dst, dst_slot):
+        trs = []
+        for k in range(1, N):
+            r = rank ^ k
+            rid, pid = topo.addr(T.cores[r], core)
+            trs.append(RemoteDMATransfer(dst_ids=[DstId(rid=rid, pnc=pid)],
+                                         dma_engine_mask=1 << topo.engines(core, T.cores[r])[k - 1],
+                                         remote_sem=T.sem["a" + tag], src=T[src][src_slot(r)], dst=T[dst][dst_slot]))
+        ops.append(("g", "l" + tag, lambda e: e.remote_dma_fused(trs, local_sem=T.sem["l" + tag]), [(src, 0, N)], []))
+
+    def arrival(tag, dst, own):
+        ops.append((None, "a" + tag, None, [], [(dst, k, k + 1) for k in range(N) if k != own]))
+
+    rows = slice(16 * rank, 16 * rank + 16)
+    slot0 = arr[0].index(rank)
+    dma("sync", D("xs0"), (T.x[:, 0:512], []))
+    dma("act", D("xs1"), (T.x[:, 512:1024], []))
+    dma("sync", D("ss"), (T.sl[:], []))
+    dma("act", D("xl0", slot0), (T.x[rows, 0:512], []))
+    dma("sync", D("xl1", slot0), (T.x[rows, 512:1024], []))
+    dma("sync", D("prs"), (T.prey[:], []))
+    dma("sync", D("sll", slot0), (T.sl[rows, :], []))
+    dma("sync", D("prl", slot0), (T.prey[rows, :], []))
+    iota(B("ci", 0, 1), [[0, 1]], 1, False)
+    iota(B("pg"), [[-16, 8]], 1)
+    iota(B("row16"), [[0, 8], [1, 16]], 0)
+    iota(B("rowx"), [[1, 256]], 0)
+    iota(B("rowq"), [[0, 2], [1, 32], [32, 4]], 0)
+    exchange("x0", "xs0", lambda r: r, "xl0", slot0)
+    exchange("x1", "xs1", lambda r: r, "xl1", slot0)
+    exchange("sl", "ss", lambda r: r, "sll", slot0)
+    exchange("pr", "prs", lambda r: r, "prl", slot0)
+    iota(B("rowy"), [[1, 16], [16, 8]], 0)
+    iota(B("rowa"), [[1, 24], [0, 4], [1, 2]], 0)
+    iota(B("rowb"), [[1, 24], [32, 4], [-15, 2]], 0)
+    iota(B("row32"), [[32, 4], [0, 32]], 0)
+    iota(B("rowg"), [[0, 4], [16, 8], [0, 16]], 0)
+    iota(B("trow"), [[16, 8], [0, 8], [1, 16]], 0)
+    arrival("x0", "xl0", slot0)
+    arrival("x1", "xl1", slot0)
+    arrival("sl", "sll", slot0)
+    arrival("pr", "prl", slot0)
+    dma("sync", B("v0", 0, 512), D("xl0"))
+    dma("sync", B("v0", 512, 1024), D("xl1"))
+    dma("sync", B("sli"), D("sll"))
+    dma("g", B("pri"), D("prl"))
+
+    ms(B("zero"), 0.0)
+    ms(B("ones"), 1.0)
+    ms(B("tie"), -1.0 / 2048)
+    ms(B("half"), 0.5)
+    ms(B("cs", 0, 112), 0.0)
+    ms(B("cs", 112, 128), 0.5)
+    ms(B("cs", 128, 240), 0.0)
+    for k, m in ((1, 16), (2, 31), (3, 112), (4, 96)):
+        ts(B("ci", k, k + 1), B("ci", 0, 1), m, Op.bitwise_and)
+    cp(B("cf", 0, 5), B("ci", 0, 5))
+    for k in range(8):
+        ts(B("vv", 128 * k, 128 * k + 128), B("row16"), B("pg", k, k + 1), Op.is_equal)
+    PP, B16, E, G16, G32, SG, SG128, SQ, SW, U15, U31, KAP, TIE, A2, A32, S128, S160, S64, S64P, NSG, NS128 = range(21)
+    ts(C(SG), C(B16), -0.125, Op.mult, 1.0, Op.add)
+    ts(B("idn"), B("rowx", 0, 128), C(PP), Op.is_equal)
+    ts(C(S64P), C(B16), -8.0, Op.mult, 64.0, Op.add)
+    ts(C(NSG), C(B16), 0.125, Op.mult, -1.0, Op.add)
+    ts(B("qs"), B("rowq"), C(PP), Op.is_equal, C(S64P), Op.mult)
+    ts(C(U15), C(G16), 15.0, Op.add)
+    ts(C(U31), C(G32), 31.0, Op.add)
+    ts(C(KAP), C(E), -511872.0, Op.mult, 7934080.0, Op.add)
+    ts(C(TIE), C(PP), -1.0 / 2048, Op.mult)
+    ts(C(A2), C(B16), 0.125, Op.mult, -2.0, Op.add)
+    ts(C(A32), C(B16), -2.0, Op.mult, 32.0, Op.add)
+    ts(C(SG128), C(SG), 1.0 / 128, Op.mult)
+    ts(C(NS128), C(SG), -1.0 / 128, Op.mult)
+    ts(C(SQ), C(E), C(SG), Op.mult, 1.0 / 64, Op.mult)
+    ts(C(SW), C(SG), 16.0, Op.mult, C(PP), Op.add)
+    ts(C(S128), C(SG), 128.0, Op.mult)
+    ts(C(S160), C(SG), -20480.0, Op.mult)
+    ts(C(S64), C(SG), -64.0, Op.mult)
+    ts(C(KAP), C(B16), 528384.0, Op.mult, C(KAP), Op.add)
+    act(B("nid"), B("idn"), -1.0)
+    act(B("dsg"), B("idn"), C(SG))
+    act(B("ndsg"), B("idn"), C(NSG))
+    for k in range(8):
+        ts(B("yy", 128 * k, 128 * k + 128), B("zero"), C(G16), Op.add, 16.0 * k, Op.is_equal)
+    cp(B("tcol"), B("rowx", 0, 128))
+    ts(B("swp"), B("rowx", 0, 128), C(SW), Op.is_equal)
+    ts(B("kp"), B("rowx", 0, 144), C(U15), Op.is_equal, 8.0, Op.mult)
+    ts(B("kn"), B("rowx", 0, 144), C(U15), Op.is_equal, -8.0, Op.mult)
+    ts(B("oa"), B("rowx", 0, 160), C(U31), Op.is_equal, 128.0, Op.mult)
+    ts(B("ob"), B("rowx", 0, 160), C(U31), Op.is_equal)
+    ts(B("id16"), B("idn"), 1.0 / 16, Op.mult)
+    ts(B("ds128"), B("idn"), C(SG128), Op.mult)
+    ts(B("nds128"), B("idn"), C(NS128), Op.mult)
+    ts(B("dm"), B("idn"), -1024.0, Op.mult)
+    ts(B("dbig"), B("idn"), 32768.0, Op.mult)
+    ts(B("dq"), B("idn"), C(SQ), Op.mult)
+    ts(B("we2"), B("idn"), C(A32), Op.mult)
+    cp(B("dsg32"), B("dsg"))
+    ts(B("q1"), B("rowy"), C(PP), Op.is_equal, C(S64P), Op.mult)
+    ts(B("rowc"), B("rowa"), 16.0, Op.is_lt, 16.0, Op.mult)
+    tt(B("rowc"), B("rowc"), B("rowb"), Op.add)
+    ts(B("q2"), B("rowc"), C(PP), Op.is_equal, C(S64P), Op.mult)
+    for k in range(2):
+        for gm in range(8):
+            gn = arr[k + 1].index(arr[k][gm])
+            cp(B("pm16", 128 * k + 16 * gn, 128 * k + 16 * gn + 16), B("idn", 16 * gm, 16 * gm + 16))
+    cp(B("pm32"), B("pm16"))
+    ts(B("we1"), B("row32"), C(G32), Op.is_equal, C(A2), Op.mult)
+    tt(B("we"), B("we1"), B("we2"), Op.add)
+    ts(B("ny"), B("rowg"), C(G16), Op.is_equal, -1.0, Op.mult)
+    for b in range(8):
+        for u in range(4):
+            s = 4 * (b % 4) + u + 1
+            o = P(b, 128 * u, 128 * u + 128)
+            q0, q1 = B("qs", 0, 128), B("qs", 4 * s, 4 * s + 128)
+            if b < 4:
+                mm(o, B("idn"), q0, True, False)
+                mm(o, B("nid"), q1, False, True)
+            elif s < 16:
+                mm(o, q0, B("dsg"), True, False)
+                mm(o, q1, B("ndsg"), False, True)
+            else:
+                mm(o, q0, B("dsg"), True, True)
+        act(B("rd" if b < 4 else "ra", 512 * (b % 4), 512 * (b % 4) + 512), P(b))
+    for b in range(4):
+        for u in range(4):
+            t = 4 * (b % 2) + u
+            o = P(b, 128 * u, 128 * u + 128)
+            q1 = B("q2", 8 * t, 8 * t + 128)
+            if b < 2:
+                mm(o, B("idn"), B("q1"), True, False)
+                mm(o, B("nid"), q1, False, True)
+            else:
+                mm(o, B("q1"), B("dsg"), True, False)
+                mm(o, q1, B("dsg"), False, True)
+        act(B("cd" if b < 2 else "ca", 512 * (b % 2), 512 * (b % 2) + 512), P(b))
+
+    def table(src, ar, off, first):
+        for k in range(16):
+            h, gm = k // 8, k % 8
+            mm(P(k % 8), B("vv", 128 * gm, 128 * gm + 128), B(src, 512 * h, 512 * h + 512), True, True)
+            o = B("w", 1024 * ar[gm] + 512 * h, 1024 * ar[gm] + 512 * h + 512)
+            if (k % 2 == 1) if first else (k == 0 or k % 2 == 1):
+                act(o, P(k % 8), 1.0, -off)
+            else:
+                ts(o, P(k % 8), -off, Op.add)
+
+    def diffs(mat, hi, lo, b, opened):
+        for u in range(4):
+            s = 4 * b + u
+            if u or not opened:
+                mm(P(b, 128 * u, 128 * u + 128), B(mat, 128 * s, 128 * s + 128), hi, True, False)
+            mm(P(b, 128 * u, 128 * u + 128), B(mat, 128 * s, 128 * s + 128), lo, False, True)
+
+    def counts(mat, out, src, n, opened):
+        for s in range(n):
+            mm(out, B(mat, 128 * s, 128 * s + 128), B(src, 128 * s, 128 * s + 128), s == 0 and not opened, s == n - 1)
+
+    def keys(mat, src, h, last):
+        for j in range(16):
+            mm(P(6 - 2 * h, 256, 320), B(mat, 15 - j, 143 - j), B(src, 1024 * h + j, 1024 * h + 1024, 16),
+               j == 0 and not last, last and j == 15)
+
+    def m1(k):
+        tt(B("m1", 512 * k, 512 * k + 512), IND(B("cw", 64 * (k // 2), 64 * (k // 2) + 64),
+                                                B("tcol", 32 * (k % 2), 32 * (k % 2) + 32)),
+           B("xg", 512 * k, 512 * k + 512), Op.max)
+
+    table("v0", arr[0], 128.0, True)
+    cp(B("lu"), B("sli"))
+    cp(B("lf"), B("sli"))
+    for rho in range(3):
+        last = rho == 2
+        for k in range(4):
+            o, i = B("xg", 512 * k, 512 * k + 512), IND(B("w"), B("lu", 32 * k, 32 * k + 32))
+            if k % 2 == 0:
+                cp(o, i)
+            else:
+                act(o, i)
+        for b in range(2):
+            mm(P(b), (T.tie[0:1, :], [("tie", 0, 128)]),
+               (T.trow[0:1, 512 * b:512 * b + 512], [("trow", 0, 1024)]), True, False)
+        for h in range(2):
+            for j in range(16):
+                mm(P(4 + 3 * h, 0, 64), B("id16"), B("xg", 1024 * h + j, 1024 * h + 1024, 16), j == 0, j == 15)
+        cp(B("cw", 0, 64), P(4, 0, 64))
+        act(B("cw", 64, 128), P(7, 0, 64))
+        cp(B("ch", 0, 64), P(4, 0, 64))
+        m1(0)
+        cp(B("ch", 64, 128), P(7, 0, 64))
+        for b in range(2):
+            mm(P(b), B("ch"), B("ny"), False, False)
+            for a in range(8):
+                mm((T["p%d" % b][:, a:32:8, :], P(b)[1]), B("yy", 128 * a, 128 * a + 128),
+                   B("ch", 64 * b, 64 * b + 64), False, a == 7)
+            act((T.gs[:, 32 * b:32 * b + 32, :], [("gs", 32 * b, 32 * b + 32)]), P(b), -1.0, C(TIE), Fn.Sign)
+        for k in range(1, 4):
+            m1(k)
+        for b in range(2):
+            half = [("gs", 32 * b, 32 * b + 32)]
+            for n in range(4 * b, 4 * b + 4):
+                mm(P(5, 128 + n, 129 + n), (T.gs[:, 8 * n:8 * n + 8, :], half), B("half", 0, 1), True, True)
+            for a in range(8):
+                mm(P(5, 64 * b, 64 * b + 64), B("cs", 112 - 16 * a, 240 - 16 * a),
+                   (T.gs[:, 32 * b + a:32 * b + 32:8, :], half), a == 0, a == 7)
+        keys("kp", "m1", 0, False)
+        ts(B("pos", 0, 136), P(5, 0, 136), 63.5, Op.add)
+        keys("kp", "m1", 1, False)
+        cp(IND(B("cp"), B("pos", 128, 136)), B("cw"))
+        mm(P(5, 384, 512), B("swp"), B("cp"), True, True)
+        act(B("csw"), P(5, 384, 512))
+        cp(IND(B("lp"), B("pos", 128, 136)), B("lf"))
+        for h in range(2):
+            tt(B("m2", 1024 * h, 1024 * h + 1024), IND(B("csw"), B("pos", 64 * h, 64 * h + 64)),
+               B("xg", 1024 * h, 1024 * h + 1024), Op.max)
+        p1, p2 = B("pp", 0, 128), B("pp", 128, 256)
+        mm(P(2, 0, 128), B("dsg32"), B("lp"), True, False)
+        act(B("hp"), B("lp"), 1.0 / 128, 160.0 - 127.0 / 256)
+        act(p1, B("hp"), C(S128), C(S160))
+        mm(P(2, 0, 128), B("nid"), p1, False, True)
+        act(p2, P(2, 0, 128), 1.0, C(S64))
+        for b in range(2):
+            diffs("cd", p1, p2, b, False)
+            act(B("gl", 512 * b, 512 * b + 512), P(b), 1.0, 0.0, Fn.Sign)
+        keys("kn", "m2", 0, True)
+        counts("ca", P(7, 0, 128), "gl", 8, False)
+        keys("kn", "m2", 1, True)
+        act(B("rr"), P(7, 0, 128), 1.0 / 128, 192.25)
+        act(B("r128"), B("rr"), 128.0, -128.0 * 192)
+        act(B("ks", 0, 64), P(6, 256, 320), 1.0, C(SQ))
+        act(B("ks", 64, 128), P(4, 256, 320), 1.0, C(SQ))
+        tt(B("com"), B("r128"), P(7, 0, 128), Op.subtract)
+        cp(IND(B("kq"), B("pos", 128, 132)), B("ks", 0, 64))
+        mm(P(5, 0, 128), B("dbig"), B("ones"), True, False)
+        mm(P(5, 0, 128), B("dq"), B("ones"), False, False)
+        mm(P(5, 0, 128), B("dm"), B("com"), False, True)
+        mm(P(5, 128, 256), B("we"), B("com"), True, True)
+        mm(P(5, 256, 384), B("dsg"), p2, True, False)
+        mm(P(5, 256, 384), B("nds128"), p1, False, True)
+        mm(P(7, 256, 384), B("ds128"), p1, True, False)
+        cp(IND(B("kq"), B("pos", 132, 136)), B("ks", 64, 128))
+        tt(B("kh"), B("kq"), P(5, 0, 128), Op.min)
+        tt(B("k32"), B("kq"), P(5, 0, 128), Op.min)
+        tt(B("kl"), B("k32"), B("kh"), Op.subtract)
+        za = P(7, 256, 384)
+        for b in range(4):
+            mm(P(b, 0, 128), B("rd", 512 * b, 512 * b + 128), B("kh"), True, False)
+        for b in range(4):
+            diffs("rd", B("kh"), B("kl"), b, True)
+            if b % 2 == 0:
+                act(B("gk", 512 * b, 512 * b + 512), P(b), 1.0, 0.0, Fn.Sign)
+            else:
+                ts(B("gk", 512 * b, 512 * b + 512), P(b), -1.0, Op.max, 1.0, Op.min)
+        counts("ra", za, "gk", 16, True)
+        ts(B("t1"), za, 4096.0, Op.mult, 0.0, Op.min)
+        tt(B("t2"), B("t1"), P(5, 128, 256), Op.max)
+        tt(B("z", 0, 128), B("t2"), za, Op.add)
+        tt(B("z", 128, 256), B("z", 0, 128), P(5, 256, 384), Op.add)
+        ts(B("z", 256, 512), B("z", 0, 256), -2048.0, Op.add)
+        if rho == 0:
+            act(B("vh"), B("v0"), 0.5, 1472.25)
+        else:
+            for h in range(2):
+                mm(P(h), B("pm16", 128 * rho - 128, 128 * rho), B("vo", 512 * h, 512 * h + 512), True, True)
+                act(B("vh", 512 * h, 512 * h + 512), P(h), 0.5, 768.25)
+            mm(P(2, 0, 64), B("pm32", 128 * rho - 128, 128 * rho), B("prf", 64 * rho - 64, 64 * rho), True, True)
+            act(B("prf", 64 * rho, 64 * rho + 64), P(2, 0, 64))
+        for e in range(16):
+            ts(B("oh", 512 * e, 512 * e + 512), B("z"), 128.0 * (e - 16), Op.max, 128.0 * (e - 15), Op.min)
+            for u in range(4):
+                e2 = e + 16 * (u // 2)
+                mm(P(6, 0, 128), B("ob" if u % 2 else "oa", 31 - e2, 159 - e2),
+                   B("oh", 512 * e + 128 * u, 512 * e + 128 * u + 128), e == 0 and u == 0, e == 15 and u == 3)
+        if rho == 0:
+            cp(B("prf", 0, 64), B("pri"))
+        cp(B("pru", 64 * rho, 64 * rho + 64), B("prf", 64 * rho, 64 * rho + 64))
+        act(B("lpos"), P(6, 0, 128), 1.0, C(KAP))
+        cp(B("lu2"), IND(B("lpos"), B("pos", 128, 136)))
+        ts(B("g1", 0, 1024), IND(B("w"), B("lu2", 0, 64)), 0.5, Op.mult)
+        act(B("g1", 1024, 2048), IND(B("w"), B("lu2", 64, 128)), 0.5)
+        act(B("lf2"), IND(B("lpos"), B("pos", 128, 136)))
+        if not last:
+            mm(P(7, 0, 128), B("pm32", 128 * rho, 128 * rho + 128), B("lf2"), True, True)
+            act(B("lf"), P(7, 0, 128))
+        for h in range(2):
+            tt(B("vo", 512 * h, 512 * h + 512), IND(B("g1"), B("pru", 64 * rho + 32 * h, 64 * rho + 32 * h + 32)),
+               B("vh", 512 * h, 512 * h + 512), Op.add)
+            if last:
+                ts(B("vb", 512 * h, 512 * h + 512), B("vo", 512 * h, 512 * h + 512), -1408.0, Op.add)
+        if not last:
+            cp(B("lu"), B("lf"))
+            table("vo", arr[rho], 1536.0, False)
+
+    slot2 = arr[2].index(rank)
+    own = slice(16 * slot2, 16 * slot2 + 16)
+    dma("act", D("ys"), B("lf2"))
+    dma("act", D("yll", rank), (T.lf2[own, :], [("lf2", 0, 128)]))
+    for h in range(2):
+        dma("sync", D("vs%d" % h), B("vb", 512 * h, 512 * h + 512))
+        dma("act", D("vl%d" % h, rank), (T.vb[own, 512 * h:512 * h + 512], [("vb", 512 * h, 512 * h + 512)]))
+    exchange("yl", "ys", lambda r: arr[2].index(r), "yll", rank)
+    for h in range(2):
+        exchange("y%d" % h, "vs%d" % h, lambda r: arr[2].index(r), "vl%d" % h, rank)
+    arrival("yl", "yll", rank)
+    dma("act", (T.yl[:], []), D("yll"))
+    for h in range(2):
+        arrival("y%d" % h, "vl%d" % h, rank)
+        dma("g", (T.yx[:, 512 * h:512 * h + 512], []), D("vl%d" % h))
+    emit(g, T, ops)

@@ -4,6 +4,7 @@ from concourse.mybir import AluOpType as Op, ActivationFunctionType as Fn
 BF, F32, F16, I32, U16 = "bfloat16", "float32", "float16", "int32", "uint16"
 N = 8
 DS = (4, 1, 7)
+CUTS = (0, 640, 1024)
 
 
 def sb(n, d):
@@ -18,7 +19,7 @@ SCRATCH = {
     "xs0": dr(64, BF), "xl0": dr(64, BF), "xs1": dr(64, BF), "xl1": dr(64, BF),
     "ss": dr(16, I32), "sll": dr(16, I32), "prs": dr(8, I32), "prl": dr(8, I32),
     "ys": dr(16, F32), "yll": dr(16, F32),
-    "vs0": dr(64, BF), "vl0": dr(64, BF), "vs1": dr(64, BF), "vl1": dr(64, BF),
+    "vs0": dr(80, BF), "vl0": dr(80, BF), "vs1": dr(48, BF), "vl1": dr(48, BF),
     "p0": ("psum", [128, 32, 16], F32), "p1": ("psum", [128, 32, 16], F32),
     "p2": ("psum", [128, 512], F32), "p3": ("psum", [128, 512], F32), "p4": ("psum", [128, 512], F32),
     "p5": ("psum", [128, 512], F32), "p6": ("psum", [128, 512], F32), "p7": ("psum", [128, 512], F32),
@@ -35,7 +36,8 @@ SCRATCH = {
     "pm32": sb(256, F32), "pm16": sb(256, BF),
     "v0": sb(1024, BF), "vo": sb(1024, F16), "vh": sb(1024, F32), "vb": sb(1024, BF),
     "w": sb(8192, BF), "xg": sb(2048, BF), "g1": sb(2048, BF),
-    "sli": sb(128, I32), "pri": sb(64, I32), "prf": sb(192, F32), "pru": sb(192, U16),
+    "sli": sb(128, I32), "pri": sb(64, I32), "prf": sb(384, F32), "pru": sb(64, U16),
+    "pti": sb(128, I32), "tu": sb(64, U16), "jb": sb(64, BF), "posf": sb(128, BF), "prow": sb(1024, BF),
     "lu": sb(128, U16), "lf": sb(128, F32), "lu2": sb(128, U16), "lf2": sb(128, F32), "lpos": sb(128, F32),
     "hp": sb(128, BF), "lp": sb(128, F32), "pp": sb(256, BF), "dsg32": sb(128, F32),
     "rowa": sb(192, BF), "rowb": sb(192, BF), "rowc": sb(192, BF), "rowy": sb(128, BF), "q1": sb(128, BF),
@@ -348,26 +350,23 @@ def rank_program(g, core, T, topo):
             else:
                 ts(o, P(k % 8), -off, Op.add)
 
-    def diffs(mat, hi, lo, b, opened):
-        for u in range(4):
-            s = 4 * b + u
-            if u or not opened:
-                mm(P(b, 128 * u, 128 * u + 128), B(mat, 128 * s, 128 * s + 128), hi, True, False)
-            mm(P(b, 128 * u, 128 * u + 128), B(mat, 128 * s, 128 * s + 128), lo, False, True)
-
-    def counts(mat, out, src, n, opened):
-        for s in range(n):
-            mm(out, B(mat, 128 * s, 128 * s + 128), B(src, 128 * s, 128 * s + 128), s == 0 and not opened, s == n - 1)
-
-    def keys(mat, src, h, last):
-        for j in range(16):
+    def keys(mat, src, h, last, js=range(16)):
+        for j in js:
             mm(P(6 - 2 * h, 256, 320), B(mat, 15 - j, 143 - j), B(src, 1024 * h + j, 1024 * h + 1024, 16),
                j == 0 and not last, last and j == 15)
 
-    def m1(k):
-        tt(B("m1", 512 * k, 512 * k + 512), IND(B("cw", 64 * (k // 2), 64 * (k // 2) + 64),
-                                                B("tcol", 32 * (k % 2), 32 * (k % 2) + 32)),
-           B("xg", 512 * k, 512 * k + 512), Op.max)
+    def m1(lo, hi):
+        h = lo // 1024
+        tt(B("m1", lo, hi), IND(B("cw", 64 * h, 64 * h + 64), B("tcol", lo % 1024 // 16, (hi - 1) % 1024 // 16 + 1)),
+           B("xg", lo, hi), Op.max)
+
+    def clamp(e, lo, hi):
+        ts(B("oh", 512 * e + 128 * lo, 512 * e + 128 * hi), B("z", 128 * lo, 128 * hi),
+           128.0 * (e - 16), Op.max, 128.0 * (e - 15), Op.min)
+        for u in range(lo, hi):
+            e2 = e + 16 * (u // 2)
+            mm(P(6, 0, 128), B("ob" if u % 2 else "oa", 31 - e2, 159 - e2),
+               B("oh", 512 * e + 128 * u, 512 * e + 128 * u + 128), e == 0 and u == 0, e == 15 and u == 3)
 
     table("v0", arr[0], 128.0, True)
     cp(B("lu"), B("sli"))
@@ -387,31 +386,32 @@ def rank_program(g, core, T, topo):
             for j in range(16):
                 mm(P(4 + 3 * h, 0, 64), B("id16"), B("xg", 1024 * h + j, 1024 * h + 1024, 16), j == 0, j == 15)
         cp(B("cw", 0, 64), P(4, 0, 64))
-        act(B("cw", 64, 128), P(7, 0, 64))
         cp(B("ch", 0, 64), P(4, 0, 64))
-        m1(0)
+        m1(0, 384)
         cp(B("ch", 64, 128), P(7, 0, 64))
+        act(B("cw", 64, 128), P(7, 0, 64))
         for b in range(2):
             mm(P(b), B("ch"), B("ny"), False, False)
             for a in range(8):
                 mm((T["p%d" % b][:, a:32:8, :], P(b)[1]), B("yy", 128 * a, 128 * a + 128),
                    B("ch", 64 * b, 64 * b + 64), False, a == 7)
             act((T.gs[:, 32 * b:32 * b + 32, :], [("gs", 32 * b, 32 * b + 32)]), P(b), -1.0, C(TIE), Fn.Sign)
-        for k in range(1, 4):
-            m1(k)
-        for b in range(2):
-            half = [("gs", 32 * b, 32 * b + 32)]
-            for n in range(4 * b, 4 * b + 4):
-                mm(P(5, 128 + n, 129 + n), (T.gs[:, 8 * n:8 * n + 8, :], half), B("half", 0, 1), True, True)
-            for a in range(8):
-                mm(P(5, 64 * b, 64 * b + 64), B("cs", 112 - 16 * a, 240 - 16 * a),
-                   (T.gs[:, 32 * b + a:32 * b + 32:8, :], half), a == 0, a == 7)
-        keys("kp", "m1", 0, False)
-        ts(B("pos", 0, 136), P(5, 0, 136), 63.5, Op.add)
-        keys("kp", "m1", 1, False)
+        m1(384, 1024)
+        m1(1024, 2048)
+        keys("kp", "m1", 0, False, range(8))
+        for n in range(8):
+            mm(P(3, n, n + 1), (T.gs[:, 8 * n:8 * n + 8, :], [("gs", 8 * n, 8 * n + 8)]), B("half", 0, 1), True, True)
+            if n == 3:
+                keys("kp", "m1", 0, False, range(8, 16))
+        for a in range(8):
+            mm(P(5, 0, 128), B("cs", 112 - 16 * a, 240 - 16 * a), (T.gs[:, a:64:8, :], [("gs", 0, 64)]), a == 0, a == 7)
+        ts(B("pos", 128, 136), P(3, 0, 8), 63.5, Op.add)
+        keys("kp", "m1", 1, False, range(8))
         cp(IND(B("cp"), B("pos", 128, 136)), B("cw"))
-        mm(P(5, 384, 512), B("swp"), B("cp"), True, True)
-        act(B("csw"), P(5, 384, 512))
+        mm(P(3, 128, 256), B("swp"), B("cp"), True, True)
+        act(B("csw"), P(3, 128, 256))
+        keys("kp", "m1", 1, False, range(8, 16))
+        ts(B("pos", 0, 128), P(5, 0, 128), 63.5, Op.add)
         cp(IND(B("lp"), B("pos", 128, 136)), B("lf"))
         for h in range(2):
             tt(B("m2", 1024 * h, 1024 * h + 1024), IND(B("csw"), B("pos", 64 * h, 64 * h + 64)),
@@ -422,74 +422,92 @@ def rank_program(g, core, T, topo):
         act(p1, B("hp"), C(S128), C(S160))
         mm(P(2, 0, 128), B("nid"), p1, False, True)
         act(p2, P(2, 0, 128), 1.0, C(S64))
+        act(B("posf"), P(5, 0, 128), 1.0, 63.5)
         for b in range(2):
-            diffs("cd", p1, p2, b, False)
+            for u in range(4):
+                s = 4 * b + u
+                mm(P(b, 128 * u, 128 * u + 128), B("cd", 128 * s, 128 * s + 128), p1, True, False)
+                mm(P(b, 128 * u, 128 * u + 128), B("cd", 128 * s, 128 * s + 128), p2, False, True)
             act(B("gl", 512 * b, 512 * b + 512), P(b), 1.0, 0.0, Fn.Sign)
         keys("kn", "m2", 0, True)
-        counts("ca", P(7, 0, 128), "gl", 8, False)
+        for s in range(8):
+            mm(P(7, 0, 128), B("ca", 128 * s, 128 * s + 128), B("gl", 128 * s, 128 * s + 128), s == 0, s == 7)
         keys("kn", "m2", 1, True)
+        act(B("ks", 0, 64), P(6, 256, 320), 1.0, C(SQ))
         act(B("rr"), P(7, 0, 128), 1.0 / 128, 192.25)
         act(B("r128"), B("rr"), 128.0, -128.0 * 192)
-        act(B("ks", 0, 64), P(6, 256, 320), 1.0, C(SQ))
         act(B("ks", 64, 128), P(4, 256, 320), 1.0, C(SQ))
-        tt(B("com"), B("r128"), P(7, 0, 128), Op.subtract)
+        if rho == 0:
+            ts(B("pti", 0, 64), B("pri"), 4, Op.arith_shift_right)
+            ts(B("pti", 64, 128), B("pri"), 15, Op.bitwise_and)
+            cp(B("prf", 0, 128), B("pti"))
         cp(IND(B("kq"), B("pos", 128, 132)), B("ks", 0, 64))
+        cp(B("tu"), B("prf", 128 * rho, 128 * rho + 64))
+        tt(B("com"), B("r128"), P(7, 0, 128), Op.subtract)
+        act(B("prow"), IND(B("posf"), B("tu")))
+        act(B("jb"), B("prf", 128 * rho + 64, 128 * rho + 128), 8.0)
         mm(P(5, 0, 128), B("dbig"), B("ones"), True, False)
         mm(P(5, 0, 128), B("dq"), B("ones"), False, False)
         mm(P(5, 0, 128), B("dm"), B("com"), False, True)
         mm(P(5, 128, 256), B("we"), B("com"), True, True)
         mm(P(5, 256, 384), B("dsg"), p2, True, False)
         mm(P(5, 256, 384), B("nds128"), p1, False, True)
-        mm(P(7, 256, 384), B("ds128"), p1, True, False)
         cp(IND(B("kq"), B("pos", 132, 136)), B("ks", 64, 128))
+        za = P(7, 256, 384)
+        mm(za, B("ds128"), p1, True, False)
         tt(B("kh"), B("kq"), P(5, 0, 128), Op.min)
         tt(B("k32"), B("kq"), P(5, 0, 128), Op.min)
         tt(B("kl"), B("k32"), B("kh"), Op.subtract)
-        za = P(7, 256, 384)
         for b in range(4):
             mm(P(b, 0, 128), B("rd", 512 * b, 512 * b + 128), B("kh"), True, False)
         for b in range(4):
-            diffs("rd", B("kh"), B("kl"), b, True)
+            for u in range(4):
+                s = 4 * b + u
+                if u:
+                    mm(P(b, 128 * u, 128 * u + 128), B("rd", 128 * s, 128 * s + 128), B("kh"), True, False)
+                mm(P(b, 128 * u, 128 * u + 128), B("rd", 128 * s, 128 * s + 128), B("kl"), False, True)
             if b % 2 == 0:
                 act(B("gk", 512 * b, 512 * b + 512), P(b), 1.0, 0.0, Fn.Sign)
             else:
                 ts(B("gk", 512 * b, 512 * b + 512), P(b), -1.0, Op.max, 1.0, Op.min)
-        counts("ra", za, "gk", 16, True)
-        ts(B("t1"), za, 4096.0, Op.mult, 0.0, Op.min)
-        tt(B("t2"), B("t1"), P(5, 128, 256), Op.max)
-        tt(B("z", 0, 128), B("t2"), za, Op.add)
-        tt(B("z", 128, 256), B("z", 0, 128), P(5, 256, 384), Op.add)
-        ts(B("z", 256, 512), B("z", 0, 256), -2048.0, Op.add)
+        for s in range(16):
+            mm(za, B("ra", 128 * s, 128 * s + 128), B("gk", 128 * s, 128 * s + 128), False, s == 15)
+        mm(P(1, 0, 64), B("idn"), B("jb"), True, False)
+        for j in range(16):
+            mm(P(1, 0, 64), B("kp", 15 - j, 143 - j), B("prow", j, 1024, 16), False, j == 15)
         if rho == 0:
             act(B("vh"), B("v0"), 0.5, 1472.25)
         else:
             for h in range(2):
-                mm(P(h), B("pm16", 128 * rho - 128, 128 * rho), B("vo", 512 * h, 512 * h + 512), True, True)
-                act(B("vh", 512 * h, 512 * h + 512), P(h), 0.5, 768.25)
-            mm(P(2, 0, 64), B("pm32", 128 * rho - 128, 128 * rho), B("prf", 64 * rho - 64, 64 * rho), True, True)
-            act(B("prf", 64 * rho, 64 * rho + 64), P(2, 0, 64))
-        for e in range(16):
-            ts(B("oh", 512 * e, 512 * e + 512), B("z"), 128.0 * (e - 16), Op.max, 128.0 * (e - 15), Op.min)
-            for u in range(4):
-                e2 = e + 16 * (u // 2)
-                mm(P(6, 0, 128), B("ob" if u % 2 else "oa", 31 - e2, 159 - e2),
-                   B("oh", 512 * e + 128 * u, 512 * e + 128 * u + 128), e == 0 and u == 0, e == 15 and u == 3)
-        if rho == 0:
-            cp(B("prf", 0, 64), B("pri"))
-        cp(B("pru", 64 * rho, 64 * rho + 64), B("prf", 64 * rho, 64 * rho + 64))
-        act(B("lpos"), P(6, 0, 128), 1.0, C(KAP))
-        cp(B("lu2"), IND(B("lpos"), B("pos", 128, 136)))
+                mm(P(2 + h), B("pm16", 128 * rho - 128, 128 * rho), B("vo", 512 * h, 512 * h + 512), True, True)
+                act(B("vh", 512 * h, 512 * h + 512), P(2 + h), 0.5, 768.25)
+        ts(B("t1"), za, 4096.0, Op.mult, 0.0, Op.min)
+        tt(B("t2"), B("t1"), P(5, 128, 256), Op.max)
+        tt(B("z", 0, 128), B("t2"), za, Op.add)
+        tt(B("z", 128, 256), B("z", 0, 128), P(5, 256, 384), Op.add)
+        clamp(0, 0, 2)
+        ts(B("z", 256, 512), B("z", 0, 256), -2048.0, Op.add)
+        clamp(1, 0, 2)
+        clamp(0, 2, 4)
+        clamp(1, 2, 4)
+        for e in range(2, 16):
+            clamp(e, 0, 4)
+        ts(B("pru"), P(1, 0, 64), 0.125, Op.mult)
+        ts(B("lu2"), P(6, 0, 128), C(KAP), Op.add)
         ts(B("g1", 0, 1024), IND(B("w"), B("lu2", 0, 64)), 0.5, Op.mult)
         act(B("g1", 1024, 2048), IND(B("w"), B("lu2", 64, 128)), 0.5)
+        act(B("lpos"), P(6, 0, 128), 1.0, C(KAP))
         act(B("lf2"), IND(B("lpos"), B("pos", 128, 136)))
         if not last:
+            mm(P(0, 0, 128), B("pm32", 128 * rho, 128 * rho + 128), B("prf", 128 * rho, 128 * rho + 128), True, True)
             mm(P(7, 0, 128), B("pm32", 128 * rho, 128 * rho + 128), B("lf2"), True, True)
+            act(B("prf", 128 * rho + 128, 128 * rho + 256), P(0, 0, 128))
             act(B("lf"), P(7, 0, 128))
-        for h in range(2):
-            tt(B("vo", 512 * h, 512 * h + 512), IND(B("g1"), B("pru", 64 * rho + 32 * h, 64 * rho + 32 * h + 32)),
-               B("vh", 512 * h, 512 * h + 512), Op.add)
+        cuts = CUTS if last else (0, 512, 1024)
+        for lo, hi in zip(cuts[:-1], cuts[1:]):
+            tt(B("vo", lo, hi), IND(B("g1"), B("pru", lo // 16, hi // 16)), B("vh", lo, hi), Op.add)
             if last:
-                ts(B("vb", 512 * h, 512 * h + 512), B("vo", 512 * h, 512 * h + 512), -1408.0, Op.add)
+                ts(B("vb", lo, hi), B("vo", lo, hi), -1408.0, Op.add)
         if not last:
             cp(B("lu"), B("lf"))
             table("vo", arr[rho], 1536.0, False)
@@ -499,8 +517,9 @@ def rank_program(g, core, T, topo):
     dma("act", D("ys"), B("lf2"))
     dma("act", D("yll", rank), (T.lf2[own, :], [("lf2", 0, 128)]))
     for h in range(2):
-        dma("sync", D("vs%d" % h), B("vb", 512 * h, 512 * h + 512))
-        dma("act", D("vl%d" % h, rank), (T.vb[own, 512 * h:512 * h + 512], [("vb", 512 * h, 512 * h + 512)]))
+        lo, hi = CUTS[h], CUTS[h + 1]
+        dma("sync", D("vs%d" % h), B("vb", lo, hi))
+        dma("act", D("vl%d" % h, rank), (T.vb[own, lo:hi], [("vb", lo, hi)]))
     exchange("yl", "ys", lambda r: arr[2].index(r), "yll", rank)
     for h in range(2):
         exchange("y%d" % h, "vs%d" % h, lambda r: arr[2].index(r), "vl%d" % h, rank)
@@ -508,5 +527,5 @@ def rank_program(g, core, T, topo):
     dma("act", (T.yl[:], []), D("yll"))
     for h in range(2):
         arrival("y%d" % h, "vl%d" % h, rank)
-        dma("g", (T.yx[:, 512 * h:512 * h + 512], []), D("vl%d" % h))
+        dma("g", (T.yx[:, CUTS[h]:CUTS[h + 1]], []), D("vl%d" % h))
     emit(g, T, ops)

@@ -1,3 +1,4 @@
+import math
 from concourse.bass import DstId, RemoteDMATransfer
 from concourse.mybir import AluOpType as Op, ActivationFunctionType as Fn
 
@@ -5,6 +6,11 @@ BF, F32, F16, I32, U16 = "bfloat16", "float32", "float16", "int32", "uint16"
 N = 8
 DS = (4, 1, 7)
 CUTS = (0, 640, 1024)
+VCUTS = (0, 256, 512, 1024)
+LN2 = math.log(2.0)
+INNER = {0: 16, 1: 16}
+EXPC = 7 * LN2 / 128
+ROUND = 1.5 * 2.0 ** 40
 
 
 def sb(n, d):
@@ -23,31 +29,35 @@ SCRATCH = {
     "p0": ("psum", [128, 32, 16], F32), "p1": ("psum", [128, 32, 16], F32),
     "p2": ("psum", [128, 512], F32), "p3": ("psum", [128, 512], F32), "p4": ("psum", [128, 512], F32),
     "p5": ("psum", [128, 512], F32), "p6": ("psum", [128, 512], F32), "p7": ("psum", [128, 512], F32),
-    "ci": sb(8, I32), "cf": sb(32, F32), "pg": sb(8, F32),
+    "ci": sb(8, I32), "cf": sb(40, F32), "pg": sb(8, F32),
     "rowx": sb(256, BF), "row16": sb(128, BF), "rowq": sb(256, BF), "row32": sb(128, BF), "rowg": sb(512, BF),
     "zero": sb(128, BF), "ones": sb(128, BF), "tie": sb(128, BF), "cs": sb(240, BF), "half": sb(8, BF),
     "trow": sb(1024, BF),
-    "idn": sb(128, BF), "nid": sb(128, BF), "id16": sb(128, BF), "dsg": sb(128, BF), "ndsg": sb(128, BF),
-    "ds128": sb(128, BF), "nds128": sb(128, BF), "dm": sb(128, BF), "dbig": sb(128, BF), "dq": sb(128, BF),
-    "we": sb(128, BF), "we1": sb(128, BF), "we2": sb(128, BF), "swp": sb(128, F32),
+    "idn": sb(128, BF), "nid": sb(128, BF), "dsg": sb(128, BF), "ndsg": sb(128, BF), "id16": sb(128, BF),
+    "dbig": sb(128, BF), "dq": sb(128, BF),
+    "we": sb(128, BF), "we1": sb(128, BF), "we2": sb(128, BF), "swp": sb(128, BF),
+    "d1": sb(128, BF), "d2": sb(128, BF), "ut": sb(128, BF), "up": sb(128, BF),
+    "ptb": sb(8, BF), "pt": sb(8, F32), "ow": sb(8 * 152, BF),
     "vv": sb(1024, BF), "yy": sb(1024, BF), "ny": sb(512, BF),
-    "kp": sb(144, BF), "kn": sb(144, BF), "oa": sb(160, BF), "ob": sb(160, BF), "qs": sb(256, BF),
-    "rd": sb(2048, BF), "ra": sb(2048, BF), "tcol": sb(128, U16),
+    "kp": sb(144, BF), "kn": sb(144, BF), "qs": sb(256, BF),
+    "rd": sb(2048, BF), "ra": sb(2048, BF),
     "pm32": sb(256, F32), "pm16": sb(256, BF),
     "v0": sb(1024, BF), "vo": sb(1024, F16), "vh": sb(1024, F32), "vb": sb(1024, BF),
     "w": sb(8192, BF), "xg": sb(2048, BF), "g1": sb(2048, BF),
     "sli": sb(128, I32), "pri": sb(64, I32), "prf": sb(384, F32), "pru": sb(64, U16),
     "pti": sb(128, I32), "tu": sb(64, U16), "jb": sb(64, BF), "posf": sb(128, BF), "prow": sb(1024, BF),
     "lu": sb(128, U16), "lf": sb(128, F32), "lu2": sb(128, U16), "lf2": sb(128, F32), "lpos": sb(128, F32),
-    "hp": sb(128, BF), "lp": sb(128, F32), "pp": sb(256, BF), "dsg32": sb(128, F32),
+    "lp": sb(128, F32), "pp": sb(256, BF),
     "rowa": sb(192, BF), "rowb": sb(192, BF), "rowc": sb(192, BF), "rowy": sb(128, BF), "q1": sb(128, BF),
     "q2": sb(192, BF), "cd": sb(1024, BF), "ca": sb(1024, BF),
-    "ch": sb(128, F16), "cw": sb(128, F32), "cp": sb(128, F32), "csw": sb(128, F32),
-    "gs": ("sbuf", [128, 64, 16], BF), "pos": sb(144, U16),
-    "m1": sb(2048, F16), "m2": sb(2048, F16), "gl": sb(1024, BF), "gk": sb(2048, BF),
-    "rr": sb(128, BF), "r128": sb(128, BF), "com": sb(128, BF),
-    "ks": sb(128, F32), "kq": sb(128, F32), "k32": sb(128, F32), "kh": sb(128, F16), "kl": sb(128, F16),
-    "t1": sb(128, F32), "t2": sb(128, F32), "z": sb(512, F16), "oh": sb(8192, F16),
+    "ch": sb(128, F16), "cp": sb(128, F32), "cq": sb(128, F16),
+    "gs": ("sbuf", [128, 64, 16], BF), "pos": sb(16, U16), "posb": sb(8, BF),
+    "m1": sb(2048, F16), "m2": sb(2048, F16),
+    "gl": sb(1024, BF), "gk": sb(2048, BF),
+    "rr": sb(128, F32), "com": sb(128, BF),
+    "ks": sb(128, F32), "kq": sb(128, F32), "kh": sb(128, F16), "kl": sb(128, F16),
+    "ew": sb(128, BF), "pwa": sb(128, BF), "pwb": sb(128, BF), "pwc": sb(128, BF),
+    "z": sb(512, BF), "oh": sb(4096, BF), "t128": sb(128, F16), "tlow": sb(128, BF),
 }
 TAGS = ["x0", "x1", "sl", "pr", "yl", "y0", "y1"]
 SEMAPHORES = ["e_pe", "e_dve", "e_act", "e_g"] + ["d%d" % k for k in range(32)] + \
@@ -71,17 +81,17 @@ def emit(g, T, ops):
         for acc, isw in ((rd, False), (wr, True)):
             for name, lo, hi in acc:
                 ps = name == "ps"
-                if ps:
-                    lo, hi = lo // 512 * 512, (hi + 511) // 512 * 512
+                blo, bhi = (lo // 512 * 512, (hi + 511) // 512 * 512) if ps else (lo, hi)
                 for lo2, hi2, k2, w2 in seen.get(name, ()):
-                    if lo2 >= hi or hi2 <= lo:
-                        continue
                     s2 = ops[k2][1]
                     if s2 == "pe" and src == "pe":
                         continue
-                    if isw or w2 or (ps and s2 != src):
-                        if hist[k2][0] > need.get(s2, (0, 0))[0]:
-                            need[s2] = (hist[k2][0], k2)
+                    if ps and s2 != src:
+                        hit = lo2 < bhi and hi2 > blo
+                    else:
+                        hit = lo2 < hi and hi2 > lo and (isw or w2)
+                    if hit and hist[k2][0] > need.get(s2, (0, 0))[0]:
+                        need[s2] = (hist[k2][0], k2)
         mine = []
         if q is not None:
             ck = clock[q]
@@ -101,11 +111,9 @@ def emit(g, T, ops):
         waits.append(mine)
         for acc, isw in ((rd, False), (wr, True)):
             for name, lo, hi in acc:
-                if name == "ps":
-                    lo, hi = lo // 512 * 512, (hi + 511) // 512 * 512
                 lst = seen.setdefault(name, [])
-                if isw:
-                    lst[:] = [e for e in lst if not (lo <= e[0] and e[1] <= hi)]
+                lst[:] = [e for e in lst if not (lo <= e[0] and e[1] <= hi and (
+                    (isw and name != "ps") or (ops[e[2]][1] == src and src in queue and (isw or not e[3]))))]
                 lst.append((lo, hi, k, isw))
     count, at, waited = {}, {}, {}
     for k, (q, src, fn, rd, wr) in enumerate(ops):
@@ -145,8 +153,8 @@ def rank_program(g, core, T, topo):
         return (T[name][:, lo:hi:step] if step > 1 else T[name][:, lo:hi], [(name, lo, hi)])
 
     def P(bank, lo=0, hi=512):
-        t = T["p%d" % bank]
-        return (t[:, lo // 16:hi // 16, :] if bank < 2 else t[:, lo:hi], [("ps", bank * 512 + lo, bank * 512 + hi)])
+        t, n = T["p%d" % bank], INNER.get(bank)
+        return (t[:, lo // n:hi // n, :] if n else t[:, lo:hi], [("ps", bank * 512 + lo, bank * 512 + hi)])
 
     def C(k):
         return B("cf", k, k + 1)
@@ -257,60 +265,70 @@ def rank_program(g, core, T, topo):
     ms(B("cs", 0, 112), 0.0)
     ms(B("cs", 112, 128), 0.5)
     ms(B("cs", 128, 240), 0.0)
-    for k, m in ((1, 16), (2, 31), (3, 112), (4, 96)):
-        ts(B("ci", k, k + 1), B("ci", 0, 1), m, Op.bitwise_and)
-    cp(B("cf", 0, 5), B("ci", 0, 5))
+    for k, m in enumerate((16, 31, 112, 96, 7, 8, 1)):
+        ts(B("ci", k + 1, k + 2), B("ci", 0, 1), m, Op.bitwise_and)
+    cp(B("cf", 0, 8), B("ci", 0, 8))
     for k in range(8):
         ts(B("vv", 128 * k, 128 * k + 128), B("row16"), B("pg", k, k + 1), Op.is_equal)
-    PP, B16, E, G16, G32, SG, SG128, SQ, SW, U15, U31, KAP, TIE, A2, A32, S128, S160, S64, S64P, NSG, NS128 = range(21)
+    (PP, B16, E, G16, G32, W7, H8, O1, SG, SQ, SW, U15, U32, KAP, TIE, A2, A32, S64P, NSG,
+     SQH, SQL, SOFF, NN, K1, K2, CU, CU1, WT, WP, Q4, QC) = range(31)
     ts(C(SG), C(B16), -0.125, Op.mult, 1.0, Op.add)
     ts(B("idn"), B("rowx", 0, 128), C(PP), Op.is_equal)
     ts(C(S64P), C(B16), -8.0, Op.mult, 64.0, Op.add)
     ts(C(NSG), C(B16), 0.125, Op.mult, -1.0, Op.add)
     ts(B("qs"), B("rowq"), C(PP), Op.is_equal, C(S64P), Op.mult)
     ts(C(U15), C(G16), 15.0, Op.add)
-    ts(C(U31), C(G32), 31.0, Op.add)
-    ts(C(KAP), C(E), -511872.0, Op.mult, 7934080.0, Op.add)
+    ts(C(U32), C(G32), 32.0, Op.add)
+    ts(C(KAP), C(O1), -173311.5, Op.mult, 8191.5, Op.add)
     ts(C(TIE), C(PP), -1.0 / 2048, Op.mult)
     ts(C(A2), C(B16), 0.125, Op.mult, -2.0, Op.add)
     ts(C(A32), C(B16), -2.0, Op.mult, 32.0, Op.add)
-    ts(C(SG128), C(SG), 1.0 / 128, Op.mult)
-    ts(C(NS128), C(SG), -1.0 / 128, Op.mult)
+    ts(C(NN), C(W7), 2.0, Op.mult, C(B16), Op.add)
+    ts(C(CU), C(W7), 2.0, Op.mult, C(G16), Op.add)
+    ts(C(WT), C(H8), -127.0 / 8, Op.mult, 128.0, Op.add)
+    ts(C(WP), C(H8), -127.0 * 16, Op.mult, 16384.0, Op.add)
+    ts(C(SQH), C(SG), 1.0 / 16384, Op.mult)
+    ts(C(SQL), C(SG), 1.0 / 128, Op.mult)
+    ts(C(SOFF), C(SG), 24512.5, Op.mult)
     ts(C(SQ), C(E), C(SG), Op.mult, 1.0 / 64, Op.mult)
     ts(C(SW), C(SG), 16.0, Op.mult, C(PP), Op.add)
-    ts(C(S128), C(SG), 128.0, Op.mult)
-    ts(C(S160), C(SG), -20480.0, Op.mult)
-    ts(C(S64), C(SG), -64.0, Op.mult)
-    ts(C(KAP), C(B16), 528384.0, Op.mult, C(KAP), Op.add)
+    ts(C(K1), C(NN), -25.0, Op.add, 256.0, Op.mult)
+    ts(C(K2), C(NN), -1.0, Op.mult, -129.0, Op.add)
+    ts(C(CU1), C(CU), 1.0, Op.add)
+    ts(C(Q4), C(SQ), 256.0, Op.mult)
+    ts(C(QC), C(SQ), 0.25, Op.mult, 32.0, Op.add)
     act(B("nid"), B("idn"), -1.0)
     act(B("dsg"), B("idn"), C(SG))
     act(B("ndsg"), B("idn"), C(NSG))
+    act(B("ptb"), B("rowx", 0, 8), -14 * LN2, 114 * LN2, Fn.Exp)
     for k in range(8):
         ts(B("yy", 128 * k, 128 * k + 128), B("zero"), C(G16), Op.add, 16.0 * k, Op.is_equal)
-    cp(B("tcol"), B("rowx", 0, 128))
     ts(B("swp"), B("rowx", 0, 128), C(SW), Op.is_equal)
     ts(B("kp"), B("rowx", 0, 144), C(U15), Op.is_equal, 8.0, Op.mult)
     ts(B("kn"), B("rowx", 0, 144), C(U15), Op.is_equal, -8.0, Op.mult)
-    ts(B("oa"), B("rowx", 0, 160), C(U31), Op.is_equal, 128.0, Op.mult)
-    ts(B("ob"), B("rowx", 0, 160), C(U31), Op.is_equal)
     ts(B("id16"), B("idn"), 1.0 / 16, Op.mult)
-    ts(B("ds128"), B("idn"), C(SG128), Op.mult)
-    ts(B("nds128"), B("idn"), C(NS128), Op.mult)
-    ts(B("dm"), B("idn"), -1024.0, Op.mult)
     ts(B("dbig"), B("idn"), 32768.0, Op.mult)
-    ts(B("dq"), B("idn"), C(SQ), Op.mult)
+    ts(B("dq"), B("idn"), C(Q4), Op.mult)
     ts(B("we2"), B("idn"), C(A32), Op.mult)
-    cp(B("dsg32"), B("dsg"))
+    cp(B("pt"), B("ptb"))
     ts(B("q1"), B("rowy"), C(PP), Op.is_equal, C(S64P), Op.mult)
     ts(B("rowc"), B("rowa"), 16.0, Op.is_lt, 16.0, Op.mult)
+    ts(B("d1"), B("idn"), C(K1), Op.mult)
     tt(B("rowc"), B("rowc"), B("rowb"), Op.add)
+    ts(B("d2"), B("idn"), C(K2), Op.mult)
     ts(B("q2"), B("rowc"), C(PP), Op.is_equal, C(S64P), Op.mult)
+    ts(B("ut"), B("rowx", 0, 128), C(CU1), Op.is_equal, C(WT), Op.mult)
+    ts(B("up"), B("rowx", 0, 128), C(CU), Op.is_equal, C(WP), Op.mult)
+    act(B("we1"), B("swp"), -127.0 / 256)
+    for w in range(8):
+        ts(B("ow", 152 * w, 152 * w + 152), B("rowx", 8 - w, 160 - w), C(U32), Op.is_equal, B("pt", w, w + 1), Op.mult)
+    tt(B("d2"), B("d2"), B("we1"), Op.add)
     for k in range(2):
         for gm in range(8):
             gn = arr[k + 1].index(arr[k][gm])
             cp(B("pm16", 128 * k + 16 * gn, 128 * k + 16 * gn + 16), B("idn", 16 * gm, 16 * gm + 16))
-    cp(B("pm32"), B("pm16"))
     ts(B("we1"), B("row32"), C(G32), Op.is_equal, C(A2), Op.mult)
+    cp(B("pm32"), B("pm16"))
     tt(B("we"), B("we1"), B("we2"), Op.add)
     ts(B("ny"), B("rowg"), C(G16), Op.is_equal, -1.0, Op.mult)
     for b in range(8):
@@ -338,39 +356,65 @@ def rank_program(g, core, T, topo):
             else:
                 mm(o, B("q1"), B("dsg"), True, False)
                 mm(o, q1, B("dsg"), False, True)
-        act(B("cd" if b < 2 else "ca", 512 * (b % 2), 512 * (b % 2) + 512), P(b))
+        act(B("cd" if b < 2 else "ca", 512 * (b % 2), 512 * (b % 2) + 512), P(b), 1.0 if b < 2 else 1024.0)
 
-    def table(src, ar, off, first):
-        for k in range(16):
-            h, gm = k // 8, k % 8
-            mm(P(k % 8), B("vv", 128 * gm, 128 * gm + 128), B(src, 512 * h, 512 * h + 512), True, True)
-            o = B("w", 1024 * ar[gm] + 512 * h, 1024 * ar[gm] + 512 * h + 512)
-            if (k % 2 == 1) if first else (k == 0 or k % 2 == 1):
-                act(o, P(k % 8), 1.0, -off)
-            else:
-                ts(o, P(k % 8), -off, Op.add)
+    def table(src, ar, off, cuts, first):
+        k = 0
+        for lo, hi in zip(cuts[:-1], cuts[1:]):
+            for gm in range(8):
+                bank = P(k % 8, 0, hi - lo)
+                mm(bank, B("vv", 128 * gm, 128 * gm + 128), B(src, lo, hi), True, True)
+                o = B("w", 1024 * ar[gm] + lo, 1024 * ar[gm] + hi)
+                if k < first or k % 2 == 1:
+                    act(o, bank, 1.0, -off)
+                else:
+                    ts(o, bank, -off, Op.add)
+                k += 1
 
-    def keys(mat, src, h, last, js=range(16)):
-        for j in js:
-            mm(P(6 - 2 * h, 256, 320), B(mat, 15 - j, 143 - j), B(src, 1024 * h + j, 1024 * h + 1024, 16),
-               j == 0 and not last, last and j == 15)
+    def repeat(mat, src, h):
+        for u in range(4):
+            mm((T["p%d" % (2 + h)][:, u:256:4], P(2 + h, 0, 256)[1]), B(mat), B(src, 64 * h, 64 * h + 64), True, True)
 
-    def m1(lo, hi):
-        h = lo // 1024
-        tt(B("m1", lo, hi), IND(B("cw", 64 * h, 64 * h + 64), B("tcol", lo % 1024 // 16, (hi - 1) % 1024 // 16 + 1)),
-           B("xg", lo, hi), Op.max)
+    def maxima(name, h, ks=range(4)):
+        for k in ks:
+            lo = 1024 * h + 256 * k
+            tt(B(name, lo, lo + 256), B("xg", 1024 * h + k, 1024 * h + 1024, 4), P(2 + h, 0, 256), Op.max)
 
-    def clamp(e, lo, hi):
-        ts(B("oh", 512 * e + 128 * lo, 512 * e + 128 * hi), B("z", 128 * lo, 128 * hi),
-           128.0 * (e - 16), Op.max, 128.0 * (e - 15), Op.min)
-        for u in range(lo, hi):
-            e2 = e + 16 * (u // 2)
-            mm(P(6, 0, 128), B("ob" if u % 2 else "oa", 31 - e2, 159 - e2),
-               B("oh", 512 * e + 128 * u, 512 * e + 128 * u + 128), e == 0 and u == 0, e == 15 and u == 3)
+    def keys(mat, name, h, ks=range(4)):
+        for k in ks:
+            for u in range(4):
+                j, lo = k + 4 * u, 1024 * h + 256 * k
+                mm(P(6 - 2 * h, 256, 320), B(mat, 15 - j, 143 - j), B(name, lo + u, lo + 256, 4),
+                   j == 0 and name == "m1", j == 15 and name == "m2")
 
-    table("v0", arr[0], 128.0, True)
+    def clamp(w, side, last=False):
+        lo = 512 * w + 256 * side
+        ts(B("oh", lo, lo + 256), B("z", 256 * side, 256 * side + 256),
+           2.0 ** (14 * w - 114), Op.max, 2.0 ** (14 * w - 106), Op.min)
+        for u in range(2):
+            at = 152 * w + 8 + 16 * side - 8 * u
+            mm(P(6, 0, 128), B("ow", at, at + 128), B("oh", lo + 128 * u, lo + 128 * u + 128), False, last and u == 1)
+
+    def sums(h):
+        for j in range(16):
+            mm(P(4 + 3 * h, 0, 64), B("id16"), B("xg", 1024 * h + j, 1024 * h + 1024, 16), j == 0, j == 15)
+        cp(B("ch", 64 * h, 64 * h + 64), P(4 + 3 * h, 0, 64))
+
+    def totals(b, stop):
+        for a in range(8):
+            mm((T["p%d" % b][:, a:32:8, :], P(b)[1]), B("yy", 128 * a, 128 * a + 128),
+               B("ch", 64 * b, 64 * b + 64), False, stop and a == 7)
+
+    def signs(b):
+        act((T.gs[:, 32 * b:32 * b + 32, :], [("gs", 32 * b, 32 * b + 32)]), P(b), -1.0, C(TIE), Fn.Sign)
+
+    def counts(b):
+        for n in range(4 * b, 4 * b + 4):
+            mm(P(7, 64 + n, 65 + n), (T.gs[:, 8 * n:8 * n + 8, :], [("gs", 8 * n, 8 * n + 8)]), B("half", 0, 1), True, True)
+
+    table("v0", arr[0], 128.0, (0, 512, 1024), 0)
     cp(B("lu"), B("sli"))
-    cp(B("lf"), B("sli"))
+    ts(B("lf"), B("sli"), C(SG), Op.mult, C(SOFF), Op.add)
     for rho in range(3):
         last = rho == 2
         for k in range(4):
@@ -383,81 +427,88 @@ def rank_program(g, core, T, topo):
             mm(P(b), (T.tie[0:1, :], [("tie", 0, 128)]),
                (T.trow[0:1, 512 * b:512 * b + 512], [("trow", 0, 1024)]), True, False)
         for h in range(2):
-            for j in range(16):
-                mm(P(4 + 3 * h, 0, 64), B("id16"), B("xg", 1024 * h + j, 1024 * h + 1024, 16), j == 0, j == 15)
-        cp(B("cw", 0, 64), P(4, 0, 64))
-        cp(B("ch", 0, 64), P(4, 0, 64))
-        m1(0, 384)
-        cp(B("ch", 64, 128), P(7, 0, 64))
-        act(B("cw", 64, 128), P(7, 0, 64))
-        for b in range(2):
-            mm(P(b), B("ch"), B("ny"), False, False)
-            for a in range(8):
-                mm((T["p%d" % b][:, a:32:8, :], P(b)[1]), B("yy", 128 * a, 128 * a + 128),
-                   B("ch", 64 * b, 64 * b + 64), False, a == 7)
-            act((T.gs[:, 32 * b:32 * b + 32, :], [("gs", 32 * b, 32 * b + 32)]), P(b), -1.0, C(TIE), Fn.Sign)
-        m1(384, 1024)
-        m1(1024, 2048)
-        keys("kp", "m1", 0, False, range(8))
-        for n in range(8):
-            mm(P(3, n, n + 1), (T.gs[:, 8 * n:8 * n + 8, :], [("gs", 8 * n, 8 * n + 8)]), B("half", 0, 1), True, True)
-            if n == 3:
-                keys("kp", "m1", 0, False, range(8, 16))
-        for a in range(8):
-            mm(P(5, 0, 128), B("cs", 112 - 16 * a, 240 - 16 * a), (T.gs[:, a:64:8, :], [("gs", 0, 64)]), a == 0, a == 7)
-        ts(B("pos", 128, 136), P(3, 0, 8), 63.5, Op.add)
-        keys("kp", "m1", 1, False, range(8))
-        cp(IND(B("cp"), B("pos", 128, 136)), B("cw"))
-        mm(P(3, 128, 256), B("swp"), B("cp"), True, True)
-        act(B("csw"), P(3, 128, 256))
-        keys("kp", "m1", 1, False, range(8, 16))
-        ts(B("pos", 0, 128), P(5, 0, 128), 63.5, Op.add)
-        cp(IND(B("lp"), B("pos", 128, 136)), B("lf"))
-        for h in range(2):
-            tt(B("m2", 1024 * h, 1024 * h + 1024), IND(B("csw"), B("pos", 64 * h, 64 * h + 64)),
-               B("xg", 1024 * h, 1024 * h + 1024), Op.max)
-        p1, p2 = B("pp", 0, 128), B("pp", 128, 256)
-        mm(P(2, 0, 128), B("dsg32"), B("lp"), True, False)
-        act(B("hp"), B("lp"), 1.0 / 128, 160.0 - 127.0 / 256)
-        act(p1, B("hp"), C(S128), C(S160))
-        mm(P(2, 0, 128), B("nid"), p1, False, True)
-        act(p2, P(2, 0, 128), 1.0, C(S64))
-        act(B("posf"), P(5, 0, 128), 1.0, 63.5)
-        for b in range(2):
-            for u in range(4):
-                s = 4 * b + u
-                mm(P(b, 128 * u, 128 * u + 128), B("cd", 128 * s, 128 * s + 128), p1, True, False)
-                mm(P(b, 128 * u, 128 * u + 128), B("cd", 128 * s, 128 * s + 128), p2, False, True)
-            act(B("gl", 512 * b, 512 * b + 512), P(b), 1.0, 0.0, Fn.Sign)
-        keys("kn", "m2", 0, True)
-        for s in range(8):
-            mm(P(7, 0, 128), B("ca", 128 * s, 128 * s + 128), B("gl", 128 * s, 128 * s + 128), s == 0, s == 7)
-        keys("kn", "m2", 1, True)
-        act(B("ks", 0, 64), P(6, 256, 320), 1.0, C(SQ))
-        act(B("rr"), P(7, 0, 128), 1.0 / 128, 192.25)
-        act(B("r128"), B("rr"), 128.0, -128.0 * 192)
-        act(B("ks", 64, 128), P(4, 256, 320), 1.0, C(SQ))
+            if rho == 0:
+                act(B("vh", 512 * h, 512 * h + 512), B("v0", 512 * h, 512 * h + 512), 0.5, 1472.25)
+            else:
+                mm(P(6 - h), B("pm16", 128 * rho - 128, 128 * rho), B("vo", 512 * h, 512 * h + 512), True, True)
+                act(B("vh", 512 * h, 512 * h + 512), P(6 - h), 0.5, 768.25)
+        sums(0)
         if rho == 0:
             ts(B("pti", 0, 64), B("pri"), 4, Op.arith_shift_right)
             ts(B("pti", 64, 128), B("pri"), 15, Op.bitwise_and)
-            cp(B("prf", 0, 128), B("pti"))
-        cp(IND(B("kq"), B("pos", 128, 132)), B("ks", 0, 64))
-        cp(B("tu"), B("prf", 128 * rho, 128 * rho + 64))
-        tt(B("com"), B("r128"), P(7, 0, 128), Op.subtract)
-        act(B("prow"), IND(B("posf"), B("tu")))
-        act(B("jb"), B("prf", 128 * rho + 64, 128 * rho + 128), 8.0)
-        mm(P(5, 0, 128), B("dbig"), B("ones"), True, False)
-        mm(P(5, 0, 128), B("dq"), B("ones"), False, False)
-        mm(P(5, 0, 128), B("dm"), B("com"), False, True)
-        mm(P(5, 128, 256), B("we"), B("com"), True, True)
-        mm(P(5, 256, 384), B("dsg"), p2, True, False)
-        mm(P(5, 256, 384), B("nds128"), p1, False, True)
-        cp(IND(B("kq"), B("pos", 132, 136)), B("ks", 64, 128))
+        repeat("idn", "ch", 0)
+        maxima("m1", 0, (0,))
+        sums(1)
+        totals(0, False)
+        maxima("m1", 0, (1, 2, 3))
+        mm(P(0), B("ch"), B("ny"), False, True)
+        signs(0)
+        repeat("idn", "ch", 1)
+        mm(P(1), B("ch"), B("ny"), False, False)
+        totals(1, True)
+        signs(1)
+        maxima("m1", 1)
+        keys("kp", "m1", 0, (0, 1))
+        counts(0)
+        keys("kp", "m1", 0, (2, 3))
+        counts(1)
+        ts(B("pos", 0, 8), P(7, 64, 72), 63.5, Op.add)
+        act(B("posb"), P(7, 64, 72))
+        keys("kp", "m1", 1, (0, 1))
+        mm(P(7, 72, 80), B("swp"), B("posb"), True, True)
+        keys("kp", "m1", 1, (2, 3))
+        p1, p2 = B("pp", 0, 128), B("pp", 128, 256)
+        cp(IND(B("lp"), B("pos", 0, 8)), B("lf"))
+        cp(IND(B("cp"), B("pos", 0, 8)), B("ch"))
+        ts(B("pos", 8, 16), P(7, 72, 80), 63.5, Op.add)
+        act(p1, B("lp"))
+        tt(p2, B("lp"), p1, Op.subtract)
+        act(B("cq"), IND(B("cp"), B("pos", 8, 16)))
+        mm(P(7, 0, 128), B("dbig"), B("ones"), True, False)
+        mm(P(7, 0, 128), B("dq"), B("ones"), False, False)
+        for b in range(2):
+            mm(P(b, 0, 128), B("cd", 512 * b, 512 * b + 128), p1, True, False)
+        for b in range(2):
+            for u in range(4):
+                s = 4 * b + u
+                if u:
+                    mm(P(b, 128 * u, 128 * u + 128), B("cd", 128 * s, 128 * s + 128), p1, True, False)
+                mm(P(b, 128 * u, 128 * u + 128), B("cd", 128 * s, 128 * s + 128), p2, False, True)
+                if s == 1:
+                    repeat("swp", "cq", 0)
+                    repeat("swp", "cq", 1)
+                    maxima("m2", 0)
+                    maxima("m2", 1)
+            act(B("gl", 512 * b, 512 * b + 512), P(b), 1.0, 0.0, Fn.Sign)
+        keys("kn", "m2", 0, (0, 1, 2))
+        for s in range(4):
+            mm(P(7, 0, 128), B("ca", 128 * s, 128 * s + 128), B("gl", 128 * s, 128 * s + 128), False, False)
+        keys("kn", "m2", 0, (3,))
+        act(B("ks", 0, 64), P(6, 256, 320), 1.0, C(SQ))
+        keys("kn", "m2", 1, (0,))
+        for s in range(4, 8):
+            mm(P(7, 0, 128), B("ca", 128 * s, 128 * s + 128), B("gl", 128 * s, 128 * s + 128), False, s == 7)
+        keys("kn", "m2", 1, (1, 2, 3))
+        act(B("ks", 64, 128), P(4, 256, 320), 1.0, C(SQ))
+        for a in range(8):
+            mm(P(3, 0, 128), B("cs", 112 - 16 * a, 240 - 16 * a), (T.gs[:, a:64:8, :], [("gs", 0, 64)]), a == 0, a == 7)
+        mm(P(6, 0, 128), B("d1"), B("ones"), True, False)
+        mm(P(6, 0, 128), B("d2"), B("ones"), False, False)
+        ts(B("rr"), P(7, 0, 128), ROUND, Op.add, -ROUND, Op.add)
+        cp(IND(B("kq"), B("pos", 0, 4)), B("ks", 0, 64))
+        tt(P(5, 0, 128), P(7, 0, 128), B("rr"), Op.subtract)
+        cp(IND(B("kq"), B("pos", 4, 8)), B("ks", 64, 128))
+        act(B("posf"), P(3, 0, 128), 1.0, 63.5)
+        act(P(4, 0, 128), p1, C(SQH), -0.5)
+        act(P(4, 128, 256), p2, C(SQL), 1.0 + 63.5 / 128)
         za = P(7, 256, 384)
-        mm(za, B("ds128"), p1, True, False)
         tt(B("kh"), B("kq"), P(5, 0, 128), Op.min)
-        tt(B("k32"), B("kq"), P(5, 0, 128), Op.min)
-        tt(B("kl"), B("k32"), B("kh"), Op.subtract)
+        tt(P(5, 128, 256), B("kq"), P(5, 0, 128), Op.min)
+        tt(B("kl"), P(5, 128, 256), B("kh"), Op.subtract)
+        act(B("com"), P(5, 0, 128), -1.0 / 1024, C(QC))
+        if rho == 0:
+            cp(B("prf", 0, 128), B("pti"))
+        cp(B("tu"), B("prf", 128 * rho, 128 * rho + 64))
         for b in range(4):
             mm(P(b, 0, 128), B("rd", 512 * b, 512 * b + 128), B("kh"), True, False)
         for b in range(4):
@@ -470,47 +521,59 @@ def rank_program(g, core, T, topo):
                 act(B("gk", 512 * b, 512 * b + 512), P(b), 1.0, 0.0, Fn.Sign)
             else:
                 ts(B("gk", 512 * b, 512 * b + 512), P(b), -1.0, Op.max, 1.0, Op.min)
+            if b == 0:
+                mm(P(5, 256, 384), B("we"), B("com"), True, True)
+                act(B("ew"), P(5, 256, 384), EXPC, 0.0, Fn.Exp)
+            if b == 1:
+                for u in range(2):
+                    tt(P(4, 256 + 128 * u, 384 + 128 * u), B("ew"), P(4, 128 * u, 128 * u + 128), Op.mult)
+        act(B("jb"), B("prf", 128 * rho + 64, 128 * rho + 128), 8.0)
         for s in range(16):
-            mm(za, B("ra", 128 * s, 128 * s + 128), B("gk", 128 * s, 128 * s + 128), False, s == 15)
-        mm(P(1, 0, 64), B("idn"), B("jb"), True, False)
-        for j in range(16):
-            mm(P(1, 0, 64), B("kp", 15 - j, 143 - j), B("prow", j, 1024, 16), False, j == 15)
-        if rho == 0:
-            act(B("vh"), B("v0"), 0.5, 1472.25)
-        else:
-            for h in range(2):
-                mm(P(2 + h), B("pm16", 128 * rho - 128, 128 * rho), B("vo", 512 * h, 512 * h + 512), True, True)
-                act(B("vh", 512 * h, 512 * h + 512), P(2 + h), 0.5, 768.25)
-        ts(B("t1"), za, 4096.0, Op.mult, 0.0, Op.min)
-        tt(B("t2"), B("t1"), P(5, 128, 256), Op.max)
-        tt(B("z", 0, 128), B("t2"), za, Op.add)
-        tt(B("z", 128, 256), B("z", 0, 128), P(5, 256, 384), Op.add)
-        clamp(0, 0, 2)
-        ts(B("z", 256, 512), B("z", 0, 256), -2048.0, Op.add)
-        clamp(1, 0, 2)
-        clamp(0, 2, 4)
-        clamp(1, 2, 4)
-        for e in range(2, 16):
-            clamp(e, 0, 4)
-        ts(B("pru"), P(1, 0, 64), 0.125, Op.mult)
-        ts(B("lu2"), P(6, 0, 128), C(KAP), Op.add)
-        ts(B("g1", 0, 1024), IND(B("w"), B("lu2", 0, 64)), 0.5, Op.mult)
-        act(B("g1", 1024, 2048), IND(B("w"), B("lu2", 64, 128)), 0.5)
-        act(B("lpos"), P(6, 0, 128), 1.0, C(KAP))
-        act(B("lf2"), IND(B("lpos"), B("pos", 128, 136)))
+            mm(za, B("ra", 128 * s, 128 * s + 128), B("gk", 128 * s, 128 * s + 128), s == 0, s == 15)
+        act(B("pwb"), za, EXPC, -117.5 * LN2, Fn.Exp)
+        act(B("pwa"), za, EXPC, -5.5 * LN2, Fn.Exp)
+        act(P(5, 384, 512), za, 2.0 ** 99, 0.0, Fn.Relu)
+        act(B("prow"), IND(B("posf"), B("tu")))
         if not last:
             mm(P(0, 0, 128), B("pm32", 128 * rho, 128 * rho + 128), B("prf", 128 * rho, 128 * rho + 128), True, True)
-            mm(P(7, 0, 128), B("pm32", 128 * rho, 128 * rho + 128), B("lf2"), True, True)
             act(B("prf", 128 * rho + 128, 128 * rho + 256), P(0, 0, 128))
-            act(B("lf"), P(7, 0, 128))
-        cuts = CUTS if last else (0, 512, 1024)
+        for u in range(2):
+            tt(B("z", 128 * u, 128 * u + 128), B("pwb"), P(4, 128 * u, 128 * u + 128), Op.mult)
+        tt(B("pwc"), B("pwa"), P(5, 384, 512), Op.max)
+        for w in range(2):
+            clamp(w, 0)
+        for u in range(2):
+            tt(B("z", 256 + 128 * u, 384 + 128 * u), B("pwc"), P(4, 256 + 128 * u, 384 + 128 * u), Op.mult)
+        for w in range(2, 8):
+            clamp(w, 0)
+        for w in range(8):
+            clamp(w, 1, w == 7)
+        cp(B("t128"), P(6, 0, 128))
+        tt(B("tlow"), P(6, 0, 128), B("t128"), Op.subtract)
+        mm(P(1, 0, 64), B("idn"), B("jb"), True, False)
+        for j in range(8):
+            mm(P(1, 0, 64), B("kp", 15 - j, 143 - j), B("prow", j, 1024, 16), False, False)
+        mm(P(7, 0, 128), B("ut"), B("t128"), True, False)
+        mm(P(7, 0, 128), B("up"), B("tlow"), False, True)
+        for j in range(8, 16):
+            mm(P(1, 0, 64), B("kp", 15 - j, 143 - j), B("prow", j, 1024, 16), False, j == 15)
+        ts(B("lu2"), P(7, 0, 128), C(KAP), Op.add)
+        act(B("lpos"), P(7, 0, 128), 1.0, C(KAP))
+        ts(B("g1", 0, 1056), IND(B("w"), B("lu2", 0, 66)), 0.5, Op.mult)
+        act(B("g1", 1056, 2048), IND(B("w"), B("lu2", 66, 128)), 0.5)
+        ts(B("pru"), P(1, 0, 64), 0.125, Op.mult)
+        act(B("lf2"), IND(B("lpos"), B("pos", 0, 8)))
+        if not last:
+            mm(P(7, 128, 256), B("pm32", 128 * rho, 128 * rho + 128), B("lf2"), True, True)
+            act(B("lf"), P(7, 128, 256), C(SG), C(SOFF))
+        cuts = CUTS if last else VCUTS
         for lo, hi in zip(cuts[:-1], cuts[1:]):
             tt(B("vo", lo, hi), IND(B("g1"), B("pru", lo // 16, hi // 16)), B("vh", lo, hi), Op.add)
             if last:
                 ts(B("vb", lo, hi), B("vo", lo, hi), -1408.0, Op.add)
         if not last:
-            cp(B("lu"), B("lf"))
-            table("vo", arr[rho], 1536.0, False)
+            ts(B("lu"), B("lf"), C(SG), Op.mult, -24512.5, Op.add)
+            table("vo", arr[rho], 1536.0, VCUTS, 3)
 
     slot2 = arr[2].index(rank)
     own = slice(16 * slot2, 16 * slot2 + 16)

@@ -5,8 +5,9 @@ from concourse.mybir import AluOpType as Op, ActivationFunctionType as Fn
 BF, F32, F16, I32, U16 = "bfloat16", "float32", "float16", "int32", "uint16"
 N = 8
 DS = (4, 1, 7)
-CUTS = (0, 640, 1024)
-VCUTS = (0, 256, 512, 1024)
+CUTS = (0, 576, 1024)
+VCUTS = (0, 128, 512, 1024)
+SITES = (0, 40, 92, 112, 128)
 LN2 = math.log(2.0)
 INNER = {0: 16, 1: 16}
 EXPC = 7 * LN2 / 128
@@ -25,37 +26,32 @@ SCRATCH = {
     "xs0": dr(64, BF), "xl0": dr(64, BF), "xs1": dr(64, BF), "xl1": dr(64, BF),
     "ss": dr(16, I32), "sll": dr(16, I32), "prs": dr(8, I32), "prl": dr(8, I32),
     "ys": dr(16, F32), "yll": dr(16, F32),
-    "vs0": dr(80, BF), "vl0": dr(80, BF), "vs1": dr(48, BF), "vl1": dr(48, BF),
+    "vs0": dr(CUTS[1] // 8, BF), "vl0": dr(CUTS[1] // 8, BF),
+    "vs1": dr(128 - CUTS[1] // 8, BF), "vl1": dr(128 - CUTS[1] // 8, BF), "vb": sb(1024, BF),
     "p0": ("psum", [128, 32, 16], F32), "p1": ("psum", [128, 32, 16], F32),
     "p2": ("psum", [128, 512], F32), "p3": ("psum", [128, 512], F32), "p4": ("psum", [128, 512], F32),
     "p5": ("psum", [128, 512], F32), "p6": ("psum", [128, 512], F32), "p7": ("psum", [128, 512], F32),
-    "ci": sb(8, I32), "cf": sb(40, F32), "pg": sb(8, F32),
-    "rowx": sb(256, BF), "row16": sb(128, BF), "rowq": sb(256, BF), "row32": sb(128, BF), "rowg": sb(512, BF),
-    "zero": sb(128, BF), "ones": sb(128, BF), "tie": sb(128, BF), "cs": sb(240, BF), "half": sb(8, BF),
-    "trow": sb(1024, BF),
-    "idn": sb(128, BF), "nid": sb(128, BF), "dsg": sb(128, BF), "ndsg": sb(128, BF), "id16": sb(128, BF),
+    "ci": sb(12, I32), "cf": sb(40, F32), "ind": sb(12, F32), "rowx": sb(160, BF),
+    "ones": sb(128, BF), "tie": sb(128, BF), "cs": sb(240, BF), "half": sb(8, BF), "mask": sb(1024, BF),
+    "trow": ("sbuf", [128, 64, 16], BF), "ny": ("sbuf", [128, 32, 16], BF), "vv": ("sbuf", [128, 8, 128], BF),
+    "idn": sb(128, BF), "nid": sb(128, BF), "dsg": sb(128, BF), "id16": sb(128, BF),
     "dbig": sb(128, BF), "dq": sb(128, BF),
-    "we": sb(128, BF), "we1": sb(128, BF), "we2": sb(128, BF), "swp": sb(128, BF),
-    "d1": sb(128, BF), "d2": sb(128, BF), "ut": sb(128, BF), "up": sb(128, BF),
-    "ptb": sb(8, BF), "pt": sb(8, F32), "ow": sb(8 * 152, BF),
-    "vv": sb(1024, BF), "yy": sb(1024, BF), "ny": sb(512, BF),
-    "kp": sb(144, BF), "kn": sb(144, BF), "qs": sb(256, BF),
-    "rd": sb(2048, BF), "ra": sb(2048, BF),
+    "we1": sb(128, BF), "we2": sb(128, BF), "swp": sb(128, BF), "sw16": sb(128, BF),
+    "d1": sb(128, BF), "d2": sb(128, BF), "d3": sb(128, BF), "ut": sb(128, BF), "up": sb(128, BF),
+    "ptb": sb(8, BF), "pt": sb(8, F32), "ow": sb(8 * 152, BF), "yy": sb(1024, BF),
+    "kp": sb(144, BF), "kn": sb(144, BF), "id64": sb(64, BF), "qs": sb(128, BF), "q1": sb(64, BF), "q2": sb(96, BF),
+    "rd": sb(1024, BF), "ra": ("sbuf", [128, 17, 64], BF), "cd": sb(512, BF), "ca": ("sbuf", [128, 9, 64], BF),
     "pm32": sb(256, F32), "pm16": sb(256, BF),
-    "v0": sb(1024, BF), "vo": sb(1024, F16), "vh": sb(1024, F32), "vb": sb(1024, BF),
-    "w": sb(8192, BF), "xg": sb(2048, BF), "g1": sb(2048, BF),
+    "xo": sb(1024, BF), "v0": sb(1024, BF), "vo": sb(1024, F16), "vh": sb(1024, F32),
+    "w": sb(8192, BF), "xg": sb(2048, BF), "xs": sb(2048, F16), "g1": sb(2048, BF),
     "sli": sb(128, I32), "pri": sb(64, I32), "prf": sb(384, F32), "pru": sb(64, U16),
     "pti": sb(128, I32), "tu": sb(64, U16), "jb": sb(64, BF), "posf": sb(128, BF), "prow": sb(1024, BF),
     "lu": sb(128, U16), "lf": sb(128, F32), "lu2": sb(128, U16), "lf2": sb(128, F32), "lpos": sb(128, F32),
-    "lp": sb(128, F32), "pp": sb(256, BF),
-    "rowa": sb(192, BF), "rowb": sb(192, BF), "rowc": sb(192, BF), "rowy": sb(128, BF), "q1": sb(128, BF),
-    "q2": sb(192, BF), "cd": sb(1024, BF), "ca": sb(1024, BF),
-    "ch": sb(128, F16), "cp": sb(128, F32), "cq": sb(128, F16),
+    "lp": sb(128, F32), "pp": sb(256, BF), "cp": sb(128, F32), "cq": sb(128, F16),
     "gs": ("sbuf", [128, 64, 16], BF), "pos": sb(16, U16), "posb": sb(8, BF),
-    "m1": sb(2048, F16), "m2": sb(2048, F16),
-    "gl": sb(1024, BF), "gk": sb(2048, BF),
+    "m1": sb(2048, F16), "m2": sb(2048, F16), "gl": sb(1024, BF), "gk": sb(2048, BF),
     "rr": sb(128, F32), "com": sb(128, BF),
-    "ks": sb(128, F32), "kq": sb(128, F32), "kh": sb(128, F16), "kl": sb(128, F16),
+    "ks": sb(128, F32), "kq": sb(128, F32), "kk": sb(256, F16),
     "ew": sb(128, BF), "pwa": sb(128, BF), "pwb": sb(128, BF), "pwc": sb(128, BF),
     "z": sb(512, BF), "oh": sb(4096, BF), "t128": sb(128, F16), "tlow": sb(128, BF),
 }
@@ -144,13 +140,23 @@ def rank_program(g, core, T, topo):
     rank = T.rank_of(core)
     if rank is None:
         return
-    ops, nd = [], [0]
+    ops, nd, fresh = [], [0], [0]
     arr = [arrangement(d) for d in DS]
 
     def B(name, lo=0, hi=None, step=1):
         if hi is None:
             hi = T[name].shape[1]
         return (T[name][:, lo:hi:step] if step > 1 else T[name][:, lo:hi], [(name, lo, hi)])
+
+    def G(name, lo, hi, step=1):
+        return (T[name][:, lo:hi:step, :], [(name, lo, hi)])
+
+    def piece(name, ap):
+        fresh[0] += 1
+        return (ap, [(name, 4096 + fresh[0], 4097 + fresh[0])])
+
+    def whole(name, ap):
+        return (ap, [(name, 0, 8192)])
 
     def P(bank, lo=0, hi=512):
         t, n = T["p%d" % bank], INNER.get(bank)
@@ -193,6 +199,10 @@ def rank_program(g, core, T, topo):
             f = lambda e: e.tensor_scalar(out[0], a[0], val(s1), val(s2), o0, o1)
         ops.append(("dve", "dve", f, sides(a, s1, s2), out[1]))
 
+    def running(out, keep, a):
+        ops.append(("dve", "dve", lambda e: e.tensor_tensor_scan(out[0], keep[0], a[0], 0.0, Op.mult, Op.add),
+                    keep[1] + a[1], out[1]))
+
     def ms(out, c):
         ops.append(("dve", "dve", lambda e: e.memset(out[0], c), [], out[1]))
 
@@ -206,6 +216,10 @@ def rank_program(g, core, T, topo):
         else:
             f = lambda e: e.iota(out[0], pat, 0, cm)
         ops.append(("g", "g", f, [], out[1]))
+
+    def diagonal(out, in_, first):
+        ops.append(("g", "g", lambda e: e.affine_select(out[0], in_[0], [[-1, 16]], Op.is_equal, 0.0, -first, 1),
+                    in_[1], out[1]))
 
     def dma(q, out, in_):
         ops.append((q, "d%d" % nd[0], lambda e: e.dma_start(out[0], in_[0]), in_[1], out[1]))
@@ -225,7 +239,8 @@ def rank_program(g, core, T, topo):
         ops.append((None, "a" + tag, None, [], [(dst, k, k + 1) for k in range(N) if k != own]))
 
     rows = slice(16 * rank, 16 * rank + 16)
-    slot0 = arr[0].index(rank)
+    slot0, slot2 = arr[0].index(rank), arr[2].index(rank)
+    own = slice(16 * slot2, 16 * slot2 + 16)
     dma("sync", D("xs0"), (T.x[:, 0:512], []))
     dma("act", D("xs1"), (T.x[:, 512:1024], []))
     dma("sync", D("ss"), (T.sl[:], []))
@@ -234,21 +249,13 @@ def rank_program(g, core, T, topo):
     dma("sync", D("prs"), (T.prey[:], []))
     dma("sync", D("sll", slot0), (T.sl[rows, :], []))
     dma("sync", D("prl", slot0), (T.prey[rows, :], []))
+    dma("sync", (T.xo[0:16, :], [("xo", 0, 1024)]), (T.x[rows, :], []))
     iota(B("ci", 0, 1), [[0, 1]], 1, False)
-    iota(B("pg"), [[-16, 8]], 1)
-    iota(B("row16"), [[0, 8], [1, 16]], 0)
-    iota(B("rowx"), [[1, 256]], 0)
-    iota(B("rowq"), [[0, 2], [1, 32], [32, 4]], 0)
+    iota(B("rowx"), [[1, 160]], 0)
     exchange("x0", "xs0", lambda r: r, "xl0", slot0)
     exchange("x1", "xs1", lambda r: r, "xl1", slot0)
     exchange("sl", "ss", lambda r: r, "sll", slot0)
     exchange("pr", "prs", lambda r: r, "prl", slot0)
-    iota(B("rowy"), [[1, 16], [16, 8]], 0)
-    iota(B("rowa"), [[1, 24], [0, 4], [1, 2]], 0)
-    iota(B("rowb"), [[1, 24], [32, 4], [-15, 2]], 0)
-    iota(B("row32"), [[32, 4], [0, 32]], 0)
-    iota(B("rowg"), [[0, 4], [16, 8], [0, 16]], 0)
-    iota(B("trow"), [[16, 8], [0, 8], [1, 16]], 0)
     arrival("x0", "xl0", slot0)
     arrival("x1", "xl1", slot0)
     arrival("sl", "sll", slot0)
@@ -256,114 +263,100 @@ def rank_program(g, core, T, topo):
     dma("sync", B("v0", 0, 512), D("xl0"))
     dma("sync", B("v0", 512, 1024), D("xl1"))
     dma("sync", B("sli"), D("sll"))
-    dma("g", B("pri"), D("prl"))
 
-    ms(B("zero"), 0.0)
     ms(B("ones"), 1.0)
+    ms(B("mask"), 1.0)
+    for k, m in enumerate((16, 31, 112, 96, 7, 8, 1, 63, 64)):
+        ts(B("ci", k + 1, k + 2), B("ci", 0, 1), m, Op.bitwise_and)
+    ms(B("mask", 0, 1024, 16), 0.0)
+    cp(B("cf", 0, 10), B("ci", 0, 10))
     ms(B("tie"), -1.0 / 2048)
     ms(B("half"), 0.5)
-    ms(B("cs", 0, 112), 0.0)
-    ms(B("cs", 112, 128), 0.5)
-    ms(B("cs", 128, 240), 0.0)
-    for k, m in enumerate((16, 31, 112, 96, 7, 8, 1)):
-        ts(B("ci", k + 1, k + 2), B("ci", 0, 1), m, Op.bitwise_and)
-    cp(B("cf", 0, 8), B("ci", 0, 8))
-    for k in range(8):
-        ts(B("vv", 128 * k, 128 * k + 128), B("row16"), B("pg", k, k + 1), Op.is_equal)
-    (PP, B16, E, G16, G32, W7, H8, O1, SG, SQ, SW, U15, U32, KAP, TIE, A2, A32, S64P, NSG,
-     SQH, SQL, SOFF, NN, K1, K2, CU, CU1, WT, WP, Q4, QC) = range(31)
-    ts(C(SG), C(B16), -0.125, Op.mult, 1.0, Op.add)
+    (PP, B16, E, G16, G32, W7, H8, O1, P63, B64, SG, SQ, SW, U15, U32, KAP, TIE, A2, A32, S64P, ONCE,
+     SQH, SQL, SOFF, NN, K1, K2, CU, CU1, WT, WP, Q4, QC) = range(33)
     ts(B("idn"), B("rowx", 0, 128), C(PP), Op.is_equal)
     ts(C(S64P), C(B16), -8.0, Op.mult, 64.0, Op.add)
-    ts(C(NSG), C(B16), 0.125, Op.mult, -1.0, Op.add)
-    ts(B("qs"), B("rowq"), C(PP), Op.is_equal, C(S64P), Op.mult)
+    ts(C(SG), C(B16), -0.125, Op.mult, 1.0, Op.add)
+    ts(B("ind", 0, 8), B("rowx", 0, 128, 16), C(G16), Op.is_equal)
+    ts(B("ind", 8, 12), B("rowx", 0, 128, 32), C(G32), Op.is_equal)
+    ts(B("id64"), B("rowx", 0, 64), C(P63), Op.is_equal, C(S64P), Op.mult)
+    act(B("nid"), B("idn"), -1.0)
+    act(B("dsg"), B("idn"), C(SG))
+    act(B("ptb"), B("rowx", 0, 8), -14 * LN2, 114 * LN2, Fn.Exp)
+    ms(G("ra", 0, 17), 0.0)
+    for k in range(4):
+        cp(piece("qs", T.qs[:, 64 * (k // 2) + k % 2:64 * (k // 2) + 64:2]), B("id64", 32 * (k % 2), 32 * (k % 2) + 32))
+    for k in range(4):
+        cp(piece("q1", T.q1[:, k:64:4]), B("id64", 16 * k, 16 * k + 16))
+    ms(G("ca", 0, 9), 0.0)
+    cp(piece("vv", T.vv[:, :, 0:16]), B("idn"))
     ts(C(U15), C(G16), 15.0, Op.add)
     ts(C(U32), C(G32), 32.0, Op.add)
     ts(C(KAP), C(O1), -173311.5, Op.mult, 8191.5, Op.add)
-    ts(C(TIE), C(PP), -1.0 / 2048, Op.mult)
-    ts(C(A2), C(B16), 0.125, Op.mult, -2.0, Op.add)
-    ts(C(A32), C(B16), -2.0, Op.mult, 32.0, Op.add)
-    ts(C(NN), C(W7), 2.0, Op.mult, C(B16), Op.add)
-    ts(C(CU), C(W7), 2.0, Op.mult, C(G16), Op.add)
-    ts(C(WT), C(H8), -127.0 / 8, Op.mult, 128.0, Op.add)
-    ts(C(WP), C(H8), -127.0 * 16, Op.mult, 16384.0, Op.add)
-    ts(C(SQH), C(SG), 1.0 / 16384, Op.mult)
-    ts(C(SQL), C(SG), 1.0 / 128, Op.mult)
-    ts(C(SOFF), C(SG), 24512.5, Op.mult)
+    ts(C(ONCE), C(B64), -1.0 / 128, Op.mult, 1.0, Op.add)
+    for dst, src in ((T.q2[:, 0:64:2], T.q1[:, 1:64:2]), (T.q2[:, 64:96:2], T.q1[:, 1:32:2]),
+                     (T.q2[:, 1:60:2], T.q1[:, 4:64:2]), (T.q2[:, 61:96:2], T.q1[:, 0:36:2])):
+        cp(piece("q2", dst), whole("q1", src))
+    columns = [(TIE, PP, -1.0 / 2048, 0.0), (A2, B16, 0.125, -2.0), (A32, B16, -2.0, 32.0), (NN, W7, 2.0, C(B16)),
+               (CU, W7, 2.0, C(G16)), (WT, H8, -127.0 / 8, 128.0), (WP, H8, -127.0 * 16, 16384.0),
+               (SQH, SG, 1.0 / 16384, 0.0), (SQL, SG, 1.0 / 128, 0.0), (SOFF, SG, 24512.5, 0.0), (SW, SG, 16.0, C(PP)),
+               (K1, NN, 256.0, -6400.0), (K2, NN, -1.0, -129.0), (CU1, CU, 1.0, 1.0)]
+    for k, (dst, src, times, plus) in enumerate(columns):
+        if k % 4 == 0 and k < 12:
+            n = 16 << k // 4
+            cp(piece("vv", T.vv[:, :, n:2 * n]), whole("vv", T.vv[:, :, 0:n]))
+        ts(C(dst), C(src), times, Op.mult, plus, Op.add)
     ts(C(SQ), C(E), C(SG), Op.mult, 1.0 / 64, Op.mult)
-    ts(C(SW), C(SG), 16.0, Op.mult, C(PP), Op.add)
-    ts(C(K1), C(NN), -25.0, Op.add, 256.0, Op.mult)
-    ts(C(K2), C(NN), -1.0, Op.mult, -129.0, Op.add)
-    ts(C(CU1), C(CU), 1.0, Op.add)
+    ms(B("cs", 0, 112), 0.0)
+    ms(B("cs", 112, 128), 0.5)
+    ms(B("cs", 128, 240), 0.0)
     ts(C(Q4), C(SQ), 256.0, Op.mult)
     ts(C(QC), C(SQ), 0.25, Op.mult, 32.0, Op.add)
-    act(B("nid"), B("idn"), -1.0)
-    act(B("dsg"), B("idn"), C(SG))
-    act(B("ndsg"), B("idn"), C(NSG))
-    act(B("ptb"), B("rowx", 0, 8), -14 * LN2, 114 * LN2, Fn.Exp)
-    for k in range(8):
-        ts(B("yy", 128 * k, 128 * k + 128), B("zero"), C(G16), Op.add, 16.0 * k, Op.is_equal)
+    for a in range(8):
+        ts(B("yy", 128 * a, 128 * a + 128), B("ones"), B("ind", a, a + 1), Op.mult, 1.0 / 16, Op.mult)
+        ts(piece("ny", T.ny[:, a:32:8, :]), B("ones", 0, 64), B("ind", a, a + 1), Op.mult, -1.0 / 16, Op.mult)
+        cp(piece("trow", T.trow[0:1, a:64:8, :]), (T.rowx[0:1, 0:128], [("rowx", 0, 128)]))
     ts(B("swp"), B("rowx", 0, 128), C(SW), Op.is_equal)
+    ts(B("sw16"), B("rowx", 0, 128), C(SW), Op.is_equal, 1.0 / 16, Op.mult)
     ts(B("kp"), B("rowx", 0, 144), C(U15), Op.is_equal, 8.0, Op.mult)
     ts(B("kn"), B("rowx", 0, 144), C(U15), Op.is_equal, -8.0, Op.mult)
-    ts(B("id16"), B("idn"), 1.0 / 16, Op.mult)
-    ts(B("dbig"), B("idn"), 32768.0, Op.mult)
-    ts(B("dq"), B("idn"), C(Q4), Op.mult)
-    ts(B("we2"), B("idn"), C(A32), Op.mult)
+    for name, times in (("id16", 1.0 / 16), ("dbig", 32768.0), ("dq", C(Q4)), ("we2", C(A32)),
+                        ("d1", C(K1)), ("d2", C(K2)), ("d3", -127.0 / 256)):
+        ts(B(name), B("idn"), times, Op.mult)
     cp(B("pt"), B("ptb"))
-    ts(B("q1"), B("rowy"), C(PP), Op.is_equal, C(S64P), Op.mult)
-    ts(B("rowc"), B("rowa"), 16.0, Op.is_lt, 16.0, Op.mult)
-    ts(B("d1"), B("idn"), C(K1), Op.mult)
-    tt(B("rowc"), B("rowc"), B("rowb"), Op.add)
-    ts(B("d2"), B("idn"), C(K2), Op.mult)
-    ts(B("q2"), B("rowc"), C(PP), Op.is_equal, C(S64P), Op.mult)
+    for q in range(4):
+        ts(B("we1", 32 * q, 32 * q + 32), B("ones", 0, 32), B("ind", 8 + q, 9 + q), Op.mult, C(A2), Op.mult)
     ts(B("ut"), B("rowx", 0, 128), C(CU1), Op.is_equal, C(WT), Op.mult)
     ts(B("up"), B("rowx", 0, 128), C(CU), Op.is_equal, C(WP), Op.mult)
-    act(B("we1"), B("swp"), -127.0 / 256)
     for w in range(8):
         ts(B("ow", 152 * w, 152 * w + 152), B("rowx", 8 - w, 160 - w), C(U32), Op.is_equal, B("pt", w, w + 1), Op.mult)
-    tt(B("d2"), B("d2"), B("we1"), Op.add)
     for k in range(2):
         for gm in range(8):
             gn = arr[k + 1].index(arr[k][gm])
-            cp(B("pm16", 128 * k + 16 * gn, 128 * k + 16 * gn + 16), B("idn", 16 * gm, 16 * gm + 16))
-    ts(B("we1"), B("row32"), C(G32), Op.is_equal, C(A2), Op.mult)
-    cp(B("pm32"), B("pm16"))
-    tt(B("we"), B("we1"), B("we2"), Op.add)
-    ts(B("ny"), B("rowg"), C(G16), Op.is_equal, -1.0, Op.mult)
-    for b in range(8):
-        for u in range(4):
-            s = 4 * (b % 4) + u + 1
-            o = P(b, 128 * u, 128 * u + 128)
-            q0, q1 = B("qs", 0, 128), B("qs", 4 * s, 4 * s + 128)
-            if b < 4:
-                mm(o, B("idn"), q0, True, False)
-                mm(o, B("nid"), q1, False, True)
-            elif s < 16:
-                mm(o, q0, B("dsg"), True, False)
-                mm(o, q1, B("ndsg"), False, True)
-            else:
-                mm(o, q0, B("dsg"), True, True)
-        act(B("rd" if b < 4 else "ra", 512 * (b % 4), 512 * (b % 4) + 512), P(b))
-    for b in range(4):
-        for u in range(4):
-            t = 4 * (b % 2) + u
-            o = P(b, 128 * u, 128 * u + 128)
-            q1 = B("q2", 8 * t, 8 * t + 128)
-            if b < 2:
-                mm(o, B("idn"), B("q1"), True, False)
-                mm(o, B("nid"), q1, False, True)
-            else:
-                mm(o, B("q1"), B("dsg"), True, False)
-                mm(o, q1, B("dsg"), False, True)
-        act(B("cd" if b < 2 else "ca", 512 * (b % 2), 512 * (b % 2) + 512), P(b), 1.0 if b < 2 else 1024.0)
+            diagonal(B("pm16", 128 * k + 16 * gn, 128 * k + 16 * gn + 16), B("ones", 0, 16), 16 * gm)
+        if k == 0:
+            dma("g", B("pri"), D("prl"))
+    for b in range(3):
+        for u in range(8):
+            o, s = P(2 + b, 64 * u, 64 * u + 64), 8 * b + u + 1
+            mm(o, B("idn"), whole("qs", T.qs[:, 0:64]) if b < 2 else whole("q1", T.q1[:, 0:64]), True, False)
+            mm(o, B("nid"), whole("qs", T.qs[:, 2 * s:2 * s + 64]) if b < 2 else whole("q2", T.q2[:, 4 * u:4 * u + 64]),
+               False, True)
+        act(B("rd", 512 * b, 512 * b + 512) if b < 2 else B("cd"), P(2 + b))
+    for b in range(12):
+        name, k = ("rd", b) if b < 8 else ("cd", b - 8)
+        mm(P(5 + b // 8, 64 * k, 64 * k + 64), (T[name][0:64, 128 * k:128 * k + 128], [(name, 128 * k, 128 * k + 128)]),
+           (T.dsg[0:64, 0:64], [("dsg", 0, 64)]), True, True)
+    act(G("ra", 1, 15, 2), P(5, 0, 448))
+    act(G("ra", 15, 16), P(5, 448, 512), C(ONCE))
+    act(G("ca", 1, 9, 2), P(6, 0, 256), 1024.0, 0.0, Fn.Abs)
 
-    def table(src, ar, off, cuts, first):
+    def table(src, ar, off, cuts, first, done=None):
         k = 0
         for lo, hi in zip(cuts[:-1], cuts[1:]):
-            for gm in range(8):
+            for gm in (gm for gm in range(8) if gm != done):
                 bank = P(k % 8, 0, hi - lo)
-                mm(bank, B("vv", 128 * gm, 128 * gm + 128), B(src, lo, hi), True, True)
+                mm(bank, whole("vv", T.vv[:, gm, :]), B(src, lo, hi), True, True)
                 o = B("w", 1024 * ar[gm] + lo, 1024 * ar[gm] + hi)
                 if k < first or k % 2 == 1:
                     act(o, bank, 1.0, -off)
@@ -371,9 +364,12 @@ def rank_program(g, core, T, topo):
                     ts(o, bank, -off, Op.add)
                 k += 1
 
+    def S(lo, hi):
+        return B("xs", 16 * lo + 15, 16 * hi, 16)
+
     def repeat(mat, src, h):
         for u in range(4):
-            mm((T["p%d" % (2 + h)][:, u:256:4], P(2 + h, 0, 256)[1]), B(mat), B(src, 64 * h, 64 * h + 64), True, True)
+            mm((T["p%d" % (2 + h)][:, u:256:4], P(2 + h, 0, 256)[1]), B(mat), src, True, True)
 
     def maxima(name, h, ks=range(4)):
         for k in ks:
@@ -387,6 +383,32 @@ def rank_program(g, core, T, topo):
                 mm(P(6 - 2 * h, 256, 320), B(mat, 15 - j, 143 - j), B(name, lo + u, lo + 256, 4),
                    j == 0 and name == "m1", j == 15 and name == "m2")
 
+    def totals(b, stop):
+        for a in range(8):
+            mm((T["p%d" % b][:, a:32:8, :], P(b)[1]), B("yy", 128 * a, 128 * a + 128), S(64 * b, 64 * b + 64),
+               False, stop and a == 7)
+
+    def signs(b):
+        act(G("gs", 32 * b, 32 * b + 32), P(b), -1.0, C(TIE), Fn.Sign)
+
+    def counts(b):
+        for n in range(4 * b, 4 * b + 4):
+            mm(P(7, 64 + n, 65 + n), G("gs", 8 * n, 8 * n + 8), B("half", 0, 1), True, True)
+
+    def half(x, h, lo, hi):
+        name = x if isinstance(x, str) else "p%d" % x
+        return (T[name][64 * h:64 * h + 64, lo:hi], (B(x, lo, hi) if name == x else P(x, lo, hi))[1])
+
+    def pairs(mat, src, bank):
+        for s in (2 * bank, 2 * bank + 1):
+            mm(P(bank, 256 * (s % 2), 256 * (s % 2) + 256), B(mat, 128 * s, 128 * s + 128), B(src), True, True)
+
+    def tally(out, mat, src, bank, start, stop):
+        for k in range(4):
+            s, h = 2 * bank + k // 2, k % 2
+            mm(out, G(mat, 2 * s + 1 - h, 2 * s + 3 - h), B(src, 256 * s + 128 * h, 256 * s + 128 * h + 128),
+               start and k == 0, stop and k == 3)
+
     def clamp(w, side, last=False):
         lo = 512 * w + 256 * side
         ts(B("oh", lo, lo + 256), B("z", 256 * side, 256 * side + 256),
@@ -395,157 +417,134 @@ def rank_program(g, core, T, topo):
             at = 152 * w + 8 + 16 * side - 8 * u
             mm(P(6, 0, 128), B("ow", at, at + 128), B("oh", lo + 128 * u, lo + 128 * u + 128), False, last and u == 1)
 
-    def sums(h):
-        for j in range(16):
-            mm(P(4 + 3 * h, 0, 64), B("id16"), B("xg", 1024 * h + j, 1024 * h + 1024, 16), j == 0, j == 15)
-        cp(B("ch", 64 * h, 64 * h + 64), P(4 + 3 * h, 0, 64))
-
-    def totals(b, stop):
-        for a in range(8):
-            mm((T["p%d" % b][:, a:32:8, :], P(b)[1]), B("yy", 128 * a, 128 * a + 128),
-               B("ch", 64 * b, 64 * b + 64), False, stop and a == 7)
-
-    def signs(b):
-        act((T.gs[:, 32 * b:32 * b + 32, :], [("gs", 32 * b, 32 * b + 32)]), P(b), -1.0, C(TIE), Fn.Sign)
-
-    def counts(b):
-        for n in range(4 * b, 4 * b + 4):
-            mm(P(7, 64 + n, 65 + n), (T.gs[:, 8 * n:8 * n + 8, :], [("gs", 8 * n, 8 * n + 8)]), B("half", 0, 1), True, True)
-
-    table("v0", arr[0], 128.0, (0, 512, 1024), 0)
+    for h in range(2):
+        mm(P(4 + h), whole("vv", T.vv[0:16, 0, :]), (T.xo[0:16, 512 * h:512 * h + 512], [("xo", 0, 1024)]), True, True)
+        act(B("w", 1024 * rank + 512 * h, 1024 * rank + 512 * h + 512), P(4 + h), 1.0, -128.0)
+    table("v0", arr[0], 128.0, (0, 512, 1024), 0, slot0)
     cp(B("lu"), B("sli"))
-    ts(B("lf"), B("sli"), C(SG), Op.mult, C(SOFF), Op.add)
     for rho in range(3):
         last = rho == 2
-        for k in range(4):
-            o, i = B("xg", 512 * k, 512 * k + 512), IND(B("w"), B("lu", 32 * k, 32 * k + 32))
-            if k % 2 == 0:
-                cp(o, i)
-            else:
-                act(o, i)
+        for k in (1, 0, 2, 3):
+            lo, hi = SITES[k], SITES[k + 1]
+            (cp if k == 1 else act)(B("xg", 16 * lo, 16 * hi), IND(B("w"), B("lu", lo, hi)))
         for b in range(2):
-            mm(P(b), (T.tie[0:1, :], [("tie", 0, 128)]),
-               (T.trow[0:1, 512 * b:512 * b + 512], [("trow", 0, 1024)]), True, False)
+            mm(P(b), (T.tie[0:1, :], [("tie", 0, 128)]), whole("trow", T.trow[0:1, 32 * b:32 * b + 32, :]), True, False)
+        for k in range(4):
+            lo, hi = SITES[k], SITES[k + 1]
+            running(B("xs", 16 * lo, 16 * hi), B("mask", 0, 16 * (hi - lo)), B("xg", 16 * lo, 16 * hi))
         for h in range(2):
             if rho == 0:
                 act(B("vh", 512 * h, 512 * h + 512), B("v0", 512 * h, 512 * h + 512), 0.5, 1472.25)
             else:
                 mm(P(6 - h), B("pm16", 128 * rho - 128, 128 * rho), B("vo", 512 * h, 512 * h + 512), True, True)
-                act(B("vh", 512 * h, 512 * h + 512), P(6 - h), 0.5, 768.25)
-        sums(0)
         if rho == 0:
             ts(B("pti", 0, 64), B("pri"), 4, Op.arith_shift_right)
             ts(B("pti", 64, 128), B("pri"), 15, Op.bitwise_and)
-        repeat("idn", "ch", 0)
-        maxima("m1", 0, (0,))
-        sums(1)
+            ts(B("lf"), B("sli"), C(SG), Op.mult, C(SOFF), Op.add)
+        else:
+            act(B("vh", 0, 512), P(6), 0.5, 768.25)
+        repeat("id16", S(0, 64), 0)
         totals(0, False)
-        maxima("m1", 0, (1, 2, 3))
-        mm(P(0), B("ch"), B("ny"), False, True)
+        mm(P(0), S(0, 128), whole("ny", T.ny[:]), False, True)
         signs(0)
-        repeat("idn", "ch", 1)
-        mm(P(1), B("ch"), B("ny"), False, False)
+        mm(P(1), S(0, 128), whole("ny", T.ny[:]), False, False)
         totals(1, True)
         signs(1)
-        maxima("m1", 1)
-        keys("kp", "m1", 0, (0, 1))
-        counts(0)
-        keys("kp", "m1", 0, (2, 3))
-        counts(1)
-        ts(B("pos", 0, 8), P(7, 64, 72), 63.5, Op.add)
-        act(B("posb"), P(7, 64, 72))
-        keys("kp", "m1", 1, (0, 1))
-        mm(P(7, 72, 80), B("swp"), B("posb"), True, True)
-        keys("kp", "m1", 1, (2, 3))
-        p1, p2 = B("pp", 0, 128), B("pp", 128, 256)
-        cp(IND(B("lp"), B("pos", 0, 8)), B("lf"))
-        cp(IND(B("cp"), B("pos", 0, 8)), B("ch"))
-        ts(B("pos", 8, 16), P(7, 72, 80), 63.5, Op.add)
-        act(p1, B("lp"))
-        tt(p2, B("lp"), p1, Op.subtract)
-        act(B("cq"), IND(B("cp"), B("pos", 8, 16)))
-        mm(P(7, 0, 128), B("dbig"), B("ones"), True, False)
-        mm(P(7, 0, 128), B("dq"), B("ones"), False, False)
-        for b in range(2):
-            mm(P(b, 0, 128), B("cd", 512 * b, 512 * b + 128), p1, True, False)
-        for b in range(2):
-            for u in range(4):
-                s = 4 * b + u
-                if u:
-                    mm(P(b, 128 * u, 128 * u + 128), B("cd", 128 * s, 128 * s + 128), p1, True, False)
-                mm(P(b, 128 * u, 128 * u + 128), B("cd", 128 * s, 128 * s + 128), p2, False, True)
-                if s == 1:
-                    repeat("swp", "cq", 0)
-                    repeat("swp", "cq", 1)
-                    maxima("m2", 0)
-                    maxima("m2", 1)
-            act(B("gl", 512 * b, 512 * b + 512), P(b), 1.0, 0.0, Fn.Sign)
-        keys("kn", "m2", 0, (0, 1, 2))
-        for s in range(4):
-            mm(P(7, 0, 128), B("ca", 128 * s, 128 * s + 128), B("gl", 128 * s, 128 * s + 128), False, False)
-        keys("kn", "m2", 0, (3,))
-        act(B("ks", 0, 64), P(6, 256, 320), 1.0, C(SQ))
-        keys("kn", "m2", 1, (0,))
-        for s in range(4, 8):
-            mm(P(7, 0, 128), B("ca", 128 * s, 128 * s + 128), B("gl", 128 * s, 128 * s + 128), False, s == 7)
-        keys("kn", "m2", 1, (1, 2, 3))
-        act(B("ks", 64, 128), P(4, 256, 320), 1.0, C(SQ))
-        for a in range(8):
-            mm(P(3, 0, 128), B("cs", 112 - 16 * a, 240 - 16 * a), (T.gs[:, a:64:8, :], [("gs", 0, 64)]), a == 0, a == 7)
-        mm(P(6, 0, 128), B("d1"), B("ones"), True, False)
-        mm(P(6, 0, 128), B("d2"), B("ones"), False, False)
-        ts(B("rr"), P(7, 0, 128), ROUND, Op.add, -ROUND, Op.add)
-        cp(IND(B("kq"), B("pos", 0, 4)), B("ks", 0, 64))
-        tt(P(5, 0, 128), P(7, 0, 128), B("rr"), Op.subtract)
-        cp(IND(B("kq"), B("pos", 4, 8)), B("ks", 64, 128))
-        act(B("posf"), P(3, 0, 128), 1.0, 63.5)
-        act(P(4, 0, 128), p1, C(SQH), -0.5)
-        act(P(4, 128, 256), p2, C(SQL), 1.0 + 63.5 / 128)
-        za = P(7, 256, 384)
-        tt(B("kh"), B("kq"), P(5, 0, 128), Op.min)
-        tt(P(5, 128, 256), B("kq"), P(5, 0, 128), Op.min)
-        tt(B("kl"), P(5, 128, 256), B("kh"), Op.subtract)
-        act(B("com"), P(5, 0, 128), -1.0 / 1024, C(QC))
+        repeat("id16", S(64, 128), 1)
+        maxima("m1", 0)
         if rho == 0:
             cp(B("prf", 0, 128), B("pti"))
+        maxima("m1", 1, (0, 1, 2))
+        counts(0)
+        keys("kp", "m1", 0, (0, 1))
+        counts(1)
+        ts(B("pos", 0, 8), P(7, 64, 72), 63.5, Op.add)
+        maxima("m1", 1, (3,))
+        act(B("posb"), P(7, 64, 72))
+        if rho:
+            act(B("vh", 512, 1024), P(5), 0.5, 768.25)
+        keys("kp", "m1", 0, (2, 3))
+        keys("kp", "m1", 1, (0,))
+        mm(P(7, 72, 80), B("swp"), B("posb"), True, True)
+        keys("kp", "m1", 1, (1, 2, 3))
+        odd = P(5, 256, 384)
+        mm(odd, B("dbig"), B("ones"), True, False)
+        mm(odd, B("dq"), B("ones"), False, False)
+        cp(IND(B("lp"), B("pos", 0, 8)), B("lf"))
+        cp(IND(B("cp"), B("pos", 0, 8)), S(0, 128))
+        ts(B("pos", 8, 16), P(7, 72, 80), 63.5, Op.add)
+        for h in range(2):
+            act(half("pp", h, 128 * h, 128 * h + 128), half("lp", h, 0, 128))
+        for h in range(2):
+            tt(half("pp", 1 - h, 128 * h, 128 * h + 128), half("lp", h, 0, 128), half("pp", h, 128 * h, 128 * h + 128),
+               Op.subtract)
+        act(B("cq"), IND(B("cp"), B("pos", 8, 16)))
         cp(B("tu"), B("prf", 128 * rho, 128 * rho + 64))
+        act(B("jb"), B("prf", 128 * rho + 64, 128 * rho + 128), 8.0)
+        repeat("sw16", B("cq", 0, 64), 0)
+        for b in range(2):
+            pairs("cd", "pp", b)
+            act(B("gl", 512 * b, 512 * b + 512), P(b), 1.0, 0.0, Fn.Sign)
+        maxima("m2", 0)
+        keys("kn", "m2", 0, (0,))
+        repeat("sw16", B("cq", 64, 128), 1)
+        maxima("m2", 1)
+        keys("kn", "m2", 0, (1,))
+        tally(odd, "ca", "gl", 0, False, False)
+        keys("kn", "m2", 0, (2, 3))
+        act(B("ks", 0, 64), P(6, 256, 320), 1.0, C(SQ))
+        keys("kn", "m2", 1, (0,))
+        tally(odd, "ca", "gl", 1, False, True)
+        keys("kn", "m2", 1, (1, 2, 3))
+        act(B("ks", 64, 128), P(4, 256, 320), 1.0, C(SQ))
+        for d in ("d1", "d2", "d3"):
+            mm(P(6, 0, 128), B(d), B("ones"), d == "d1", False)
+        ts(B("rr"), odd, ROUND, Op.add, -ROUND, Op.add)
+        cp(IND(B("kq"), B("pos", 0, 4)), B("ks", 0, 64))
+        tt(P(5, 0, 128), odd, B("rr"), Op.subtract)
+        cp(IND(B("kq"), B("pos", 4, 8)), B("ks", 64, 128))
+        act(B("com"), P(5, 0, 128), -1.0 / 1024, C(QC))
+        for h in range(2):
+            act(half(4, h, 0, 128), half("pp", h, 128 * h, 128 * h + 128), half("cf", h, SQH, SQH + 1), -0.5)
+            act(half(4, h, 128, 256), half("pp", 1 - h, 128 * h, 128 * h + 128), half("cf", 1 - h, SQL, SQL + 1),
+                1.0 + 63.5 / 128)
+        mm(P(7, 128, 256), B("we1"), B("com"), True, False)
+        mm(P(7, 128, 256), B("we2"), B("com"), False, True)
+        act(B("ew"), P(7, 128, 256), EXPC, 0.0, Fn.Exp)
+        if rho == 0:
+            act(B("pm32"), B("pm16"))
+        za = P(7, 256, 384)
+        tt(P(5, 128, 256), B("kq"), P(5, 0, 128), Op.min)
+        for h in range(2):
+            tt(half("kk", h, 128 * h, 128 * h + 128), half("kq", h, 0, 128), half(5, h, 0, 128), Op.min)
+        for h in range(2):
+            tt(half("kk", 1 - h, 128 * h, 128 * h + 128), half(5, h, 128, 256), half("kk", h, 128 * h, 128 * h + 128),
+               Op.subtract)
+        for u in range(2):
+            tt(P(4, 256 + 128 * u, 384 + 128 * u), B("ew"), P(4, 128 * u, 128 * u + 128), Op.mult)
         for b in range(4):
-            mm(P(b, 0, 128), B("rd", 512 * b, 512 * b + 128), B("kh"), True, False)
-        for b in range(4):
-            for u in range(4):
-                s = 4 * b + u
-                if u:
-                    mm(P(b, 128 * u, 128 * u + 128), B("rd", 128 * s, 128 * s + 128), B("kh"), True, False)
-                mm(P(b, 128 * u, 128 * u + 128), B("rd", 128 * s, 128 * s + 128), B("kl"), False, True)
+            pairs("rd", "kk", b)
             if b % 2 == 0:
                 act(B("gk", 512 * b, 512 * b + 512), P(b), 1.0, 0.0, Fn.Sign)
             else:
                 ts(B("gk", 512 * b, 512 * b + 512), P(b), -1.0, Op.max, 1.0, Op.min)
-            if b == 0:
-                mm(P(5, 256, 384), B("we"), B("com"), True, True)
-                act(B("ew"), P(5, 256, 384), EXPC, 0.0, Fn.Exp)
-            if b == 1:
-                for u in range(2):
-                    tt(P(4, 256 + 128 * u, 384 + 128 * u), B("ew"), P(4, 128 * u, 128 * u + 128), Op.mult)
-        act(B("jb"), B("prf", 128 * rho + 64, 128 * rho + 128), 8.0)
-        for s in range(16):
-            mm(za, B("ra", 128 * s, 128 * s + 128), B("gk", 128 * s, 128 * s + 128), s == 0, s == 15)
+        for b in range(4):
+            tally(za, "ra", "gk", b, b == 0, b == 3)
+        for a in range(8):
+            mm(P(2, 0, 128), B("cs", 112 - 16 * a, 240 - 16 * a), G("gs", a, 64, 8), a == 0, a == 7)
         act(B("pwb"), za, EXPC, -117.5 * LN2, Fn.Exp)
         act(B("pwa"), za, EXPC, -5.5 * LN2, Fn.Exp)
         act(P(5, 384, 512), za, 2.0 ** 99, 0.0, Fn.Relu)
+        act(B("posf"), P(2, 0, 128), 1.0, 63.5)
         act(B("prow"), IND(B("posf"), B("tu")))
-        if not last:
-            mm(P(0, 0, 128), B("pm32", 128 * rho, 128 * rho + 128), B("prf", 128 * rho, 128 * rho + 128), True, True)
-            act(B("prf", 128 * rho + 128, 128 * rho + 256), P(0, 0, 128))
         for u in range(2):
             tt(B("z", 128 * u, 128 * u + 128), B("pwb"), P(4, 128 * u, 128 * u + 128), Op.mult)
         tt(B("pwc"), B("pwa"), P(5, 384, 512), Op.max)
-        for w in range(2):
+        for w in range(8):
             clamp(w, 0)
-        for u in range(2):
-            tt(B("z", 256 + 128 * u, 384 + 128 * u), B("pwc"), P(4, 256 + 128 * u, 384 + 128 * u), Op.mult)
-        for w in range(2, 8):
-            clamp(w, 0)
+            if w in (3, 5):
+                u = w // 5
+                tt(B("z", 256 + 128 * u, 384 + 128 * u), B("pwc"), P(4, 256 + 128 * u, 384 + 128 * u), Op.mult)
         for w in range(8):
             clamp(w, 1, w == 7)
         cp(B("t128"), P(6, 0, 128))
@@ -558,14 +557,20 @@ def rank_program(g, core, T, topo):
         for j in range(8, 16):
             mm(P(1, 0, 64), B("kp", 15 - j, 143 - j), B("prow", j, 1024, 16), False, j == 15)
         ts(B("lu2"), P(7, 0, 128), C(KAP), Op.add)
+        if not last:
+            mm(P(0, 0, 128), B("pm32", 128 * rho, 128 * rho + 128), B("prf", 128 * rho, 128 * rho + 128), True, True)
         act(B("lpos"), P(7, 0, 128), 1.0, C(KAP))
         ts(B("g1", 0, 1056), IND(B("w"), B("lu2", 0, 66)), 0.5, Op.mult)
-        act(B("g1", 1056, 2048), IND(B("w"), B("lu2", 66, 128)), 0.5)
         ts(B("pru"), P(1, 0, 64), 0.125, Op.mult)
+        act(B("g1", 1056, 2048), IND(B("w"), B("lu2", 66, 128)), 0.5)
         act(B("lf2"), IND(B("lpos"), B("pos", 0, 8)))
         if not last:
+            act(B("prf", 128 * rho + 128, 128 * rho + 256), P(0, 0, 128))
             mm(P(7, 128, 256), B("pm32", 128 * rho, 128 * rho + 128), B("lf2"), True, True)
             act(B("lf"), P(7, 128, 256), C(SG), C(SOFF))
+        else:
+            dma("sync", D("ys"), B("lf2"))
+            dma("sync", D("yll", rank), (T.lf2[own, :], [("lf2", 0, 128)]))
         cuts = CUTS if last else VCUTS
         for lo, hi in zip(cuts[:-1], cuts[1:]):
             tt(B("vo", lo, hi), IND(B("g1"), B("pru", lo // 16, hi // 16)), B("vh", lo, hi), Op.add)
@@ -573,12 +578,8 @@ def rank_program(g, core, T, topo):
                 ts(B("vb", lo, hi), B("vo", lo, hi), -1408.0, Op.add)
         if not last:
             ts(B("lu"), B("lf"), C(SG), Op.mult, -24512.5, Op.add)
-            table("vo", arr[rho], 1536.0, VCUTS, 3)
+            table("vo", arr[rho], 1536.0, VCUTS, FIRST)
 
-    slot2 = arr[2].index(rank)
-    own = slice(16 * slot2, 16 * slot2 + 16)
-    dma("act", D("ys"), B("lf2"))
-    dma("act", D("yll", rank), (T.lf2[own, :], [("lf2", 0, 128)]))
     for h in range(2):
         lo, hi = CUTS[h], CUTS[h + 1]
         dma("sync", D("vs%d" % h), B("vb", lo, hi))
@@ -592,3 +593,6 @@ def rank_program(g, core, T, topo):
         arrival("y%d" % h, "vl%d" % h, rank)
         dma("g", (T.yx[:, CUTS[h]:CUTS[h + 1]], []), D("vl%d" % h))
     emit(g, T, ops)
+
+
+FIRST = 8

@@ -5,9 +5,10 @@ from concourse.mybir import AluOpType as Op, ActivationFunctionType as Fn
 BF, F32, F16, I32, U16 = "bfloat16", "float32", "float16", "int32", "uint16"
 N = 8
 DS = (4, 1, 7)
-CUTS = (0, 576, 1024)
+CUTS = (0, 512, 1024)
 VCUTS = (0, 128, 512, 1024)
 SITES = (0, 40, 92, 112, 128)
+XC = 384
 LN2 = math.log(2.0)
 INNER = {0: 16, 1: 16}
 EXPC = 7 * LN2 / 128
@@ -23,7 +24,7 @@ def dr(n, d):
 
 
 SCRATCH = {
-    "xs0": dr(64, BF), "xl0": dr(64, BF), "xs1": dr(64, BF), "xl1": dr(64, BF),
+    "xs0": dr(XC // 8, BF), "xl0": dr(XC // 8, BF), "xs1": dr(128 - XC // 8, BF), "xl1": dr(128 - XC // 8, BF),
     "ss": dr(16, I32), "sll": dr(16, I32), "prs": dr(8, I32), "prl": dr(8, I32),
     "ys": dr(16, F32), "yll": dr(16, F32),
     "vs0": dr(CUTS[1] // 8, BF), "vl0": dr(CUTS[1] // 8, BF),
@@ -37,8 +38,8 @@ SCRATCH = {
     "idn": sb(128, BF), "nid": sb(128, BF), "dsg": sb(128, BF), "id16": sb(128, BF),
     "dbig": sb(128, BF), "dq": sb(128, BF),
     "we1": sb(128, BF), "we2": sb(128, BF), "swp": sb(128, BF), "sw16": sb(128, BF),
-    "d1": sb(128, BF), "d2": sb(128, BF), "d3": sb(128, BF), "ut": sb(128, BF), "up": sb(128, BF),
-    "ptb": sb(8, BF), "pt": sb(8, F32), "ow": sb(8 * 152, BF), "yy": sb(1024, BF),
+    "d1": sb(128, BF), "d2": sb(128, BF), "d3": sb(128, BF), "ut": sb(512, BF),
+    "ptb": sb(8, BF), "pt": sb(8, F32), "ow": sb(8 * 72, BF), "yy": sb(1024, BF),
     "kp": sb(144, BF), "kn": sb(144, BF), "id64": sb(64, BF), "qs": sb(128, BF), "q1": sb(64, BF), "q2": sb(96, BF),
     "rd": sb(1024, BF), "ra": ("sbuf", [128, 17, 64], BF), "cd": sb(512, BF), "ca": ("sbuf", [128, 9, 64], BF),
     "pm32": sb(256, F32), "pm16": sb(256, BF),
@@ -53,10 +54,10 @@ SCRATCH = {
     "rr": sb(128, F32), "com": sb(128, BF),
     "ks": sb(128, F32), "kq": sb(128, F32), "kk": sb(256, F16),
     "ew": sb(128, BF), "pwa": sb(128, BF), "pwb": sb(128, BF), "pwc": sb(128, BF),
-    "z": sb(512, BF), "oh": sb(4096, BF), "t128": sb(128, F16), "tlow": sb(128, BF),
+    "z": sb(512, BF), "oh": sb(4096, BF), "t128": sb(256, F16), "tlow": sb(256, BF),
 }
 TAGS = ["x0", "x1", "sl", "pr", "yl", "y0", "y1"]
-SEMAPHORES = ["e_pe", "e_dve", "e_act", "e_g"] + ["d%d" % k for k in range(32)] + \
+SEMAPHORES = ["e_pe", "e_dve", "e_act", "e_g"] + ["d%d" % k for k in range(72)] + \
     ["a" + t for t in TAGS] + ["l" + t for t in TAGS]
 
 
@@ -241,11 +242,11 @@ def rank_program(g, core, T, topo):
     rows = slice(16 * rank, 16 * rank + 16)
     slot0, slot2 = arr[0].index(rank), arr[2].index(rank)
     own = slice(16 * slot2, 16 * slot2 + 16)
-    dma("sync", D("xs0"), (T.x[:, 0:512], []))
-    dma("act", D("xs1"), (T.x[:, 512:1024], []))
+    dma("sync", D("xs0"), (T.x[:, 0:XC], []))
+    dma("sync", D("xs1"), (T.x[:, XC:1024], []))
     dma("sync", D("ss"), (T.sl[:], []))
-    dma("act", D("xl0", slot0), (T.x[rows, 0:512], []))
-    dma("sync", D("xl1", slot0), (T.x[rows, 512:1024], []))
+    dma("sync", D("xl0", slot0), (T.x[rows, 0:XC], []))
+    dma("sync", D("xl1", slot0), (T.x[rows, XC:1024], []))
     dma("sync", D("prs"), (T.prey[:], []))
     dma("sync", D("sll", slot0), (T.sl[rows, :], []))
     dma("sync", D("prl", slot0), (T.prey[rows, :], []))
@@ -260,20 +261,29 @@ def rank_program(g, core, T, topo):
     arrival("x1", "xl1", slot0)
     arrival("sl", "sll", slot0)
     arrival("pr", "prl", slot0)
-    dma("sync", B("v0", 0, 512), D("xl0"))
-    dma("sync", B("v0", 512, 1024), D("xl1"))
+    dma("sync", B("v0", 0, XC), D("xl0"))
+    dma("sync", B("v0", XC, 1024), D("xl1"))
     dma("sync", B("sli"), D("sll"))
+    direct = [[(slot0 + 1 + DIRECT * h + k) % N for k in range(DIRECT)] for h in range(2)]
+
+    def spread(queue, h):
+        for gm in direct[h]:
+            lo, hi = 1024 * arr[0][gm] + XC * h, 1024 * arr[0][gm] + (1024 if h else XC)
+            for k in range(8):
+                dma(queue, (T.w[16 * k:16 * k + 16, lo:hi], [("w%d" % k, lo, hi)]), D("xl%d" % h, gm))
+
+    spread("sync", 1)
 
     ms(B("ones"), 1.0)
     ms(B("mask"), 1.0)
-    for k, m in enumerate((16, 31, 112, 96, 7, 8, 1, 63, 64)):
+    for k, m in enumerate((16, 31, 112, 96, 15, 1, 63, 64)):
         ts(B("ci", k + 1, k + 2), B("ci", 0, 1), m, Op.bitwise_and)
     ms(B("mask", 0, 1024, 16), 0.0)
-    cp(B("cf", 0, 10), B("ci", 0, 10))
+    cp(B("cf", 0, 9), B("ci", 0, 9))
     ms(B("tie"), -1.0 / 2048)
     ms(B("half"), 0.5)
-    (PP, B16, E, G16, G32, W7, H8, O1, P63, B64, SG, SQ, SW, U15, U32, KAP, TIE, A2, A32, S64P, ONCE,
-     SQH, SQL, SOFF, NN, K1, K2, CU, CU1, WT, WP, Q4, QC) = range(33)
+    (PP, B16, E, G16, G32, P15, O1, P63, B64, SG, SQ, SW, U15, U32, KAP, TIE, A2, A32, S64P, ONCE,
+     SQH, SQL, SOFF, NN, K1, K2, CU, CU1, Q4, QC) = range(30)
     ts(B("idn"), B("rowx", 0, 128), C(PP), Op.is_equal)
     ts(C(S64P), C(B16), -8.0, Op.mult, 64.0, Op.add)
     ts(C(SG), C(B16), -0.125, Op.mult, 1.0, Op.add)
@@ -291,14 +301,14 @@ def rank_program(g, core, T, topo):
     ms(G("ca", 0, 9), 0.0)
     cp(piece("vv", T.vv[:, :, 0:16]), B("idn"))
     ts(C(U15), C(G16), 15.0, Op.add)
-    ts(C(U32), C(G32), 32.0, Op.add)
+    ts(C(U32), C(G32), 0.5, Op.mult, 16.0, Op.add)
     ts(C(KAP), C(O1), -173311.5, Op.mult, 8191.5, Op.add)
     ts(C(ONCE), C(B64), -1.0 / 128, Op.mult, 1.0, Op.add)
     for dst, src in ((T.q2[:, 0:64:2], T.q1[:, 1:64:2]), (T.q2[:, 64:96:2], T.q1[:, 1:32:2]),
                      (T.q2[:, 1:60:2], T.q1[:, 4:64:2]), (T.q2[:, 61:96:2], T.q1[:, 0:36:2])):
         cp(piece("q2", dst), whole("q1", src))
-    columns = [(TIE, PP, -1.0 / 2048, 0.0), (A2, B16, 0.125, -2.0), (A32, B16, -2.0, 32.0), (NN, W7, 2.0, C(B16)),
-               (CU, W7, 2.0, C(G16)), (WT, H8, -127.0 / 8, 128.0), (WP, H8, -127.0 * 16, 16384.0),
+    columns = [(TIE, PP, -1.0 / 2048, 0.0), (A2, B16, 0.125, -2.0), (A32, B16, -2.0, 32.0), (NN, P15, 2.0, 0.0),
+               (CU, PP, 2.0, 0.0),
                (SQH, SG, 1.0 / 16384, 0.0), (SQL, SG, 1.0 / 128, 0.0), (SOFF, SG, 24512.5, 0.0), (SW, SG, 16.0, C(PP)),
                (K1, NN, 256.0, -6400.0), (K2, NN, -1.0, -129.0), (CU1, CU, 1.0, 1.0)]
     for k, (dst, src, times, plus) in enumerate(columns):
@@ -326,10 +336,10 @@ def rank_program(g, core, T, topo):
     cp(B("pt"), B("ptb"))
     for q in range(4):
         ts(B("we1", 32 * q, 32 * q + 32), B("ones", 0, 32), B("ind", 8 + q, 9 + q), Op.mult, C(A2), Op.mult)
-    ts(B("ut"), B("rowx", 0, 128), C(CU1), Op.is_equal, C(WT), Op.mult)
-    ts(B("up"), B("rowx", 0, 128), C(CU), Op.is_equal, C(WP), Op.mult)
+    for k, (at, times) in enumerate(((CU1, 128.0), (CU1, 1.0), (CU, 16384.0), (CU, 128.0))):
+        ts(B("ut", 128 * k, 128 * k + 128), B("rowx", 0, 128), C(at), Op.is_equal, times, Op.mult)
     for w in range(8):
-        ts(B("ow", 152 * w, 152 * w + 152), B("rowx", 8 - w, 160 - w), C(U32), Op.is_equal, B("pt", w, w + 1), Op.mult)
+        ts(B("ow", 72 * w, 72 * w + 72), B("rowx", 8 - w, 80 - w), C(U32), Op.is_equal, B("pt", w, w + 1), Op.mult)
     for k in range(2):
         for gm in range(8):
             gn = arr[k + 1].index(arr[k][gm])
@@ -351,11 +361,11 @@ def rank_program(g, core, T, topo):
     act(G("ra", 15, 16), P(5, 448, 512), C(ONCE))
     act(G("ca", 1, 9, 2), P(6, 0, 256), 1024.0, 0.0, Fn.Abs)
 
-    def table(src, ar, off, cuts, first, done=None):
+    def table(src, ar, off, cuts, first, done=((), (), ())):
         k = 0
-        for lo, hi in zip(cuts[:-1], cuts[1:]):
-            for gm in (gm for gm in range(8) if gm != done):
-                bank = P(k % 8, 0, hi - lo)
+        for lo, hi, skip in zip(cuts[:-1], cuts[1:], done):
+            for gm in (gm for gm in range(8) if gm not in skip):
+                bank = P(k % 8 if k < 23 else 0, 0, hi - lo)
                 mm(bank, whole("vv", T.vv[:, gm, :]), B(src, lo, hi), True, True)
                 o = B("w", 1024 * ar[gm] + lo, 1024 * ar[gm] + hi)
                 if k < first or k % 2 == 1:
@@ -368,20 +378,19 @@ def rank_program(g, core, T, topo):
         return B("xs", 16 * lo + 15, 16 * hi, 16)
 
     def repeat(mat, src, h):
-        for u in range(4):
-            mm((T["p%d" % (2 + h)][:, u:256:4], P(2 + h, 0, 256)[1]), B(mat), src, True, True)
+        for u in range(2):
+            mm((T["p%d" % (2 + h)][:, u:128:2], P(2 + h, 0, 128)[1]), B(mat), src, True, True)
 
     def maxima(name, h, ks=range(4)):
-        for k in ks:
-            lo = 1024 * h + 256 * k
-            tt(B(name, lo, lo + 256), B("xg", 1024 * h + k, 1024 * h + 1024, 4), P(2 + h, 0, 256), Op.max)
+        for j in (2 * k + i for k in ks for i in range(2)):
+            lo = 1024 * h + 128 * j
+            tt(B(name, lo, lo + 128), B("xg", 1024 * h + j, 1024 * h + 1024, 8), P(2 + h, 0, 128), Op.max)
 
     def keys(mat, name, h, ks=range(4)):
-        for k in ks:
-            for u in range(4):
-                j, lo = k + 4 * u, 1024 * h + 256 * k
-                mm(P(6 - 2 * h, 256, 320), B(mat, 15 - j, 143 - j), B(name, lo + u, lo + 256, 4),
-                   j == 0 and name == "m1", j == 15 and name == "m2")
+        for j in (2 * k + i + 8 * u for k in ks for i in range(2) for u in range(2)):
+            lo = 1024 * h + 128 * (j % 8)
+            mm(P(6 - 2 * h, 256, 320), B(mat, 15 - j, 143 - j), B(name, lo + j // 8, lo + 128, 2),
+               j == 0 and name == "m1", j == 15 and name == "m2")
 
     def totals(b, stop):
         for a in range(8):
@@ -409,28 +418,88 @@ def rank_program(g, core, T, topo):
             mm(out, G(mat, 2 * s + 1 - h, 2 * s + 3 - h), B(src, 256 * s + 128 * h, 256 * s + 128 * h + 128),
                start and k == 0, stop and k == 3)
 
-    def clamp(w, side, last=False):
-        lo = 512 * w + 256 * side
-        ts(B("oh", lo, lo + 256), B("z", 256 * side, 256 * side + 256),
-           2.0 ** (14 * w - 114), Op.max, 2.0 ** (14 * w - 106), Op.min)
-        for u in range(2):
-            at = 152 * w + 8 + 16 * side - 8 * u
-            mm(P(6, 0, 128), B("ow", at, at + 128), B("oh", lo + 128 * u, lo + 128 * u + 128), False, last and u == 1)
+    def window(h):
+        return half(6 - 3 * h, 0, 0, 128)
+
+    def upper(p):
+        for h in range(2):
+            lo = 128 * p + 64 * h
+            tt(half("kk", h, lo, lo + 64), half("kq", h, 64 * p, 64 * p + 64), half(5, h, 64 * p, 64 * p + 64), Op.min)
+
+    def lower(p):
+        for h in range(2):
+            lo = 128 * p + 64 * h
+            tt(half("kk", 1 - h, lo, lo + 64), half(5, h, 128 + 64 * p, 192 + 64 * p), half("kk", h, lo, lo + 64), Op.subtract)
+
+    def differences(b):
+        for u in range(4):
+            s = 4 * (b % 2) + u
+            mm(P(b, 128 * u, 128 * u + 128), B("rd", 128 * s, 128 * s + 128), B("kk", 128 * (b // 2), 128 * (b // 2) + 128),
+               True, True)
+
+    def order(b):
+        if b % 2 == 0:
+            act(B("gk", 512 * b, 512 * b + 512), P(b), 1.0, 0.0, Fn.Sign)
+        else:
+            ts(B("gk", 512 * b, 512 * b + 512), P(b), -1.0, Op.max, 1.0, Op.min)
+
+    ZA = (P(7, 256, 320), P(0, 0, 64))
+
+    def ranks(b):
+        for k in range(8):
+            s, h, lo = 4 * (b % 2) + k // 2, k % 2, 512 * b + 64 * k
+            mm(ZA[b // 2], G("ra", 2 * s + 1 - h, 2 * s + 3 - h), B("gk", lo, lo + 64), b % 2 == 0 and k == 0,
+               b % 2 == 1 and k == 7)
+
+    def powers(h):
+        za, lo, hi = ZA[h], 64 * h, 64 * h + 64
+        act(B("pwb", lo, hi), za, EXPC, -117.5 * LN2, Fn.Exp)
+        act(B("pwa", lo, hi), za, EXPC, -5.5 * LN2, Fn.Exp)
+        act(P(5, 384 + lo, 384 + hi), za, 2.0 ** 99, 0.0, Fn.Relu)
+
+    def scaled(h, side):
+        for u in (2 * side, 2 * side + 1):
+            tt(B("z", 256 * h + 64 * u, 256 * h + 64 * u + 64), B("pwc" if side else "pwb", 64 * h, 64 * h + 64),
+               P(4, 128 * u + 64 * h, 128 * u + 64 * h + 64), Op.mult)
+        if side == 0:
+            tt(B("pwc", 64 * h, 64 * h + 64), B("pwa", 64 * h, 64 * h + 64), P(5, 384 + 64 * h, 448 + 64 * h), Op.max)
+
+    def clamp(h, ws, first=0, final=1, stop=False):
+        for w in ws:
+            lo = 2048 * h + 256 * w
+            ts(B("oh", lo + 128 * first, lo + 128 * final + 128), B("z", 256 * h + 128 * first, 256 * h + 128 * final + 128),
+               2.0 ** (14 * w - 114), Op.max, 2.0 ** (14 * w - 106), Op.min)
+            for side in range(first, final + 1):
+                mm(window(h), B("ow", 72 * w + 8 * side, 72 * w + 8 * side + 64),
+                   B("oh", lo + 128 * side, lo + 128 * side + 128), False, stop and w == ws[-1] and side == final)
+
+    def digits(h):
+        lo = 128 * h
+        tt(half("tlow", 0, lo, lo + 128), window(h), half("t128", 0, lo, lo + 128), Op.subtract)
+        for k, name in enumerate(("t128", "t128", "tlow", "tlow")):
+            at = lo + 64 * (k % 2)
+            mm(P(7, 64 * h, 64 * h + 64), half("ut", 0, 128 * k, 128 * k + 128), half(name, 0, at, at + 64), k == 0, k == 3)
 
     for h in range(2):
         mm(P(4 + h), whole("vv", T.vv[0:16, 0, :]), (T.xo[0:16, 512 * h:512 * h + 512], [("xo", 0, 1024)]), True, True)
-        act(B("w", 1024 * rank + 512 * h, 1024 * rank + 512 * h + 512), P(4 + h), 1.0, -128.0)
-    table("v0", arr[0], 128.0, (0, 512, 1024), 0, slot0)
+        act(B("w", 1024 * rank + 512 * h, 1024 * rank + 512 * h + 512), P(4 + h))
+    spread("act", 0)
+    table("v0", arr[0], 0.0, (0, XC, XC // 2 + 512, 1024), 0, [[slot0] + direct[0]] + 2 * [[slot0] + direct[1]])
     cp(B("lu"), B("sli"))
+    W = (T.w[:], [("w", 0, 8192)] + [("w%d" % k, 0, 8192) for k in range(8)])
     for rho in range(3):
         last = rho == 2
+        less = -128.0 if rho == 0 else 0.0
         for k in (1, 0, 2, 3):
             lo, hi = SITES[k], SITES[k + 1]
-            (cp if k == 1 else act)(B("xg", 16 * lo, 16 * hi), IND(B("w"), B("lu", lo, hi)))
+            o, i = B("xg", 16 * lo, 16 * hi), IND(W, B("lu", lo, hi))
+            if k == 1:
+                ts(o, i, less, Op.add)
+            else:
+                act(o, i, 1.0, less)
         for b in range(2):
             mm(P(b), (T.tie[0:1, :], [("tie", 0, 128)]), whole("trow", T.trow[0:1, 32 * b:32 * b + 32, :]), True, False)
-        for k in range(4):
-            lo, hi = SITES[k], SITES[k + 1]
+        for lo, hi in ((0, SITES[1]), (SITES[1], 64), (64, SITES[3]), (SITES[3], 128)):
             running(B("xs", 16 * lo, 16 * hi), B("mask", 0, 16 * (hi - lo)), B("xg", 16 * lo, 16 * hi))
         for h in range(2):
             if rho == 0:
@@ -442,6 +511,7 @@ def rank_program(g, core, T, topo):
             ts(B("pti", 64, 128), B("pri"), 15, Op.bitwise_and)
             ts(B("lf"), B("sli"), C(SG), Op.mult, C(SOFF), Op.add)
         else:
+            act(B("lf"), P(7, 128, 256), C(SG), C(SOFF))
             act(B("vh", 0, 512), P(6), 0.5, 768.25)
         repeat("id16", S(0, 64), 0)
         totals(0, False)
@@ -461,7 +531,9 @@ def rank_program(g, core, T, topo):
         ts(B("pos", 0, 8), P(7, 64, 72), 63.5, Op.add)
         maxima("m1", 1, (3,))
         act(B("posb"), P(7, 64, 72))
-        if rho:
+        if rho == 0:
+            act(B("pm32"), B("pm16"))
+        else:
             act(B("vh", 512, 1024), P(5), 0.5, 768.25)
         keys("kp", "m1", 0, (2, 3))
         keys("kp", "m1", 1, (0,))
@@ -470,115 +542,117 @@ def rank_program(g, core, T, topo):
         odd = P(5, 256, 384)
         mm(odd, B("dbig"), B("ones"), True, False)
         mm(odd, B("dq"), B("ones"), False, False)
-        cp(IND(B("lp"), B("pos", 0, 8)), B("lf"))
         cp(IND(B("cp"), B("pos", 0, 8)), S(0, 128))
         ts(B("pos", 8, 16), P(7, 72, 80), 63.5, Op.add)
-        for h in range(2):
-            act(half("pp", h, 128 * h, 128 * h + 128), half("lp", h, 0, 128))
-        for h in range(2):
-            tt(half("pp", 1 - h, 128 * h, 128 * h + 128), half("lp", h, 0, 128), half("pp", h, 128 * h, 128 * h + 128),
-               Op.subtract)
+        cp(IND(B("lp"), B("pos", 0, 8)), B("lf"))
         act(B("cq"), IND(B("cp"), B("pos", 8, 16)))
         cp(B("tu"), B("prf", 128 * rho, 128 * rho + 64))
+        ts(P(7, 128, 256), B("lp"), ROUND / 1024, Op.add, -ROUND / 1024, Op.add)
+        for h in range(2):
+            act(half("pp", h, 128 * h, 128 * h + 128), half("lp", h, 0, 128))
         act(B("jb"), B("prf", 128 * rho + 64, 128 * rho + 128), 8.0)
         repeat("sw16", B("cq", 0, 64), 0)
+        repeat("sw16", B("cq", 64, 128), 1)
+        maxima("m2", 0, (0,))
+        for h in range(2):
+            tt(half("pp", 1 - h, 128 * h, 128 * h + 128), half("lp", h, 0, 128), half(7, h, 128, 256), Op.subtract)
+        maxima("m2", 0, (1, 2, 3))
+        maxima("m2", 1)
+        keys("kn", "m2", 0, (0,))
         for b in range(2):
             pairs("cd", "pp", b)
             act(B("gl", 512 * b, 512 * b + 512), P(b), 1.0, 0.0, Fn.Sign)
-        maxima("m2", 0)
-        keys("kn", "m2", 0, (0,))
-        repeat("sw16", B("cq", 64, 128), 1)
-        maxima("m2", 1)
-        keys("kn", "m2", 0, (1,))
-        tally(odd, "ca", "gl", 0, False, False)
-        keys("kn", "m2", 0, (2, 3))
+        keys("kn", "m2", 0, (1, 2, 3))
         act(B("ks", 0, 64), P(6, 256, 320), 1.0, C(SQ))
-        keys("kn", "m2", 1, (0,))
+        keys("kn", "m2", 1, (0, 1))
+        tally(odd, "ca", "gl", 0, False, False)
+        keys("kn", "m2", 1, (2, 3))
         tally(odd, "ca", "gl", 1, False, True)
-        keys("kn", "m2", 1, (1, 2, 3))
         act(B("ks", 64, 128), P(4, 256, 320), 1.0, C(SQ))
-        for d in ("d1", "d2", "d3"):
-            mm(P(6, 0, 128), B(d), B("ones"), d == "d1", False)
-        ts(B("rr"), odd, ROUND, Op.add, -ROUND, Op.add)
         cp(IND(B("kq"), B("pos", 0, 4)), B("ks", 0, 64))
-        tt(P(5, 0, 128), odd, B("rr"), Op.subtract)
+        ts(B("rr"), odd, ROUND, Op.add, -ROUND, Op.add)
         cp(IND(B("kq"), B("pos", 4, 8)), B("ks", 64, 128))
-        act(B("com"), P(5, 0, 128), -1.0 / 1024, C(QC))
+        tt(P(5, 0, 128), odd, B("rr"), Op.subtract)
+        for a in range(8):
+            mm(P(2, 256, 384), B("cs", 112 - 16 * a, 240 - 16 * a), G("gs", a, 64, 8), a == 0, a == 7)
+        act(B("posf"), P(2, 256, 384), 1.0, 63.5)
         for h in range(2):
             act(half(4, h, 0, 128), half("pp", h, 128 * h, 128 * h + 128), half("cf", h, SQH, SQH + 1), -0.5)
             act(half(4, h, 128, 256), half("pp", 1 - h, 128 * h, 128 * h + 128), half("cf", 1 - h, SQL, SQL + 1),
                 1.0 + 63.5 / 128)
-        mm(P(7, 128, 256), B("we1"), B("com"), True, False)
-        mm(P(7, 128, 256), B("we2"), B("com"), False, True)
-        act(B("ew"), P(7, 128, 256), EXPC, 0.0, Fn.Exp)
-        if rho == 0:
-            act(B("pm32"), B("pm16"))
-        za = P(7, 256, 384)
-        tt(P(5, 128, 256), B("kq"), P(5, 0, 128), Op.min)
-        for h in range(2):
-            tt(half("kk", h, 128 * h, 128 * h + 128), half("kq", h, 0, 128), half(5, h, 0, 128), Op.min)
-        for h in range(2):
-            tt(half("kk", 1 - h, 128 * h, 128 * h + 128), half(5, h, 128, 256), half("kk", h, 128 * h, 128 * h + 128),
-               Op.subtract)
+        tt(P(5, 128, 192), B("kq", 0, 64), P(5, 0, 64), Op.min)
+        upper(0)
+        tt(P(5, 192, 256), B("kq", 64, 128), P(5, 64, 128), Op.min)
+        lower(0)
+        upper(1)
+        ts(B("com"), P(5, 0, 128), -1.0 / 1024, Op.mult, C(QC), Op.add)
+        differences(0)
+        differences(1)
+        lower(1)
+        order(0)
+        order(1)
+        differences(2)
+        differences(3)
+        mm(P(6, 128, 256), B("we1"), B("com"), True, False)
+        mm(P(6, 128, 256), B("we2"), B("com"), False, True)
+        order(2)
+        act(B("ew"), P(6, 128, 256), EXPC, 0.0, Fn.Exp)
+        order(3)
+        ranks(0)
+        ranks(1)
         for u in range(2):
             tt(P(4, 256 + 128 * u, 384 + 128 * u), B("ew"), P(4, 128 * u, 128 * u + 128), Op.mult)
-        for b in range(4):
-            pairs("rd", "kk", b)
-            if b % 2 == 0:
-                act(B("gk", 512 * b, 512 * b + 512), P(b), 1.0, 0.0, Fn.Sign)
-            else:
-                ts(B("gk", 512 * b, 512 * b + 512), P(b), -1.0, Op.max, 1.0, Op.min)
-        for b in range(4):
-            tally(za, "ra", "gk", b, b == 0, b == 3)
-        for a in range(8):
-            mm(P(2, 0, 128), B("cs", 112 - 16 * a, 240 - 16 * a), G("gs", a, 64, 8), a == 0, a == 7)
-        act(B("pwb"), za, EXPC, -117.5 * LN2, Fn.Exp)
-        act(B("pwa"), za, EXPC, -5.5 * LN2, Fn.Exp)
-        act(P(5, 384, 512), za, 2.0 ** 99, 0.0, Fn.Relu)
-        act(B("posf"), P(2, 0, 128), 1.0, 63.5)
-        act(B("prow"), IND(B("posf"), B("tu")))
-        for u in range(2):
-            tt(B("z", 128 * u, 128 * u + 128), B("pwb"), P(4, 128 * u, 128 * u + 128), Op.mult)
-        tt(B("pwc"), B("pwa"), P(5, 384, 512), Op.max)
-        for w in range(8):
-            clamp(w, 0)
-            if w in (3, 5):
-                u = w // 5
-                tt(B("z", 256 + 128 * u, 384 + 128 * u), B("pwc"), P(4, 256 + 128 * u, 384 + 128 * u), Op.mult)
-        for w in range(8):
-            clamp(w, 1, w == 7)
-        cp(B("t128"), P(6, 0, 128))
-        tt(B("tlow"), P(6, 0, 128), B("t128"), Op.subtract)
+        powers(0)
+        ranks(2)
+        ranks(3)
+        scaled(0, 0)
+        powers(1)
+        for h in range(2):
+            for d in ("d1", "d2", "d3"):
+                mm(window(h), half(d, 0, 0, 64), half("ones", 0, 0, 128), d == "d1", False)
+        act(B("prow", 0, PROW), IND(B("posf"), B("tu", 0, PROW // 16)))
+        clamp(0, range(2), 0, 0)
+        scaled(0, 1)
+        clamp(0, range(2, 4), 0, 0)
+        clamp(0, range(4, 8))
+        scaled(1, 0)
+        clamp(0, range(4), 1, 1, True)
+        scaled(1, 1)
+        act(half("t128", 0, 0, 128), window(0))
+        act(B("prow", PROW, 1024), IND(B("posf"), B("tu", PROW // 16, 64)))
+        clamp(1, range(LATE), 0, 0)
+        clamp(1, range(LATE, 8))
+        digits(0)
+        clamp(1, range(LATE), 1, 1, True)
         mm(P(1, 0, 64), B("idn"), B("jb"), True, False)
-        for j in range(8):
-            mm(P(1, 0, 64), B("kp", 15 - j, 143 - j), B("prow", j, 1024, 16), False, False)
-        mm(P(7, 0, 128), B("ut"), B("t128"), True, False)
-        mm(P(7, 0, 128), B("up"), B("tlow"), False, True)
-        for j in range(8, 16):
+        for j in range(16):
             mm(P(1, 0, 64), B("kp", 15 - j, 143 - j), B("prow", j, 1024, 16), False, j == 15)
-        ts(B("lu2"), P(7, 0, 128), C(KAP), Op.add)
-        if not last:
-            mm(P(0, 0, 128), B("pm32", 128 * rho, 128 * rho + 128), B("prf", 128 * rho, 128 * rho + 128), True, True)
-        act(B("lpos"), P(7, 0, 128), 1.0, C(KAP))
-        ts(B("g1", 0, 1056), IND(B("w"), B("lu2", 0, 66)), 0.5, Op.mult)
+        ts(B("lu2", 0, 64), P(7, 0, 64), C(KAP), Op.add)
+        act(B("g1", 0, 1024), IND(W, B("lu2", 0, 64)), 0.5, less / 2)
+        cp(half("t128", 0, 128, 256), window(1))
+        digits(1)
         ts(B("pru"), P(1, 0, 64), 0.125, Op.mult)
-        act(B("g1", 1056, 2048), IND(B("w"), B("lu2", 66, 128)), 0.5)
-        act(B("lf2"), IND(B("lpos"), B("pos", 0, 8)))
+        ts(B("lu2", 64, 128), P(7, 64, 128), C(KAP), Op.add)
+        ts(B("g1", 1024, 16 * GCUT), IND(W, B("lu2", 64, GCUT)), 0.5, Op.mult, less / 2, Op.add)
+        act(B("g1", 16 * GCUT, 2048), IND(W, B("lu2", GCUT, 128)), 0.5, less / 2)
+        act(B("lpos"), P(7, 0, 128), 1.0, C(KAP))
         if not last:
-            act(B("prf", 128 * rho + 128, 128 * rho + 256), P(0, 0, 128))
-            mm(P(7, 128, 256), B("pm32", 128 * rho, 128 * rho + 128), B("lf2"), True, True)
-            act(B("lf"), P(7, 128, 256), C(SG), C(SOFF))
-        else:
+            mm(P(2, 0, 128), B("pm32", 128 * rho, 128 * rho + 128), B("prf", 128 * rho, 128 * rho + 128), True, True)
+            act(B("prf", 128 * rho + 128, 128 * rho + 256), P(2, 0, 128))
+        act(B("lf2"), IND(B("lpos"), B("pos", 0, 8)))
+        if last:
             dma("sync", D("ys"), B("lf2"))
             dma("sync", D("yll", rank), (T.lf2[own, :], [("lf2", 0, 128)]))
-        cuts = CUTS if last else VCUTS
-        for lo, hi in zip(cuts[:-1], cuts[1:]):
+        cuts = (0, CUTS[1], CUTS[1] + 128, 1024) if last else VCUTS
+        for k in range(3):
+            lo, hi = cuts[k], cuts[k + 1]
             tt(B("vo", lo, hi), IND(B("g1"), B("pru", lo // 16, hi // 16)), B("vh", lo, hi), Op.add)
-            if last:
-                ts(B("vb", lo, hi), B("vo", lo, hi), -1408.0, Op.add)
+            if last and k:
+                ts(B("vb", CUTS[k - 1], CUTS[k]), B("vo", CUTS[k - 1], CUTS[k]), -1408.0, Op.add)
         if not last:
-            ts(B("lu"), B("lf"), C(SG), Op.mult, -24512.5, Op.add)
             table("vo", arr[rho], 1536.0, VCUTS, FIRST)
+            mm(P(7, 128, 256), B("pm32", 128 * rho, 128 * rho + 128), B("lf2"), True, True)
+            cp(B("lu"), P(7, 128, 256))
 
     for h in range(2):
         lo, hi = CUTS[h], CUTS[h + 1]
@@ -596,3 +670,7 @@ def rank_program(g, core, T, topo):
 
 
 FIRST = 8
+GCUT = 100
+LATE = 6
+PROW = 768
+DIRECT = 1

import math
from concourse.bass import DstId, RemoteDMATransfer
from concourse.mybir import AluOpType as Op, ActivationFunctionType as Fn

BF, F32, F16, I32, U16 = "bfloat16", "float32", "float16", "int32", "uint16"
N = 8
DS = (4, 1, 7)
CUTS = (0, 512, 1024)
VCUTS = (0, 128, 512, 1024)
SITES = (0, 40, 92, 112, 128)
XC = 384
LN2 = math.log(2.0)
INNER = {0: 16, 1: 16}
EXPC = 7 * LN2 / 128
ROUND = 1.5 * 2.0 ** 40


def sb(n, d):
    return ("sbuf", [128, n], d)


def dr(n, d):
    return ("dram", [8, 128, n], d)


SCRATCH = {
    "xs0": dr(XC // 8, BF), "xl0": dr(XC // 8, BF), "xs1": dr(128 - XC // 8, BF), "xl1": dr(128 - XC // 8, BF),
    "ss": dr(16, I32), "sll": dr(16, I32), "prs": dr(8, I32), "prl": dr(8, I32),
    "ys": dr(16, F32), "yll": dr(16, F32),
    "vs0": dr(CUTS[1] // 8, BF), "vl0": dr(CUTS[1] // 8, BF),
    "vs1": dr(128 - CUTS[1] // 8, BF), "vl1": dr(128 - CUTS[1] // 8, BF), "vb": sb(1024, BF),
    "p0": ("psum", [128, 32, 16], F32), "p1": ("psum", [128, 32, 16], F32),
    "p2": ("psum", [128, 512], F32), "p3": ("psum", [128, 512], F32), "p4": ("psum", [128, 512], F32),
    "p5": ("psum", [128, 512], F32), "p6": ("psum", [128, 512], F32), "p7": ("psum", [128, 512], F32),
    "ci": sb(12, I32), "cf": sb(40, F32), "ind": sb(12, F32), "rowx": sb(160, BF),
    "ones": sb(128, BF), "tie": sb(128, BF), "cs": sb(240, BF), "half": sb(8, BF), "mask": sb(1024, BF),
    "trow": ("sbuf", [128, 64, 16], BF), "ny": ("sbuf", [128, 32, 16], BF), "vv": ("sbuf", [128, 8, 128], BF),
    "idn": sb(128, BF), "nid": sb(128, BF), "dsg": sb(128, BF), "id16": sb(128, BF),
    "dbig": sb(128, BF), "dq": sb(128, BF),
    "we1": sb(128, BF), "we2": sb(128, BF), "swp": sb(128, BF), "sw16": sb(128, BF),
    "d1": sb(128, BF), "d2": sb(128, BF), "d3": sb(128, BF), "ut": sb(512, BF),
    "ptb": sb(8, BF), "pt": sb(8, F32), "ow": sb(8 * 72, BF), "yy": sb(1024, BF),
    "kp": sb(144, BF), "kn": sb(144, BF), "id64": sb(64, BF), "qs": sb(128, BF), "q1": sb(64, BF), "q2": sb(96, BF),
    "rd": sb(1024, BF), "ra": ("sbuf", [128, 17, 64], BF), "cd": sb(512, BF), "ca": ("sbuf", [128, 9, 64], BF),
    "pm32": sb(256, F32), "pm16": sb(256, BF),
    "xo": sb(1024, BF), "v0": sb(1024, BF), "vo": sb(1024, F16), "vh": sb(1024, F32),
    "w": sb(8192, BF), "xg": sb(2048, BF), "xs": sb(2048, F16), "g1": sb(2048, BF),
    "sli": sb(128, I32), "pri": sb(64, I32), "prf": sb(384, F32), "pru": sb(64, U16),
    "pti": sb(128, I32), "tu": sb(64, U16), "jb": sb(64, BF), "posf": sb(128, BF), "prow": sb(1024, BF),
    "lu": sb(128, U16), "lf": sb(128, F32), "lu2": sb(128, U16), "lf2": sb(128, F32), "lpos": sb(128, F32),
    "lp": sb(128, F32), "pp": sb(256, BF), "cp": sb(128, F32), "cq": sb(128, F16),
    "gs": ("sbuf", [128, 64, 16], BF), "pos": sb(16, U16), "posb": sb(8, BF),
    "m1": sb(2048, F16), "m2": sb(2048, F16), "gl": sb(1024, BF), "gk": sb(2048, BF),
    "rr": sb(128, F32), "com": sb(128, BF),
    "ks": sb(128, F32), "kq": sb(128, F32), "kk": sb(256, F16),
    "ew": sb(128, BF), "pwa": sb(128, BF), "pwb": sb(128, BF), "pwc": sb(128, BF),
    "z": sb(512, BF), "oh": sb(4096, BF), "t128": sb(256, F16), "tlow": sb(256, BF),
}
TAGS = ["x0", "x1", "sl", "pr", "yl", "y0", "y1"]
SEMAPHORES = ["e_pe", "e_dve", "e_act", "e_g"] + ["d%d" % k for k in range(72)] + \
    ["a" + t for t in TAGS] + ["l" + t for t in TAGS]


def arrangement(d):
    out = []
    for a in range(N):
        if a < (a ^ d):
            out += [a, a ^ d]
    return out


def emit(g, T, ops):
    queue = {"pe": g.tensor, "dve": g.vector, "act": g.scalar, "g": g, "sync": g.sync}
    seen, clock, nseq, hist = {}, {q: {} for q in queue}, {}, []
    waits, marked = [], set()
    for k, (q, src, fn, rd, wr) in enumerate(ops):
        need = {}
        for acc, isw in ((rd, False), (wr, True)):
            for name, lo, hi in acc:
                ps = name == "ps"
                blo, bhi = (lo // 512 * 512, (hi + 511) // 512 * 512) if ps else (lo, hi)
                for lo2, hi2, k2, w2 in seen.get(name, ()):
                    s2 = ops[k2][1]
                    if s2 == "pe" and src == "pe":
                        continue
                    if ps and s2 != src:
                        hit = lo2 < bhi and hi2 > blo
                    else:
                        hit = lo2 < hi and hi2 > lo and (isw or w2)
                    if hit and hist[k2][0] > need.get(s2, (0, 0))[0]:
                        need[s2] = (hist[k2][0], k2)
        mine = []
        if q is not None:
            ck = clock[q]
            for s2, (n2, k2) in sorted(need.items(), key=lambda it: -it[1][1]):
                if ck.get(s2, 0) < n2:
                    mine.append(k2)
                    marked.add(k2)
                    for s3, n3 in hist[k2][1].items():
                        if ck.get(s3, 0) < n3:
                            ck[s3] = n3
            snap = dict(ck)
        else:
            snap = {}
        nseq[src] = nseq.get(src, 0) + 1
        snap[src] = nseq[src]
        hist.append((nseq[src], snap))
        waits.append(mine)
        for acc, isw in ((rd, False), (wr, True)):
            for name, lo, hi in acc:
                lst = seen.setdefault(name, [])
                lst[:] = [e for e in lst if not (lo <= e[0] and e[1] <= hi and (
                    (isw and name != "ps") or (ops[e[2]][1] == src and src in queue and (isw or not e[3]))))]
                lst.append((lo, hi, k, isw))
    count, at, waited = {}, {}, {}
    for k, (q, src, fn, rd, wr) in enumerate(ops):
        for k2 in waits[k]:
            queue[q].wait_ge(T.sem[at[k2][0]], at[k2][1])
            waited[at[k2][0]] = max(waited.get(at[k2][0], 0), at[k2][1])
        if src in queue:
            ins = fn(queue[q])
            if k in marked:
                count["e_" + src] = count.get("e_" + src, 0) + 1
                ins.then_inc(T.sem["e_" + src], 1)
                at[k] = ("e_" + src, count["e_" + src])
        elif src[0] == "d":
            fn(queue[q]).then_inc(T.sem[src], 16)
            count[src] = 16
            at[k] = (src, 16)
        else:
            if fn is not None:
                fn(queue[q])
            count[src] = N - 1
            at[k] = (src, N - 1)
    for s in sorted(count):
        if waited.get(s, 0) < count[s]:
            g.wait_ge(T.sem[s], count[s])


def rank_program(g, core, T, topo):
    rank = T.rank_of(core)
    if rank is None:
        return
    ops, nd, fresh = [], [0], [0]
    arr = [arrangement(d) for d in DS]

    def B(name, lo=0, hi=None, step=1):
        if hi is None:
            hi = T[name].shape[1]
        return (T[name][:, lo:hi:step] if step > 1 else T[name][:, lo:hi], [(name, lo, hi)])

    def G(name, lo, hi, step=1):
        return (T[name][:, lo:hi:step, :], [(name, lo, hi)])

    def piece(name, ap):
        fresh[0] += 1
        return (ap, [(name, 4096 + fresh[0], 4097 + fresh[0])])

    def whole(name, ap):
        return (ap, [(name, 0, 8192)])

    def P(bank, lo=0, hi=512):
        t, n = T["p%d" % bank], INNER.get(bank)
        return (t[:, lo // n:hi // n, :] if n else t[:, lo:hi], [("ps", bank * 512 + lo, bank * 512 + hi)])

    def C(k):
        return B("cf", k, k + 1)

    def IND(win, off):
        return (win[0].indirect(off[0]), win[1] + off[1])

    def D(name, slot=None):
        if slot is None:
            return (T[name][:], [(name, 0, N)])
        return (T[name][slot], [(name, slot, slot + 1)])

    def sides(*xs):
        r = []
        for x in xs:
            if isinstance(x, tuple):
                r += x[1]
        return r

    def val(x):
        return x[0] if isinstance(x, tuple) else x

    def mm(out, lhsT, rhs, start, stop):
        ops.append(("pe", "pe", lambda e: e.matmul(out[0], lhsT[0], rhs[0], start, stop), lhsT[1] + rhs[1], out[1]))

    def cp(out, in_):
        ops.append(("dve", "dve", lambda e: e.tensor_copy(out[0], in_[0]), in_[1] + out[1][1:], out[1][:1]))

    def tt(out, a, b, op):
        ops.append(("dve", "dve", lambda e: e.tensor_tensor(out[0], a[0], b[0], op), a[1] + b[1], out[1]))

    def ts(out, a, s1, o0, s2=None, o1=None):
        if o1 is None:
            f = lambda e: e.tensor_scalar(out[0], a[0], val(s1), None, o0)
        else:
            f = lambda e: e.tensor_scalar(out[0], a[0], val(s1), val(s2), o0, o1)
        ops.append(("dve", "dve", f, sides(a, s1, s2), out[1]))

    def running(out, keep, a):
        ops.append(("dve", "dve", lambda e: e.tensor_tensor_scan(out[0], keep[0], a[0], 0.0, Op.mult, Op.add),
                    keep[1] + a[1], out[1]))

    def ms(out, c):
        ops.append(("dve", "dve", lambda e: e.memset(out[0], c), [], out[1]))

    def act(out, a, scale=1.0, bias=0.0, fn=Fn.Identity):
        ops.append(("act", "act", lambda e: e.activation(out[0], a[0], fn, bias=val(bias), scale=val(scale)),
                    sides(a, scale, bias), out[1]))

    def iota(out, pat, cm, small=True):
        if small:
            f = lambda e: e.iota(out[0], pat, 0, cm, allow_small_or_imprecise_dtypes=True)
        else:
            f = lambda e: e.iota(out[0], pat, 0, cm)
        ops.append(("g", "g", f, [], out[1]))

    def diagonal(out, in_, first):
        ops.append(("g", "g", lambda e: e.affine_select(out[0], in_[0], [[-1, 16]], Op.is_equal, 0.0, -first, 1),
                    in_[1], out[1]))

    def dma(q, out, in_):
        ops.append((q, "d%d" % nd[0], lambda e: e.dma_start(out[0], in_[0]), in_[1], out[1]))
        nd[0] += 1

    def exchange(tag, src, src_slot, dst, dst_slot):
        trs = []
        for k in range(1, N):
            r = rank ^ k
            rid, pid = topo.addr(T.cores[r], core)
            trs.append(RemoteDMATransfer(dst_ids=[DstId(rid=rid, pnc=pid)],
                                         dma_engine_mask=1 << topo.engines(core, T.cores[r])[k - 1],
                                         remote_sem=T.sem["a" + tag], src=T[src][src_slot(r)], dst=T[dst][dst_slot]))
        ops.append(("g", "l" + tag, lambda e: e.remote_dma_fused(trs, local_sem=T.sem["l" + tag]), [(src, 0, N)], []))

    def arrival(tag, dst, own):
        ops.append((None, "a" + tag, None, [], [(dst, k, k + 1) for k in range(N) if k != own]))

    rows = slice(16 * rank, 16 * rank + 16)
    slot0, slot2 = arr[0].index(rank), arr[2].index(rank)
    own = slice(16 * slot2, 16 * slot2 + 16)
    dma("sync", D("xs0"), (T.x[:, 0:XC], []))
    dma("sync", D("xs1"), (T.x[:, XC:1024], []))
    dma("sync", D("ss"), (T.sl[:], []))
    dma("sync", D("xl0", slot0), (T.x[rows, 0:XC], []))
    dma("sync", D("xl1", slot0), (T.x[rows, XC:1024], []))
    dma("sync", D("prs"), (T.prey[:], []))
    dma("sync", D("sll", slot0), (T.sl[rows, :], []))
    dma("sync", D("prl", slot0), (T.prey[rows, :], []))
    dma("sync", (T.xo[0:16, :], [("xo", 0, 1024)]), (T.x[rows, :], []))
    iota(B("ci", 0, 1), [[0, 1]], 1, False)
    iota(B("rowx"), [[1, 160]], 0)
    exchange("x0", "xs0", lambda r: r, "xl0", slot0)
    exchange("x1", "xs1", lambda r: r, "xl1", slot0)
    exchange("sl", "ss", lambda r: r, "sll", slot0)
    exchange("pr", "prs", lambda r: r, "prl", slot0)
    arrival("x0", "xl0", slot0)
    arrival("x1", "xl1", slot0)
    arrival("sl", "sll", slot0)
    arrival("pr", "prl", slot0)
    dma("sync", B("v0", 0, XC), D("xl0"))
    dma("sync", B("v0", XC, 1024), D("xl1"))
    dma("sync", B("sli"), D("sll"))
    direct = [[(slot0 + 1 + DIRECT * h + k) % N for k in range(DIRECT)] for h in range(2)]

    def spread(queue, h):
        for gm in direct[h]:
            lo, hi = 1024 * arr[0][gm] + XC * h, 1024 * arr[0][gm] + (1024 if h else XC)
            for k in range(8):
                dma(queue, (T.w[16 * k:16 * k + 16, lo:hi], [("w%d" % k, lo, hi)]), D("xl%d" % h, gm))

    spread("sync", 1)

    ms(B("ones"), 1.0)
    ms(B("mask"), 1.0)
    for k, m in enumerate((16, 31, 112, 96, 15, 1, 63, 64)):
        ts(B("ci", k + 1, k + 2), B("ci", 0, 1), m, Op.bitwise_and)
    ms(B("mask", 0, 1024, 16), 0.0)
    cp(B("cf", 0, 9), B("ci", 0, 9))
    ms(B("tie"), -1.0 / 2048)
    ms(B("half"), 0.5)
    (PP, B16, E, G16, G32, P15, O1, P63, B64, SG, SQ, SW, U15, U32, KAP, TIE, A2, A32, S64P, ONCE,
     SQH, SQL, SOFF, NN, K1, K2, CU, CU1, Q4, QC) = range(30)
    ts(B("idn"), B("rowx", 0, 128), C(PP), Op.is_equal)
    ts(C(S64P), C(B16), -8.0, Op.mult, 64.0, Op.add)
    ts(C(SG), C(B16), -0.125, Op.mult, 1.0, Op.add)
    ts(B("ind", 0, 8), B("rowx", 0, 128, 16), C(G16), Op.is_equal)
    ts(B("ind", 8, 12), B("rowx", 0, 128, 32), C(G32), Op.is_equal)
    ts(B("id64"), B("rowx", 0, 64), C(P63), Op.is_equal, C(S64P), Op.mult)
    act(B("nid"), B("idn"), -1.0)
    act(B("dsg"), B("idn"), C(SG))
    act(B("ptb"), B("rowx", 0, 8), -14 * LN2, 114 * LN2, Fn.Exp)
    ms(G("ra", 0, 17), 0.0)
    for k in range(4):
        cp(piece("qs", T.qs[:, 64 * (k // 2) + k % 2:64 * (k // 2) + 64:2]), B("id64", 32 * (k % 2), 32 * (k % 2) + 32))
    for k in range(4):
        cp(piece("q1", T.q1[:, k:64:4]), B("id64", 16 * k, 16 * k + 16))
    ms(G("ca", 0, 9), 0.0)
    cp(piece("vv", T.vv[:, :, 0:16]), B("idn"))
    ts(C(U15), C(G16), 15.0, Op.add)
    ts(C(U32), C(G32), 0.5, Op.mult, 16.0, Op.add)
    ts(C(KAP), C(O1), -173311.5, Op.mult, 8191.5, Op.add)
    ts(C(ONCE), C(B64), -1.0 / 128, Op.mult, 1.0, Op.add)
    for dst, src in ((T.q2[:, 0:64:2], T.q1[:, 1:64:2]), (T.q2[:, 64:96:2], T.q1[:, 1:32:2]),
                     (T.q2[:, 1:60:2], T.q1[:, 4:64:2]), (T.q2[:, 61:96:2], T.q1[:, 0:36:2])):
        cp(piece("q2", dst), whole("q1", src))
    columns = [(TIE, PP, -1.0 / 2048, 0.0), (A2, B16, 0.125, -2.0), (A32, B16, -2.0, 32.0), (NN, P15, 2.0, 0.0),
               (CU, PP, 2.0, 0.0),
               (SQH, SG, 1.0 / 16384, 0.0), (SQL, SG, 1.0 / 128, 0.0), (SOFF, SG, 24512.5, 0.0), (SW, SG, 16.0, C(PP)),
               (K1, NN, 256.0, -6400.0), (K2, NN, -1.0, -129.0), (CU1, CU, 1.0, 1.0)]
    for k, (dst, src, times, plus) in enumerate(columns):
        if k % 4 == 0 and k < 12:
            n = 16 << k // 4
            cp(piece("vv", T.vv[:, :, n:2 * n]), whole("vv", T.vv[:, :, 0:n]))
        ts(C(dst), C(src), times, Op.mult, plus, Op.add)
    ts(C(SQ), C(E), C(SG), Op.mult, 1.0 / 64, Op.mult)
    ms(B("cs", 0, 112), 0.0)
    ms(B("cs", 112, 128), 0.5)
    ms(B("cs", 128, 240), 0.0)
    ts(C(Q4), C(SQ), 256.0, Op.mult)
    ts(C(QC), C(SQ), 0.25, Op.mult, 32.0, Op.add)
    for a in range(8):
        ts(B("yy", 128 * a, 128 * a + 128), B("ones"), B("ind", a, a + 1), Op.mult, 1.0 / 16, Op.mult)
        ts(piece("ny", T.ny[:, a:32:8, :]), B("ones", 0, 64), B("ind", a, a + 1), Op.mult, -1.0 / 16, Op.mult)
        cp(piece("trow", T.trow[0:1, a:64:8, :]), (T.rowx[0:1, 0:128], [("rowx", 0, 128)]))
    ts(B("swp"), B("rowx", 0, 128), C(SW), Op.is_equal)
    ts(B("sw16"), B("rowx", 0, 128), C(SW), Op.is_equal, 1.0 / 16, Op.mult)
    ts(B("kp"), B("rowx", 0, 144), C(U15), Op.is_equal, 8.0, Op.mult)
    ts(B("kn"), B("rowx", 0, 144), C(U15), Op.is_equal, -8.0, Op.mult)
    for name, times in (("id16", 1.0 / 16), ("dbig", 32768.0), ("dq", C(Q4)), ("we2", C(A32)),
                        ("d1", C(K1)), ("d2", C(K2)), ("d3", -127.0 / 256)):
        ts(B(name), B("idn"), times, Op.mult)
    cp(B("pt"), B("ptb"))
    for q in range(4):
        ts(B("we1", 32 * q, 32 * q + 32), B("ones", 0, 32), B("ind", 8 + q, 9 + q), Op.mult, C(A2), Op.mult)
    for k, (at, times) in enumerate(((CU1, 128.0), (CU1, 1.0), (CU, 16384.0), (CU, 128.0))):
        ts(B("ut", 128 * k, 128 * k + 128), B("rowx", 0, 128), C(at), Op.is_equal, times, Op.mult)
    for w in range(8):
        ts(B("ow", 72 * w, 72 * w + 72), B("rowx", 8 - w, 80 - w), C(U32), Op.is_equal, B("pt", w, w + 1), Op.mult)
    for k in range(2):
        for gm in range(8):
            gn = arr[k + 1].index(arr[k][gm])
            diagonal(B("pm16", 128 * k + 16 * gn, 128 * k + 16 * gn + 16), B("ones", 0, 16), 16 * gm)
        if k == 0:
            dma("g", B("pri"), D("prl"))
    for b in range(3):
        for u in range(8):
            o, s = P(2 + b, 64 * u, 64 * u + 64), 8 * b + u + 1
            mm(o, B("idn"), whole("qs", T.qs[:, 0:64]) if b < 2 else whole("q1", T.q1[:, 0:64]), True, False)
            mm(o, B("nid"), whole("qs", T.qs[:, 2 * s:2 * s + 64]) if b < 2 else whole("q2", T.q2[:, 4 * u:4 * u + 64]),
               False, True)
        act(B("rd", 512 * b, 512 * b + 512) if b < 2 else B("cd"), P(2 + b))
    for b in range(12):
        name, k = ("rd", b) if b < 8 else ("cd", b - 8)
        mm(P(5 + b // 8, 64 * k, 64 * k + 64), (T[name][0:64, 128 * k:128 * k + 128], [(name, 128 * k, 128 * k + 128)]),
           (T.dsg[0:64, 0:64], [("dsg", 0, 64)]), True, True)
    act(G("ra", 1, 15, 2), P(5, 0, 448))
    act(G("ra", 15, 16), P(5, 448, 512), C(ONCE))
    act(G("ca", 1, 9, 2), P(6, 0, 256), 1024.0, 0.0, Fn.Abs)

    def table(src, ar, off, cuts, first, done=((), (), ())):
        k = 0
        for lo, hi, skip in zip(cuts[:-1], cuts[1:], done):
            for gm in (gm for gm in range(8) if gm not in skip):
                bank = P(k % 8 if k < 23 else 0, 0, hi - lo)
                mm(bank, whole("vv", T.vv[:, gm, :]), B(src, lo, hi), True, True)
                o = B("w", 1024 * ar[gm] + lo, 1024 * ar[gm] + hi)
                if k < first or k % 2 == 1:
                    act(o, bank, 1.0, -off)
                else:
                    ts(o, bank, -off, Op.add)
                k += 1

    def S(lo, hi):
        return B("xs", 16 * lo + 15, 16 * hi, 16)

    def repeat(mat, src, h):
        for u in range(2):
            mm((T["p%d" % (2 + h)][:, u:128:2], P(2 + h, 0, 128)[1]), B(mat), src, True, True)

    def maxima(name, h, ks=range(4)):
        for j in (2 * k + i for k in ks for i in range(2)):
            lo = 1024 * h + 128 * j
            tt(B(name, lo, lo + 128), B("xg", 1024 * h + j, 1024 * h + 1024, 8), P(2 + h, 0, 128), Op.max)

    def keys(mat, name, h, ks=range(4)):
        for j in (2 * k + i + 8 * u for k in ks for i in range(2) for u in range(2)):
            lo = 1024 * h + 128 * (j % 8)
            mm(P(6 - 2 * h, 256, 320), B(mat, 15 - j, 143 - j), B(name, lo + j // 8, lo + 128, 2),
               j == 0 and name == "m1", j == 15 and name == "m2")

    def totals(b, stop):
        for a in range(8):
            mm((T["p%d" % b][:, a:32:8, :], P(b)[1]), B("yy", 128 * a, 128 * a + 128), S(64 * b, 64 * b + 64),
               False, stop and a == 7)

    def signs(b):
        act(G("gs", 32 * b, 32 * b + 32), P(b), -1.0, C(TIE), Fn.Sign)

    def counts(b):
        for n in range(4 * b, 4 * b + 4):
            mm(P(7, 64 + n, 65 + n), G("gs", 8 * n, 8 * n + 8), B("half", 0, 1), True, True)

    def half(x, h, lo, hi):
        name = x if isinstance(x, str) else "p%d" % x
        return (T[name][64 * h:64 * h + 64, lo:hi], (B(x, lo, hi) if name == x else P(x, lo, hi))[1])

    def pairs(mat, src, bank):
        for s in (2 * bank, 2 * bank + 1):
            mm(P(bank, 256 * (s % 2), 256 * (s % 2) + 256), B(mat, 128 * s, 128 * s + 128), B(src), True, True)

    def tally(out, mat, src, bank, start, stop):
        for k in range(4):
            s, h = 2 * bank + k // 2, k % 2
            mm(out, G(mat, 2 * s + 1 - h, 2 * s + 3 - h), B(src, 256 * s + 128 * h, 256 * s + 128 * h + 128),
               start and k == 0, stop and k == 3)

    def window(h):
        return half(6 - 3 * h, 0, 0, 128)

    def upper(p):
        for h in range(2):
            lo = 128 * p + 64 * h
            tt(half("kk", h, lo, lo + 64), half("kq", h, 64 * p, 64 * p + 64), half(5, h, 64 * p, 64 * p + 64), Op.min)

    def lower(p):
        for h in range(2):
            lo = 128 * p + 64 * h
            tt(half("kk", 1 - h, lo, lo + 64), half(5, h, 128 + 64 * p, 192 + 64 * p), half("kk", h, lo, lo + 64), Op.subtract)

    def differences(b):
        for u in range(4):
            s = 4 * (b % 2) + u
            mm(P(b, 128 * u, 128 * u + 128), B("rd", 128 * s, 128 * s + 128), B("kk", 128 * (b // 2), 128 * (b // 2) + 128),
               True, True)

    def order(b):
        if b % 2 == 0:
            act(B("gk", 512 * b, 512 * b + 512), P(b), 1.0, 0.0, Fn.Sign)
        else:
            ts(B("gk", 512 * b, 512 * b + 512), P(b), -1.0, Op.max, 1.0, Op.min)

    ZA = (P(7, 256, 320), P(0, 0, 64))

    def ranks(b):
        for k in range(8):
            s, h, lo = 4 * (b % 2) + k // 2, k % 2, 512 * b + 64 * k
            mm(ZA[b // 2], G("ra", 2 * s + 1 - h, 2 * s + 3 - h), B("gk", lo, lo + 64), b % 2 == 0 and k == 0,
               b % 2 == 1 and k == 7)

    def powers(h):
        za, lo, hi = ZA[h], 64 * h, 64 * h + 64
        act(B("pwb", lo, hi), za, EXPC, -117.5 * LN2, Fn.Exp)
        act(B("pwa", lo, hi), za, EXPC, -5.5 * LN2, Fn.Exp)
        act(P(5, 384 + lo, 384 + hi), za, 2.0 ** 99, 0.0, Fn.Relu)

    def scaled(h, side):
        for u in (2 * side, 2 * side + 1):
            tt(B("z", 256 * h + 64 * u, 256 * h + 64 * u + 64), B("pwc" if side else "pwb", 64 * h, 64 * h + 64),
               P(4, 128 * u + 64 * h, 128 * u + 64 * h + 64), Op.mult)
        if side == 0:
            tt(B("pwc", 64 * h, 64 * h + 64), B("pwa", 64 * h, 64 * h + 64), P(5, 384 + 64 * h, 448 + 64 * h), Op.max)

    def clamp(h, ws, first=0, final=1, stop=False):
        for w in ws:
            lo = 2048 * h + 256 * w
            ts(B("oh", lo + 128 * first, lo + 128 * final + 128), B("z", 256 * h + 128 * first, 256 * h + 128 * final + 128),
               2.0 ** (14 * w - 114), Op.max, 2.0 ** (14 * w - 106), Op.min)
            for side in range(first, final + 1):
                mm(window(h), B("ow", 72 * w + 8 * side, 72 * w + 8 * side + 64),
                   B("oh", lo + 128 * side, lo + 128 * side + 128), False, stop and w == ws[-1] and side == final)

    def digits(h):
        lo = 128 * h
        tt(half("tlow", 0, lo, lo + 128), window(h), half("t128", 0, lo, lo + 128), Op.subtract)
        for k, name in enumerate(("t128", "t128", "tlow", "tlow")):
            at = lo + 64 * (k % 2)
            mm(P(7, 64 * h, 64 * h + 64), half("ut", 0, 128 * k, 128 * k + 128), half(name, 0, at, at + 64), k == 0, k == 3)

    for h in range(2):
        mm(P(4 + h), whole("vv", T.vv[0:16, 0, :]), (T.xo[0:16, 512 * h:512 * h + 512], [("xo", 0, 1024)]), True, True)
        act(B("w", 1024 * rank + 512 * h, 1024 * rank + 512 * h + 512), P(4 + h))
    spread("act", 0)
    table("v0", arr[0], 0.0, (0, XC, XC // 2 + 512, 1024), 0, [[slot0] + direct[0]] + 2 * [[slot0] + direct[1]])
    cp(B("lu"), B("sli"))
    W = (T.w[:], [("w", 0, 8192)] + [("w%d" % k, 0, 8192) for k in range(8)])
    for rho in range(3):
        last = rho == 2
        less = -128.0 if rho == 0 else 0.0
        for k in (1, 0, 2, 3):
            lo, hi = SITES[k], SITES[k + 1]
            o, i = B("xg", 16 * lo, 16 * hi), IND(W, B("lu", lo, hi))
            if k == 1:
                ts(o, i, less, Op.add)
            else:
                act(o, i, 1.0, less)
        for b in range(2):
            mm(P(b), (T.tie[0:1, :], [("tie", 0, 128)]), whole("trow", T.trow[0:1, 32 * b:32 * b + 32, :]), True, False)
        for lo, hi in ((0, SITES[1]), (SITES[1], 64), (64, SITES[3]), (SITES[3], 128)):
            running(B("xs", 16 * lo, 16 * hi), B("mask", 0, 16 * (hi - lo)), B("xg", 16 * lo, 16 * hi))
        for h in range(2):
            if rho == 0:
                act(B("vh", 512 * h, 512 * h + 512), B("v0", 512 * h, 512 * h + 512), 0.5, 1472.25)
            else:
                mm(P(6 - h), B("pm16", 128 * rho - 128, 128 * rho), B("vo", 512 * h, 512 * h + 512), True, True)
        if rho == 0:
            ts(B("pti", 0, 64), B("pri"), 4, Op.arith_shift_right)
            ts(B("pti", 64, 128), B("pri"), 15, Op.bitwise_and)
            ts(B("lf"), B("sli"), C(SG), Op.mult, C(SOFF), Op.add)
        else:
            act(B("lf"), P(7, 128, 256), C(SG), C(SOFF))
            act(B("vh", 0, 512), P(6), 0.5, 768.25)
        repeat("id16", S(0, 64), 0)
        totals(0, False)
        mm(P(0), S(0, 128), whole("ny", T.ny[:]), False, True)
        signs(0)
        mm(P(1), S(0, 128), whole("ny", T.ny[:]), False, False)
        totals(1, True)
        signs(1)
        repeat("id16", S(64, 128), 1)
        maxima("m1", 0)
        if rho == 0:
            cp(B("prf", 0, 128), B("pti"))
        maxima("m1", 1, (0, 1, 2))
        counts(0)
        keys("kp", "m1", 0, (0, 1))
        counts(1)
        ts(B("pos", 0, 8), P(7, 64, 72), 63.5, Op.add)
        maxima("m1", 1, (3,))
        act(B("posb"), P(7, 64, 72))
        if rho == 0:
            act(B("pm32"), B("pm16"))
        else:
            act(B("vh", 512, 1024), P(5), 0.5, 768.25)
        keys("kp", "m1", 0, (2, 3))
        keys("kp", "m1", 1, (0,))
        mm(P(7, 72, 80), B("swp"), B("posb"), True, True)
        keys("kp", "m1", 1, (1, 2, 3))
        odd = P(5, 256, 384)
        mm(odd, B("dbig"), B("ones"), True, False)
        mm(odd, B("dq"), B("ones"), False, False)
        cp(IND(B("cp"), B("pos", 0, 8)), S(0, 128))
        ts(B("pos", 8, 16), P(7, 72, 80), 63.5, Op.add)
        cp(IND(B("lp"), B("pos", 0, 8)), B("lf"))
        act(B("cq"), IND(B("cp"), B("pos", 8, 16)))
        cp(B("tu"), B("prf", 128 * rho, 128 * rho + 64))
        ts(P(7, 128, 256), B("lp"), ROUND / 1024, Op.add, -ROUND / 1024, Op.add)
        for h in range(2):
            act(half("pp", h, 128 * h, 128 * h + 128), half("lp", h, 0, 128))
        act(B("jb"), B("prf", 128 * rho + 64, 128 * rho + 128), 8.0)
        repeat("sw16", B("cq", 0, 64), 0)
        repeat("sw16", B("cq", 64, 128), 1)
        maxima("m2", 0, (0,))
        for h in range(2):
            tt(half("pp", 1 - h, 128 * h, 128 * h + 128), half("lp", h, 0, 128), half(7, h, 128, 256), Op.subtract)
        maxima("m2", 0, (1, 2, 3))
        maxima("m2", 1)
        keys("kn", "m2", 0, (0,))
        for b in range(2):
            pairs("cd", "pp", b)
            act(B("gl", 512 * b, 512 * b + 512), P(b), 1.0, 0.0, Fn.Sign)
        keys("kn", "m2", 0, (1, 2, 3))
        act(B("ks", 0, 64), P(6, 256, 320), 1.0, C(SQ))
        keys("kn", "m2", 1, (0, 1))
        tally(odd, "ca", "gl", 0, False, False)
        keys("kn", "m2", 1, (2, 3))
        tally(odd, "ca", "gl", 1, False, True)
        act(B("ks", 64, 128), P(4, 256, 320), 1.0, C(SQ))
        cp(IND(B("kq"), B("pos", 0, 4)), B("ks", 0, 64))
        ts(B("rr"), odd, ROUND, Op.add, -ROUND, Op.add)
        cp(IND(B("kq"), B("pos", 4, 8)), B("ks", 64, 128))
        tt(P(5, 0, 128), odd, B("rr"), Op.subtract)
        for a in range(8):
            mm(P(2, 256, 384), B("cs", 112 - 16 * a, 240 - 16 * a), G("gs", a, 64, 8), a == 0, a == 7)
        act(B("posf"), P(2, 256, 384), 1.0, 63.5)
        for h in range(2):
            act(half(4, h, 0, 128), half("pp", h, 128 * h, 128 * h + 128), half("cf", h, SQH, SQH + 1), -0.5)
            act(half(4, h, 128, 256), half("pp", 1 - h, 128 * h, 128 * h + 128), half("cf", 1 - h, SQL, SQL + 1),
                1.0 + 63.5 / 128)
        tt(P(5, 128, 192), B("kq", 0, 64), P(5, 0, 64), Op.min)
        upper(0)
        tt(P(5, 192, 256), B("kq", 64, 128), P(5, 64, 128), Op.min)
        lower(0)
        upper(1)
        ts(B("com"), P(5, 0, 128), -1.0 / 1024, Op.mult, C(QC), Op.add)
        differences(0)
        differences(1)
        lower(1)
        order(0)
        order(1)
        differences(2)
        differences(3)
        mm(P(6, 128, 256), B("we1"), B("com"), True, False)
        mm(P(6, 128, 256), B("we2"), B("com"), False, True)
        order(2)
        act(B("ew"), P(6, 128, 256), EXPC, 0.0, Fn.Exp)
        order(3)
        ranks(0)
        ranks(1)
        for u in range(2):
            tt(P(4, 256 + 128 * u, 384 + 128 * u), B("ew"), P(4, 128 * u, 128 * u + 128), Op.mult)
        powers(0)
        ranks(2)
        ranks(3)
        scaled(0, 0)
        powers(1)
        for h in range(2):
            for d in ("d1", "d2", "d3"):
                mm(window(h), half(d, 0, 0, 64), half("ones", 0, 0, 128), d == "d1", False)
        act(B("prow", 0, PROW), IND(B("posf"), B("tu", 0, PROW // 16)))
        clamp(0, range(2), 0, 0)
        scaled(0, 1)
        clamp(0, range(2, 4), 0, 0)
        clamp(0, range(4, 8))
        scaled(1, 0)
        clamp(0, range(4), 1, 1, True)
        scaled(1, 1)
        act(half("t128", 0, 0, 128), window(0))
        act(B("prow", PROW, 1024), IND(B("posf"), B("tu", PROW // 16, 64)))
        clamp(1, range(LATE), 0, 0)
        clamp(1, range(LATE, 8))
        digits(0)
        clamp(1, range(LATE), 1, 1, True)
        mm(P(1, 0, 64), B("idn"), B("jb"), True, False)
        for j in range(16):
            mm(P(1, 0, 64), B("kp", 15 - j, 143 - j), B("prow", j, 1024, 16), False, j == 15)
        ts(B("lu2", 0, 64), P(7, 0, 64), C(KAP), Op.add)
        act(B("g1", 0, 1024), IND(W, B("lu2", 0, 64)), 0.5, less / 2)
        cp(half("t128", 0, 128, 256), window(1))
        digits(1)
        ts(B("pru"), P(1, 0, 64), 0.125, Op.mult)
        ts(B("lu2", 64, 128), P(7, 64, 128), C(KAP), Op.add)
        ts(B("g1", 1024, 16 * GCUT), IND(W, B("lu2", 64, GCUT)), 0.5, Op.mult, less / 2, Op.add)
        act(B("g1", 16 * GCUT, 2048), IND(W, B("lu2", GCUT, 128)), 0.5, less / 2)
        act(B("lpos"), P(7, 0, 128), 1.0, C(KAP))
        if not last:
            mm(P(2, 0, 128), B("pm32", 128 * rho, 128 * rho + 128), B("prf", 128 * rho, 128 * rho + 128), True, True)
            act(B("prf", 128 * rho + 128, 128 * rho + 256), P(2, 0, 128))
        act(B("lf2"), IND(B("lpos"), B("pos", 0, 8)))
        if last:
            dma("sync", D("ys"), B("lf2"))
            dma("sync", D("yll", rank), (T.lf2[own, :], [("lf2", 0, 128)]))
        cuts = (0, CUTS[1], CUTS[1] + 128, 1024) if last else VCUTS
        for k in range(3):
            lo, hi = cuts[k], cuts[k + 1]
            tt(B("vo", lo, hi), IND(B("g1"), B("pru", lo // 16, hi // 16)), B("vh", lo, hi), Op.add)
            if last and k:
                ts(B("vb", CUTS[k - 1], CUTS[k]), B("vo", CUTS[k - 1], CUTS[k]), -1408.0, Op.add)
        if not last:
            table("vo", arr[rho], 1536.0, VCUTS, FIRST)
            mm(P(7, 128, 256), B("pm32", 128 * rho, 128 * rho + 128), B("lf2"), True, True)
            cp(B("lu"), P(7, 128, 256))

    for h in range(2):
        lo, hi = CUTS[h], CUTS[h + 1]
        dma("sync", D("vs%d" % h), B("vb", lo, hi))
        dma("act", D("vl%d" % h, rank), (T.vb[own, lo:hi], [("vb", lo, hi)]))
    exchange("yl", "ys", lambda r: arr[2].index(r), "yll", rank)
    for h in range(2):
        exchange("y%d" % h, "vs%d" % h, lambda r: arr[2].index(r), "vl%d" % h, rank)
    arrival("yl", "yll", rank)
    dma("act", (T.yl[:], []), D("yll"))
    for h in range(2):
        arrival("y%d" % h, "vl%d" % h, rank)
        dma("g", (T.yx[:, CUTS[h]:CUTS[h + 1]], []), D("vl%d" % h))
    emit(g, T, ops)


FIRST = 8
GCUT = 100
LATE = 6
PROW = 768
DIRECT = 1
